import numpy as np
import ml_dtypes


def mxq(x, axis, fmt="e4m3"):
    dtype, down = {"e4m3": (ml_dtypes.float8_e4m3fn, 7), "e5m2": (ml_dtypes.float8_e5m2, 14)}[fmt]
    v = np.moveaxis(np.asarray(x, np.float32).astype(ml_dtypes.bfloat16).astype(np.float64), axis, -1)
    blocks = v.reshape(v.shape[:-1] + (-1, 32))
    amax = np.abs(blocks).max(-1, keepdims=True)
    byte = np.maximum(np.where(amax > 0, np.frexp(amax)[1] - 1 + 127, 0) - down, 1)
    scale = np.exp2(byte - 127.0)
    codes = (blocks / scale).astype(np.float32).astype(dtype).astype(np.float64)
    return np.moveaxis((codes * scale).reshape(v.shape), -1, axis)


WIDE = False


def mx_kscale(k):
    if not WIDE:
        return np.ones(k)
    levels = np.array([30, -30])
    if k % 512:
        return np.exp2(np.random.permutation(np.resize(levels, k // 32))).repeat(32)
    a = np.empty((k // 512, 16))
    for p in range(k // 512):
        a[p, :8] = np.random.permutation(np.resize(levels, 8))
        for g in range(8):
            far = levels[np.abs(levels - a[p, g]) >= 10]
            a[p, g + 8] = far[np.random.randint(len(far))]
    return np.exp2(a.ravel()).repeat(32)


def f64(x):
    return np.asarray(x).astype(np.float64)


def striped(idx):
    return np.tile(idx.reshape(-1, 16).T, (8, 1)).astype(np.uint16)


def unstriped(offs):
    return offs[:16].T.reshape(-1).astype(np.int64)


E2M1 = np.array([0.0, 0.5, 1.0, 1.5, 2.0, 3.0, 4.0, 6.0, -0.0, -0.5, -1.0, -1.5, -2.0, -3.0, -4.0, -6.0])


def pack_weight(w, fmt):
    k, n = w.shape
    w = f64(np.asarray(w, np.float32).astype(ml_dtypes.bfloat16)).reshape(k // 32, 32, n)
    amax = np.abs(w).max(1)
    if fmt == "e4m3":
        byte = np.frexp(amax)[1] - 1 + 127 - 7
    else:
        mant, ex = np.frexp(amax / 6.0)
        byte = np.where(mant > 0.5, ex, ex - 1) + 127
    byte = np.clip(np.where(amax > 0, byte, 1), 1, 254)
    scaled = (w * np.exp2(127.0 - byte)[:, None, :]).reshape(k, n).astype(np.float32)
    by_word = np.ascontiguousarray(scaled.reshape(k // 512, 128, 4, n).transpose(0, 1, 3, 2))
    if fmt == "e4m3":
        words = by_word.astype(ml_dtypes.float8_e4m3fn).view(np.uint8)
    else:
        c = by_word.astype(ml_dtypes.float4_e2m1fn).view(np.uint8) & 0xF
        words = (c[..., 0::2] | (c[..., 1::2] << 4)).reshape(k // 512, 128, 2 * n)
    return np.ascontiguousarray(words), np.ascontiguousarray(byte.astype(np.uint8).reshape(k // 512, 16, n))


def unpack_weight(words, scales, fmt):
    g, _, n = scales.shape
    words = np.ascontiguousarray(words).reshape(g, 128, n, -1)
    if fmt == "e4m3":
        vals = words.view(ml_dtypes.float8_e4m3fn).astype(np.float64)
    else:
        nib = np.empty((g, 128, n, 4), np.uint8)
        nib[..., 0::2] = words & 0xF
        nib[..., 1::2] = words >> 4
        vals = E2M1[nib]
    vals = vals * np.repeat(np.exp2(scales.astype(np.float64) - 127.0), 8, axis=1)[..., None]
    return vals.transpose(0, 1, 3, 2).reshape(g * 512, n)


def sigmoid(v):
    return 1.0 / (1.0 + np.exp(-np.maximum(v, -700.0)))


def d_sigmoid(v):
    s = 1.0 / (1.0 + np.exp(-np.maximum(v, -700.0)))
    return s * (1.0 - s)


K, T, E, C, H, N = 128, 1024, 2, 512, 1024, 1024


def by_expert(wq, xq):
    return np.concatenate([wq[e].T @ xq[:, e * C:(e + 1) * C] for e in range(E)], axis=1)


def setup_inputs():
    n = np.random.standard_normal
    s = mx_kscale(N)[:, None]
    u = mx_kscale(H)
    w2 = [pack_weight(m, "e2m1") for m in n((E, N, H)) / np.sqrt(N) / s[None] * u[None, None, :]]
    w1 = [pack_weight(m, "e2m1") for m in n((E, H, K)) / np.sqrt(H) / u[None, :, None]]
    w3 = [pack_weight(m, "e2m1") for m in n((E, H, K)) / np.sqrt(H) / u[None, :, None]]
    return {
        "dyT": (n((N, T)) * s).astype(np.float32),
        "a1": n((H, E * C)).astype(np.float32),
        "a3": n((H, E * C)).astype(np.float32),
        "w2_words": np.stack([m[0] for m in w2]),
        "w2_scales": np.stack([m[1] for m in w2]),
        "w1_words": np.stack([m[0] for m in w1]),
        "w1_scales": np.stack([m[1] for m in w1]),
        "w3_words": np.stack([m[0] for m in w3]),
        "w3_scales": np.stack([m[1] for m in w3]),
        "gate": np.tile(np.random.uniform(0.2, 1.0, E * C), (N, 1)).astype(np.float32),
        "offs": striped(np.random.permutation(T)[:E * C]),
    }


def reference(dyT, a1, a3, w2_words, w2_scales, w1_words, w1_scales, w3_words, w3_scales, gate, offs):
    idx = unstriped(offs)
    w2 = np.stack([unpack_weight(w2_words[e], w2_scales[e], "e2m1") for e in range(E)])
    w1 = np.stack([unpack_weight(w1_words[e], w1_scales[e], "e2m1") for e in range(E)])
    w3 = np.stack([unpack_weight(w3_words[e], w3_scales[e], "e2m1") for e in range(E)])
    gq = mxq(f64(gate) * f64(dyT)[:, idx], 0, "e5m2")
    dh = by_expert(w2, gq)
    da1 = dh * f64(a3) * d_sigmoid(f64(a1))
    da3 = dh * sigmoid(f64(a1))
    dx = by_expert(w1, mxq(da1, 0, "e5m2")) + by_expert(w3, mxq(da3, 0, "e5m2"))
    out = np.zeros((K, T))
    out[:, idx] = dx
    return out

@@ -1,0 +1,231 @@
+from contextlib import ExitStack
+
+import concourse.mybir as mybir
+
+F32 = mybir.dt.float32
+BF16 = mybir.dt.bfloat16
+I32 = mybir.dt.int32
+U32 = mybir.dt.uint32
+U16 = mybir.dt.uint16
+U8 = mybir.dt.uint8
+E5M2X4 = mybir.dt.float8_e5m2_x4
+E2M1X4 = mybir.dt.float4_e2m1fn_x4
+ACT = mybir.ActivationFunctionType
+MULT = mybir.AluOpType.mult
+SUB = mybir.AluOpType.subtract
+
+P = 128
+PACK = 4
+PASS = P * PACK
+K, T, E, C, H, N = 128, 1024, 2, 512, 1024, 1024
+FLOPS = 2 * E * C * (N * H + 2 * H * K)
+
+
+def tile_moe_bdx_glu_sigmoid_kernel(
+    tc, dyT, a1, a3, w2_words, w2_scales, w1_words, w1_scales, w3_words, w3_scales, gate, offs, out
+):
+    nc = tc.nc
+    with ExitStack() as ctx:
+        keep = ctx.enter_context(tc.tile_pool(name="keep", bufs=1))
+        ring2 = ctx.enter_context(tc.tile_pool(name="ring2", bufs=2))
+        banks = ctx.enter_context(tc.psum_pool(name="banks", bufs=6))
+        sums = ctx.enter_context(tc.psum_pool(name="sums", bufs=1))
+
+        offsets = keep.tile([P, E * C // 16], U16, name="offsets")
+        gates = keep.tile([P, E * C], F32, name="gates")
+        dy = [keep.tile([P, T + 8], F32, name=f"dy{b}") for b in range(N // P)]
+        w2_raw = [keep.tile([P, 2 * H], U8, name=f"w2_raw{b}", align_bytes=64) for b in range(4)]
+        w2_put = [keep.tile([P, 2 * H], U8, name=f"w2_put{b}", align_bytes=64) for b in range(4)]
+        w2s_raw = keep.tile([P, H], U8, name="w2s_raw", align_bytes=64)
+        w2s_put = [keep.tile([P, H], U8, name=f"w2s_put{b}", align_bytes=64) for b in range(4)]
+        w13 = [keep.tile([P, 4, 2 * K], U8, name=f"w13_{b}", align_bytes=64) for b in range(2)]
+        w13s = keep.tile([P, 2, 4, K], U8, name="w13s", align_bytes=64)
+        a1_t = [keep.tile([P, PACK, C], F32, name=f"a1_{b}") for b in range(4)]
+        a3_t = [keep.tile([P, PACK, C], F32, name=f"a3_{b}") for b in range(4)]
+        result = keep.tile([P, T], F32, name="result")
+
+        nc.gpsimd.memset(w2s_raw[:].bitcast(I32), 0)
+        for b in range(8):
+            nc.gpsimd.memset(dy[b][:, T:], 0.0)
+        for b in range(1, 4):
+            nc.gpsimd.memset(w2s_put[b][:].bitcast(I32), 0)
+        nc.gpsimd.memset(w13s[:].rearrange("p w b k -> p (w b k)").bitcast(I32), 0)
+
+        def load_w2(b):
+            nc.sync.dma_start(out=w2_raw[b][:].bitcast(I32), in_=w2_words[b // 2, b % 2].bitcast(I32))
+
+        def load_dy(b):
+            s, j = divmod(b, PACK)
+            nc.sync.dma_start(out=dy[b][:, 0:T], in_=dyT[s * PASS:(s + 1) * PASS].rearrange("(p j) w -> p j w", j=PACK)[:, j, :])
+
+        for b in range(4):
+            load_w2(b)
+        nc.sync.dma_start(offsets[:], offs)
+        for e in range(E):
+            nc.sync.dma_start(out=gates[:, e * C:(e + 1) * C], in_=gate[0:P, e * C:(e + 1) * C])
+            load_dy(e)
+        for b in range(2, 8):
+            load_dy(b)
+        for q in range(4):
+            nc.scalar.dma_start(
+                out=w2s_raw[32 * q:32 * q + 16, :].bitcast(I32),
+                in_=w2_scales[:, :, 4 * q:4 * q + 4, :].bitcast(I32).rearrange("e s q i -> (e s) q i"),
+            )
+        for w, (words, scales) in enumerate(((w1_words, w1_scales), (w3_words, w3_scales))):
+            nc.scalar.dma_start(
+                out=w13[w][:].rearrange("p b i -> p (b i)").bitcast(I32).rearrange("p (b i) -> p b i", b=4),
+                in_=words.bitcast(I32).rearrange("e s p i -> p (e s) i"),
+            )
+            for q in range(4):
+                nc.scalar.dma_start(
+                    out=w13s[32 * q:32 * q + 4, w].rearrange("p b i -> p (b i)").bitcast(I32).rearrange("p (b i) -> p b i", b=4),
+                    in_=scales[:, :, 4 * q:4 * q + 4, :].bitcast(I32).rearrange("e s q i -> q (e s) i"),
+                )
+        for b in range(4):
+            e, h = divmod(b, 2)
+            for src, dst in ((a1, a1_t[b]), (a3, a3_t[b])):
+                nc.sync.dma_start(
+                    out=dst[:],
+                    in_=src[h * PASS:(h + 1) * PASS, e * C:(e + 1) * C].rearrange("(p j) c -> p j c", j=PACK),
+                )
+
+        for b in range(4):
+            nc.vector.tensor_copy(
+                out=w2_put[b][:].bitcast(U16).rearrange("p (h t m) -> p h t m", h=2, t=PACK),
+                in_=w2_raw[b][:].bitcast(U16).rearrange("p (h m t) -> p h t m", h=2, t=PACK),
+            )
+        nc.vector.tensor_copy(
+            out=w2s_put[0][:].rearrange("p (h t m) -> p h t m", h=2, t=PACK),
+            in_=w2s_raw[:].rearrange("p (h m t) -> p h t m", h=2, t=PACK),
+        )
+        for b in range(1, 4):
+            for q in range(4):
+                nc.scalar.dma_start(
+                    out=w2s_put[b][32 * q:32 * q + 4, :].bitcast(I32),
+                    in_=w2s_put[0][32 * q + 4 * b:32 * q + 4 * b + 4, :].bitcast(I32),
+                )
+
+        g_codes, g_scales = {}, {}
+
+        def gather(s, j, g4, first, last):
+            slots = slice(first * C, last * C)
+            nc.vector.tensor_tensor(
+                out=g4[:, j, slots],
+                in0=dy[s * PACK + j][:].indirect(offsets[:, first * C // 16:last * C // 16]),
+                in1=gates[:, slots],
+                op=MULT,
+            )
+
+        def interleaved(dst):
+            return dst.rearrange("p (c i) t -> p c t i", i=4)
+
+        def planes(src):
+            return src.rearrange("p t (c i) -> p c t i", i=4)
+
+        def quantise(src, name):
+            codes = keep.tile([P, C], U32, name=name + "_codes", align_bytes=64)
+            scales = keep.tile([P, C], U8, name=name + "_scales", align_bytes=64)
+            nc.vector.quantize_mx(
+                out=codes[:].bitcast(E5M2X4), scales=scales[:], in_=src.rearrange("p c t -> p (c t)")
+            )
+            return codes, scales
+
+        def finish_g(e, s, g4):
+            gb = ring2.tile([P, C, PACK], BF16, name="gb", align_bytes=64)
+            nc.scalar.copy(out=interleaved(gb[:]), in_=planes(g4[:, :, e * C:(e + 1) * C]))
+            g_codes[e, s], g_scales[e, s] = quantise(gb[:], f"g{e}{s}")
+
+        g4 = [ring2.tile([P, PACK, E * C], F32, name="g4") for s in range(2)]
+        gather(0, 0, g4[0], 0, 1)
+        gather(0, 0, g4[0], 1, 2)
+        for j in range(1, PACK):
+            gather(0, j, g4[0], 0, E)
+        for e in range(E):
+            finish_g(e, 0, g4[0])
+        for e in range(E):
+            for j in range(PACK):
+                gather(1, j, g4[1], e, e + 1)
+            finish_g(e, 1, g4[1])
+
+        dx = [sums.tile([P, C], F32, name=f"dx{e}") for e in range(E)]
+        held = {}
+
+        def saved(b):
+            s = a1_t[b]
+            nc.scalar.activation(out=s[:], in_=s[:], func=ACT.Sigmoid)
+            v = a3_t[b]
+            nc.vector.scalar_tensor_tensor(out=v[:], in0=s[:], scalar=1.0, in1=v[:], op0=SUB, op1=MULT)
+
+        def first_products(b):
+            e, h = divmod(b, 2)
+            u = ring2.tile([P, PACK, C], F32, name="u")
+            for t in range(PACK):
+                dh = banks.tile([P, C], F32, name="dh")
+                col = h * PASS + t * P
+                for s in range(2):
+                    nc.tensor.matmul_mx(
+                        out=dh[:],
+                        lhsT=w2_put[2 * e + s][:, 2 * col:2 * (col + P)].bitcast(E2M1X4),
+                        lhsT_scale=w2s_put[2 * e + s][:, col:col + P],
+                        rhs=g_codes[e, s][:].bitcast(E5M2X4),
+                        rhs_scale=g_scales[e, s][:],
+                        start=(s == 0),
+                        stop=(s == 1),
+                    )
+                nc.vector.tensor_tensor(out=u[:, t, :], in0=dh[:], in1=a1_t[b][:, t, :], op=MULT)
+            held[b] = u
+
+        def product(engine, b, first, last):
+            u, d = held[b]
+            engine.tensor_tensor(
+                out=interleaved(d[:, 0, first:last, :]),
+                in0=planes(u[:, :, first:last]),
+                in1=planes(a3_t[b][:, :, first:last]),
+                op=MULT,
+            )
+
+        def gradients(b, share):
+            u = held[b]
+            d = ring2.tile([P, 2, C, PACK], BF16, name="d", align_bytes=64)
+            held[b] = (u, d)
+            for first in range(0, share, 128):
+                product(nc.gpsimd, b, first, first + 128)
+            nc.scalar.activation(out=interleaved(d[:, 1]), in_=planes(u[:]), func=ACT.Copy, scale=-1.0)
+
+        def second_products(b):
+            e, h = divmod(b, 2)
+            for w in range(2):
+                codes, scales = quantise(held[b][1][:, w], f"d{w}_{b}")
+                nc.tensor.matmul_mx(
+                    out=dx[e][:],
+                    lhsT=w13[w][:, b, :].bitcast(E2M1X4),
+                    lhsT_scale=w13s[:, w, b, :],
+                    rhs=codes[:].bitcast(E5M2X4),
+                    rhs_scale=scales[:],
+                    start=(h == 0 and w == 0),
+                    stop=(h == 1 and w == 1),
+                )
+
+        def finish(e, dx_sb):
+            nc.scalar.activation(out=dx_sb[:, 0, :], in_=dx[e][:], func=ACT.Copy, scale=-1.0)
+
+        def scatter(e, dx_sb):
+            nc.vector.tensor_copy(result[:].indirect(offsets[:, e * C // 16:(e + 1) * C // 16]), dx_sb[:, 0, :])
+
+        saved(0)
+        first_products(0)
+        saved(1)
+        for b in range(4):
+            share = 256 if b < 3 else 0
+            gradients(b, share)
+            if b < 3:
+                first_products(b + 1)
+            product(nc.vector, b, share, C)
+            if b < 2:
+                saved(b + 2)
+            second_products(b)
+        landing = [ring2.tile([P, PACK, C], F32, name="u") for z in range(2)]
+        for e in range(E):
+            finish(e, landing[1 - e])
+            scatter(e, landing[1 - e])
+        nc.sync.dma_start(out=out, in_=result[:])

@@ -1,6 +1,7 @@
 from contextlib import ExitStack
 
 import concourse.mybir as mybir
+from concourse.masks import make_identity
 
 F32 = mybir.dt.float32
 BF16 = mybir.dt.bfloat16
@@ -27,13 +28,16 @@ def tile_moe_bdx_glu_sigmoid_kernel(
     nc = tc.nc
     with ExitStack() as ctx:
         keep = ctx.enter_context(tc.tile_pool(name="keep", bufs=1))
+        ring4 = ctx.enter_context(tc.tile_pool(name="ring4", bufs=4))
         ring2 = ctx.enter_context(tc.tile_pool(name="ring2", bufs=2))
         banks = ctx.enter_context(tc.psum_pool(name="banks", bufs=6))
         sums = ctx.enter_context(tc.psum_pool(name="sums", bufs=1))
 
         offsets = keep.tile([P, E * C // 16], U16, name="offsets")
-        gates = keep.tile([P, E * C], F32, name="gates")
-        dy = [keep.tile([P, T + 8], F32, name=f"dy{b}") for b in range(N // P)]
+        gate_rows = keep.tile([P, P], F32, name="gate_rows")
+        gate_cols = keep.tile([P, E * C // P], F32, name="gate_cols")
+        ident = keep.tile([P, P], F32, name="ident")
+        dy = [keep.tile([P, T], F32, name=f"dy{b}") for b in range(N // P)]
         w2_raw = [keep.tile([P, 2 * H], U8, name=f"w2_raw{b}", align_bytes=64) for b in range(4)]
         w2_put = [keep.tile([P, 2 * H], U8, name=f"w2_put{b}", align_bytes=64) for b in range(4)]
         w2s_raw = keep.tile([P, H], U8, name="w2s_raw", align_bytes=64)
@@ -45,8 +49,8 @@ def tile_moe_bdx_glu_sigmoid_kernel(
         result = keep.tile([P, T], F32, name="result")
 
         nc.gpsimd.memset(w2s_raw[:].bitcast(I32), 0)
-        for b in range(8):
-            nc.gpsimd.memset(dy[b][:, T:], 0.0)
+        nc.gpsimd.memset(gate_rows[:], 0.0)
+        make_identity(nc, ident[:])
         for b in range(1, 4):
             nc.gpsimd.memset(w2s_put[b][:].bitcast(I32), 0)
         nc.gpsimd.memset(w13s[:].rearrange("p w b k -> p (w b k)").bitcast(I32), 0)
@@ -56,38 +60,52 @@ def tile_moe_bdx_glu_sigmoid_kernel(
 
         def load_dy(b):
             s, j = divmod(b, PACK)
-            nc.sync.dma_start(out=dy[b][:, 0:T], in_=dyT[s * PASS:(s + 1) * PASS].rearrange("(p j) w -> p j w", j=PACK)[:, j, :])
+            nc.sync.dma_start(out=dy[b][:], in_=dyT[s * PASS:(s + 1) * PASS].rearrange("(p j) w -> p j w", j=PACK)[:, j, :])
 
-        for b in range(4):
-            load_w2(b)
-        nc.sync.dma_start(offsets[:], offs)
-        for e in range(E):
-            nc.sync.dma_start(out=gates[:, e * C:(e + 1) * C], in_=gate[0:P, e * C:(e + 1) * C])
-            load_dy(e)
-        for b in range(2, 8):
-            load_dy(b)
-        for q in range(4):
-            nc.scalar.dma_start(
-                out=w2s_raw[32 * q:32 * q + 16, :].bitcast(I32),
-                in_=w2_scales[:, :, 4 * q:4 * q + 4, :].bitcast(I32).rearrange("e s q i -> (e s) q i"),
-            )
-        for w, (words, scales) in enumerate(((w1_words, w1_scales), (w3_words, w3_scales))):
-            nc.scalar.dma_start(
+        def load_w13(w, words, scales):
+            nc.sync.dma_start(
                 out=w13[w][:].rearrange("p b i -> p (b i)").bitcast(I32).rearrange("p (b i) -> p b i", b=4),
                 in_=words.bitcast(I32).rearrange("e s p i -> p (e s) i"),
             )
             for q in range(4):
-                nc.scalar.dma_start(
+                nc.sync.dma_start(
                     out=w13s[32 * q:32 * q + 4, w].rearrange("p b i -> p (b i)").bitcast(I32).rearrange("p (b i) -> p b i", b=4),
                     in_=scales[:, :, 4 * q:4 * q + 4, :].bitcast(I32).rearrange("e s q i -> q (e s) i"),
                 )
-        for b in range(4):
+
+        def load_saved(src, dst, b, first=0, last=PACK):
             e, h = divmod(b, 2)
-            for src, dst in ((a1, a1_t[b]), (a3, a3_t[b])):
+            nc.sync.dma_start(
+                out=dst[b][:, first:last, :],
+                in_=src[h * PASS:(h + 1) * PASS, e * C:(e + 1) * C].rearrange("(p j) c -> p j c", j=PACK)[:, first:last, :],
+            )
+
+        def move_scales(b):
+            for q in range(4):
                 nc.sync.dma_start(
-                    out=dst[:],
-                    in_=src[h * PASS:(h + 1) * PASS, e * C:(e + 1) * C].rearrange("(p j) c -> p j c", j=PACK),
+                    out=w2s_put[b][32 * q:32 * q + 4, :].bitcast(I32),
+                    in_=w2s_put[0][32 * q + 4 * b:32 * q + 4 * b + 4, :].bitcast(I32),
                 )
+
+        for b in range(4):
+            load_w2(b)
+        nc.sync.dma_start(offsets[:], offs)
+        load_dy(0)
+        for q in range(4):
+            nc.sync.dma_start(
+                out=w2s_raw[32 * q:32 * q + 16, :].bitcast(I32),
+                in_=w2_scales[:, :, 4 * q:4 * q + 4, :].bitcast(I32).rearrange("e s q i -> (e s) q i"),
+            )
+        load_dy(1)
+        nc.sync.dma_start(out=gate_rows[0:E * C // P, :], in_=gate[0].rearrange("(c m) -> c m", m=P))
+        load_dy(2)
+        load_saved(a1, a1_t, 0)
+        load_saved(a1, a1_t, 1)
+        for b in range(3, 6):
+            load_dy(b)
+        load_saved(a1, a1_t, 2)
+        load_dy(6)
+        load_dy(7)
 
         for b in range(4):
             nc.vector.tensor_copy(
@@ -98,23 +116,32 @@ def tile_moe_bdx_glu_sigmoid_kernel(
             out=w2s_put[0][:].rearrange("p (h t m) -> p h t m", h=2, t=PACK),
             in_=w2s_raw[:].rearrange("p (h m t) -> p h t m", h=2, t=PACK),
         )
-        for b in range(1, 4):
-            for q in range(4):
-                nc.scalar.dma_start(
-                    out=w2s_put[b][32 * q:32 * q + 4, :].bitcast(I32),
-                    in_=w2s_put[0][32 * q + 4 * b:32 * q + 4 * b + 4, :].bitcast(I32),
-                )
+        load_saved(a3, a3_t, 0)
+        move_scales(1)
+        load_saved(a3, a3_t, 1)
+        load_w13(0, w1_words, w1_scales)
+        load_saved(a1, a1_t, 3)
+        load_w13(1, w3_words, w3_scales)
+        load_saved(a3, a3_t, 2)
+        move_scales(2)
+        load_saved(a3, a3_t, 3)
+        move_scales(3)
 
         g_codes, g_scales = {}, {}
 
-        def gather(s, j, g4, first, last):
-            slots = slice(first * C, last * C)
-            nc.vector.tensor_tensor(
-                out=g4[:, j, slots],
-                in0=dy[s * PACK + j][:].indirect(offsets[:, first * C // 16:last * C // 16]),
-                in1=gates[:, slots],
-                op=MULT,
-            )
+        turned = banks.tile([P, C], F32, name="dh")
+        nc.tensor.transpose(turned[:, 0:P], gate_rows[:], ident[:])
+        nc.scalar.copy(out=gate_cols[:], in_=turned[:, 0:E * C // P])
+
+        def gather(s):
+            g4 = [keep.tile([P, PACK, C], F32, name=f"g4_{e}{s}") for e in range(E)]
+            for j in range(PACK):
+                for e in range(E):
+                    nc.vector.tensor_copy(
+                        out=g4[e][:, j, :],
+                        in_=dy[s * PACK + j][:].indirect(offsets[:, e * C // 16:(e + 1) * C // 16]),
+                    )
+            return g4
 
         def interleaved(dst):
             return dst.rearrange("p (c i) t -> p c t i", i=4)
@@ -130,31 +157,58 @@ def tile_moe_bdx_glu_sigmoid_kernel(
             )
             return codes, scales
 
-        def finish_g(e, s, g4):
+        def weigh(e, g4):
             gb = ring2.tile([P, C, PACK], BF16, name="gb", align_bytes=64)
-            nc.scalar.copy(out=interleaved(gb[:]), in_=planes(g4[:, :, e * C:(e + 1) * C]))
+            words = gb[:].rearrange("p c t -> p (c t)").bitcast(F32).rearrange("p (a c u) -> p a c u", a=PACK, u=2)
+            for half in range(2):
+                back = sums.tile([P, C], F32, name=f"dx{half}")
+                back4 = back[:].rearrange("p (a u c) -> p a u c", a=2, u=2)
+                for a in range(2):
+                    tile = 2 * half + a
+                    across = banks.tile([P, C], F32, name="dh")
+                    for j in reversed(range(PACK)):
+                        nc.tensor.transpose(across[:, j * P:(j + 1) * P], g4[:, j, tile * P:(tile + 1) * P], ident[:])
+                    rounded = ring4.tile([P, PASS], BF16, name="rounded")
+                    nc.scalar.activation(
+                        out=rounded[:].rearrange("c (u p v) -> c u p v", u=2, v=2),
+                        in_=across[:].rearrange("c (u v p) -> c u p v", u=2, v=2),
+                        func=ACT.Copy,
+                        scale=gate_cols[:, e * PACK + tile:e * PACK + tile + 1],
+                    )
+                    pairs = rounded[:].bitcast(F32)
+                    for u in range(2):
+                        nc.tensor.transpose(back4[:, a, u, :], pairs[:, u * P:(u + 1) * P], ident[:])
+                nc.scalar.copy(out=words[:, 2 * half:2 * half + 2], in_=back4.rearrange("p a u c -> p a c u"))
+            return gb
+
+        def finish_g(e, s, gb):
             g_codes[e, s], g_scales[e, s] = quantise(gb[:], f"g{e}{s}")
 
-        g4 = [ring2.tile([P, PACK, E * C], F32, name="g4") for s in range(2)]
-        gather(0, 0, g4[0], 0, 1)
-        gather(0, 0, g4[0], 1, 2)
-        for j in range(1, PACK):
-            gather(0, j, g4[0], 0, E)
-        for e in range(E):
-            finish_g(e, 0, g4[0])
-        for e in range(E):
-            for j in range(PACK):
-                gather(1, j, g4[1], e, e + 1)
-            finish_g(e, 1, g4[1])
+        def sigmoid(b):
+            nc.scalar.activation(out=a1_t[b][:], in_=a1_t[b][:], func=ACT.Sigmoid)
+
+        def slope(b):
+            v = a3_t[b]
+            nc.vector.scalar_tensor_tensor(out=v[:], in0=a1_t[b][:], scalar=1.0, in1=v[:], op0=SUB, op1=MULT)
+
+        g4 = gather(0)
+        sigmoid(0)
+        sigmoid(1)
+        gb00 = weigh(0, g4[0])
+        gb10 = weigh(1, g4[1])
+        finish_g(0, 0, gb00)
+        finish_g(1, 0, gb10)
+        g4 = gather(1)
+        sigmoid(2)
+        gb01 = weigh(0, g4[0])
+        finish_g(0, 1, gb01)
+        gb11 = weigh(1, g4[1])
+        slope(0)
+        slope(1)
+        slope(2)
 
         dx = [sums.tile([P, C], F32, name=f"dx{e}") for e in range(E)]
         held = {}
-
-        def saved(b):
-            s = a1_t[b]
-            nc.scalar.activation(out=s[:], in_=s[:], func=ACT.Sigmoid)
-            v = a3_t[b]
-            nc.vector.scalar_tensor_tensor(out=v[:], in0=s[:], scalar=1.0, in1=v[:], op0=SUB, op1=MULT)
 
         def first_products(b):
             e, h = divmod(b, 2)
@@ -212,17 +266,19 @@ def tile_moe_bdx_glu_sigmoid_kernel(
         def scatter(e, dx_sb):
             nc.vector.tensor_copy(result[:].indirect(offsets[:, e * C // 16:(e + 1) * C // 16]), dx_sb[:, 0, :])
 
-        saved(0)
         first_products(0)
-        saved(1)
         for b in range(4):
             share = 256 if b < 3 else 0
             gradients(b, share)
+            if b == 1:
+                finish_g(1, 1, gb11)
             if b < 3:
                 first_products(b + 1)
             product(nc.vector, b, share, C)
-            if b < 2:
-                saved(b + 2)
+            if b == 0:
+                sigmoid(3)
+            if b == 1:
+                slope(3)
             second_products(b)
         landing = [ring2.tile([P, PACK, C], F32, name="u") for z in range(2)]
         for e in range(E):

@@ -30,12 +30,14 @@ def tile_moe_bdx_glu_sigmoid_kernel(
         keep = ctx.enter_context(tc.tile_pool(name="keep", bufs=1))
         ring4 = ctx.enter_context(tc.tile_pool(name="ring4", bufs=4))
         ring2 = ctx.enter_context(tc.tile_pool(name="ring2", bufs=2))
-        banks = ctx.enter_context(tc.psum_pool(name="banks", bufs=6))
+        banks = ctx.enter_context(tc.psum_pool(name="banks", bufs=4))
+        turns = ctx.enter_context(tc.psum_pool(name="turns", bufs=2))
         sums = ctx.enter_context(tc.psum_pool(name="sums", bufs=1))
 
         offsets = keep.tile([P, E * C // 16], U16, name="offsets")
+        gates = keep.tile([P, C], F32, name="gates", align_bytes=64)
         gate_rows = keep.tile([P, P], F32, name="gate_rows")
-        gate_cols = keep.tile([P, E * C // P], F32, name="gate_cols")
+        gate_cols = keep.tile([P, C // P], F32, name="gate_cols")
         ident = keep.tile([P, P], F32, name="ident")
         dy = [keep.tile([P, T], F32, name=f"dy{b}") for b in range(N // P)]
         w2_raw = [keep.tile([P, 2 * H], U8, name=f"w2_raw{b}", align_bytes=64) for b in range(4)]
@@ -45,7 +47,7 @@ def tile_moe_bdx_glu_sigmoid_kernel(
         w13 = [keep.tile([P, 4, 2 * K], U8, name=f"w13_{b}", align_bytes=64) for b in range(2)]
         w13s = keep.tile([P, 2, 4, K], U8, name="w13s", align_bytes=64)
         a1_t = [keep.tile([P, PACK, C], F32, name=f"a1_{b}") for b in range(4)]
-        a3_t = [keep.tile([P, PACK, C], F32, name=f"a3_{b}") for b in range(4)]
+        a3_t = [keep.tile([P, PACK, C], F32, name=f"a3_{b}", align_bytes=64) for b in range(4)]
         result = keep.tile([P, T], F32, name="result")
 
         nc.gpsimd.memset(w2s_raw[:].bitcast(I32), 0)
@@ -87,60 +89,80 @@ def tile_moe_bdx_glu_sigmoid_kernel(
                     in_=w2s_put[0][32 * q + 4 * b:32 * q + 4 * b + 4, :].bitcast(I32),
                 )
 
-        for b in range(4):
-            load_w2(b)
+        def load_plane(k):
+            b, t = divmod(k, PACK)
+            load_saved(a1, a1_t, b, t, t + 1)
+            load_saved(a3, a3_t, b, t, t + 1)
+
+        load_w2(0)
         nc.sync.dma_start(offsets[:], offs)
+        load_w2(1)
+        nc.sync.dma_start(out=gates[:], in_=gate[0:P, 0:C])
         load_dy(0)
+        load_dy(1)
+        load_plane(0)
         for q in range(4):
             nc.sync.dma_start(
                 out=w2s_raw[32 * q:32 * q + 16, :].bitcast(I32),
                 in_=w2_scales[:, :, 4 * q:4 * q + 4, :].bitcast(I32).rearrange("e s q i -> (e s) q i"),
             )
-        load_dy(1)
-        nc.sync.dma_start(out=gate_rows[0:E * C // P, :], in_=gate[0].rearrange("(c m) -> c m", m=P))
         load_dy(2)
-        load_saved(a1, a1_t, 0)
-        load_saved(a1, a1_t, 1)
-        for b in range(3, 6):
-            load_dy(b)
-        load_saved(a1, a1_t, 2)
-        load_dy(6)
-        load_dy(7)
+        load_plane(1)
+        nc.sync.dma_start(out=gate_rows[0:C // P, :], in_=gate[0, C:].rearrange("(c m) -> c m", m=P))
+        load_dy(3)
+        load_plane(2)
 
-        for b in range(4):
+        def permute_w2(b):
             nc.vector.tensor_copy(
                 out=w2_put[b][:].bitcast(U16).rearrange("p (h t m) -> p h t m", h=2, t=PACK),
                 in_=w2_raw[b][:].bitcast(U16).rearrange("p (h m t) -> p h t m", h=2, t=PACK),
             )
+
+        permute_w2(0)
+        permute_w2(1)
         nc.vector.tensor_copy(
             out=w2s_put[0][:].rearrange("p (h t m) -> p h t m", h=2, t=PACK),
             in_=w2s_raw[:].rearrange("p (h m t) -> p h t m", h=2, t=PACK),
         )
-        load_saved(a3, a3_t, 0)
+        load_dy(4)
+        load_plane(3)
+        load_dy(5)
+        load_plane(4)
         move_scales(1)
-        load_saved(a3, a3_t, 1)
+        load_dy(6)
+        load_plane(5)
+        load_dy(7)
+        load_plane(6)
+        load_plane(7)
+        load_w2(2)
+        load_w2(3)
+        load_saved(a1, a1_t, 2)
         load_w13(0, w1_words, w1_scales)
-        load_saved(a1, a1_t, 3)
-        load_w13(1, w3_words, w3_scales)
         load_saved(a3, a3_t, 2)
+        load_w13(1, w3_words, w3_scales)
+        load_saved(a1, a1_t, 3)
         move_scales(2)
         load_saved(a3, a3_t, 3)
         move_scales(3)
 
         g_codes, g_scales = {}, {}
 
-        turned = banks.tile([P, C], F32, name="dh")
+        turned = turns.tile([P, C], F32, name="across")
         nc.tensor.transpose(turned[:, 0:P], gate_rows[:], ident[:])
-        nc.scalar.copy(out=gate_cols[:], in_=turned[:, 0:E * C // P])
+        nc.scalar.copy(out=gate_cols[:], in_=turned[:, 0:C // P])
+
+        rest = [[a1_t[b][:, t, :] for t in range(PACK)] for b in range(4)]
 
         def gather(s):
             g4 = [keep.tile([P, PACK, C], F32, name=f"g4_{e}{s}") for e in range(E)]
             for j in range(PACK):
-                for e in range(E):
-                    nc.vector.tensor_copy(
-                        out=g4[e][:, j, :],
-                        in_=dy[s * PACK + j][:].indirect(offsets[:, e * C // 16:(e + 1) * C // 16]),
-                    )
+                k = s * PACK + j
+                nc.vector.tensor_tensor(out=g4[0][:, j, :], in0=dy[k][:].indirect(offsets[:, 0:C // 16]), in1=gates[:], op=MULT)
+                nc.vector.tensor_copy(out=g4[1][:, j, :], in_=dy[k][:].indirect(offsets[:, C // 16:]))
+                rest[s][j] = keep.tile([P, C], F32, name=f"dy{k}")[:]
+                nc.scalar.activation(out=rest[s][j], in_=a1_t[s][:, j, :], func=ACT.Sigmoid, scale=-1.0)
+                engine = nc.gpsimd if k < 7 else nc.vector
+                engine.tensor_tensor(out=a3_t[s][:, j, :], in0=rest[s][j], in1=a3_t[s][:, j, :], op=MULT)
             return g4
 
         def interleaved(dst):
@@ -149,23 +171,28 @@ def tile_moe_bdx_glu_sigmoid_kernel(
         def planes(src):
             return src.rearrange("p t (c i) -> p c t i", i=4)
 
-        def quantise(src, name):
-            codes = keep.tile([P, C], U32, name=name + "_codes", align_bytes=64)
+        def quantise(src, name, slot=None):
+            codes = keep.tile([P, C], U32, name=slot or name + "_codes", align_bytes=64)
             scales = keep.tile([P, C], U8, name=name + "_scales", align_bytes=64)
             nc.vector.quantize_mx(
                 out=codes[:].bitcast(E5M2X4), scales=scales[:], in_=src.rearrange("p c t -> p (c t)")
             )
             return codes, scales
 
-        def weigh(e, g4):
+        def round_g(g4):
+            gb = ring2.tile([P, C, PACK], BF16, name="gb", align_bytes=64)
+            nc.scalar.copy(out=interleaved(gb[:]), in_=planes(g4[:]))
+            return gb
+
+        def weigh(g4):
             gb = ring2.tile([P, C, PACK], BF16, name="gb", align_bytes=64)
             words = gb[:].rearrange("p c t -> p (c t)").bitcast(F32).rearrange("p (a c u) -> p a c u", a=PACK, u=2)
             for half in range(2):
-                back = sums.tile([P, C], F32, name=f"dx{half}")
+                back = sums.tile([P, C], F32, name="dx1")
                 back4 = back[:].rearrange("p (a u c) -> p a u c", a=2, u=2)
                 for a in range(2):
                     tile = 2 * half + a
-                    across = banks.tile([P, C], F32, name="dh")
+                    across = turns.tile([P, C], F32, name="across")
                     for j in reversed(range(PACK)):
                         nc.tensor.transpose(across[:, j * P:(j + 1) * P], g4[:, j, tile * P:(tile + 1) * P], ident[:])
                     rounded = ring4.tile([P, PASS], BF16, name="rounded")
@@ -173,7 +200,7 @@ def tile_moe_bdx_glu_sigmoid_kernel(
                         out=rounded[:].rearrange("c (u p v) -> c u p v", u=2, v=2),
                         in_=across[:].rearrange("c (u v p) -> c u p v", u=2, v=2),
                         func=ACT.Copy,
-                        scale=gate_cols[:, e * PACK + tile:e * PACK + tile + 1],
+                        scale=gate_cols[:, tile:tile + 1],
                     )
                     pairs = rounded[:].bitcast(F32)
                     for u in range(2):
@@ -181,31 +208,25 @@ def tile_moe_bdx_glu_sigmoid_kernel(
                 nc.scalar.copy(out=words[:, 2 * half:2 * half + 2], in_=back4.rearrange("p a u c -> p a c u"))
             return gb
 
-        def finish_g(e, s, gb):
-            g_codes[e, s], g_scales[e, s] = quantise(gb[:], f"g{e}{s}")
+        def finish_g(e, s, gb, slot=None):
+            g_codes[e, s], g_scales[e, s] = quantise(gb[:], f"g{e}{s}", slot)
 
         def sigmoid(b):
-            nc.scalar.activation(out=a1_t[b][:], in_=a1_t[b][:], func=ACT.Sigmoid)
+            nc.scalar.activation(out=a1_t[b][:], in_=a1_t[b][:], func=ACT.Sigmoid, scale=-1.0)
 
         def slope(b):
-            v = a3_t[b]
-            nc.vector.scalar_tensor_tensor(out=v[:], in0=a1_t[b][:], scalar=1.0, in1=v[:], op0=SUB, op1=MULT)
+            nc.vector.tensor_tensor(out=a3_t[b][:], in0=a1_t[b][:], in1=a3_t[b][:], op=MULT)
 
-        g4 = gather(0)
-        sigmoid(0)
-        sigmoid(1)
-        gb00 = weigh(0, g4[0])
-        gb10 = weigh(1, g4[1])
+
+        g4_0 = gather(0)
+        gb00 = round_g(g4_0[0])
+        gb10 = weigh(g4_0[1])
+        g4_1 = gather(1)
         finish_g(0, 0, gb00)
-        finish_g(1, 0, gb10)
-        g4 = gather(1)
-        sigmoid(2)
-        gb01 = weigh(0, g4[0])
-        finish_g(0, 1, gb01)
-        gb11 = weigh(1, g4[1])
-        slope(0)
-        slope(1)
-        slope(2)
+        finish_g(0, 1, round_g(g4_1[0]))
+        finish_g(1, 0, gb10, "gates")
+        permute_w2(2)
+        permute_w2(3)
 
         dx = [sums.tile([P, C], F32, name=f"dx{e}") for e in range(E)]
         held = {}
@@ -226,13 +247,15 @@ def tile_moe_bdx_glu_sigmoid_kernel(
                         start=(s == 0),
                         stop=(s == 1),
                     )
-                nc.vector.tensor_tensor(out=u[:, t, :], in0=dh[:], in1=a1_t[b][:, t, :], op=MULT)
+                nc.vector.scalar_tensor_tensor(
+                    out=u[:, t, :], in0=rest[b][t], scalar=1.0, in1=dh[:], op0=SUB, op1=MULT
+                )
             held[b] = u
 
         def product(engine, b, first, last):
-            u, d = held[b]
+            u, d1, d3 = held[b]
             engine.tensor_tensor(
-                out=interleaved(d[:, 0, first:last, :]),
+                out=interleaved(d1[:, first:last, :]),
                 in0=planes(u[:, :, first:last]),
                 in1=planes(a3_t[b][:, :, first:last]),
                 op=MULT,
@@ -240,16 +263,17 @@ def tile_moe_bdx_glu_sigmoid_kernel(
 
         def gradients(b, share):
             u = held[b]
-            d = ring2.tile([P, 2, C, PACK], BF16, name="d", align_bytes=64)
-            held[b] = (u, d)
+            d1 = ring2.tile([P, C, PACK], BF16, name="d1", align_bytes=64)
+            d3 = ring2.tile([P, C, PACK], BF16, name="d3", align_bytes=64)
+            held[b] = (u, d1[:], d3[:])
             for first in range(0, share, 128):
                 product(nc.gpsimd, b, first, first + 128)
-            nc.scalar.activation(out=interleaved(d[:, 1]), in_=planes(u[:]), func=ACT.Copy, scale=-1.0)
+            nc.scalar.copy(out=interleaved(d3[:]), in_=planes(u[:]))
 
         def second_products(b):
             e, h = divmod(b, 2)
             for w in range(2):
-                codes, scales = quantise(held[b][1][:, w], f"d{w}_{b}")
+                codes, scales = quantise(held[b][1 + w], f"d{w}_{b}")
                 nc.tensor.matmul_mx(
                     out=dx[e][:],
                     lhsT=w13[w][:, b, :].bitcast(E2M1X4),
@@ -270,15 +294,16 @@ def tile_moe_bdx_glu_sigmoid_kernel(
         for b in range(4):
             share = 256 if b < 3 else 0
             gradients(b, share)
+            if b == 0:
+                gb11 = weigh(g4_1[1])
             if b == 1:
                 finish_g(1, 1, gb11)
             if b < 3:
                 first_products(b + 1)
             product(nc.vector, b, share, C)
-            if b == 0:
-                sigmoid(3)
-            if b == 1:
-                slope(3)
+            if b < 2:
+                sigmoid(b + 2)
+                slope(b + 2)
             second_products(b)
         landing = [ring2.tile([P, PACK, C], F32, name="u") for z in range(2)]
         for e in range(E):

@@ -39,9 +39,9 @@ def tile_moe_bdx_glu_sigmoid_kernel(
         gate_rows = keep.tile([P, P], F32, name="gate_rows")
         gate_cols = keep.tile([P, C // P], F32, name="gate_cols")
         ident = keep.tile([P, P], F32, name="ident")
-        dy = [keep.tile([P, T], F32, name=f"dy{b}") for b in range(N // P)]
+        dy = [keep.tile([P, T], F32, name=f"dy{b}", align_bytes=64) for b in range(N // P)]
         w2_raw = [keep.tile([P, 2 * H], U8, name=f"w2_raw{b}", align_bytes=64) for b in range(4)]
-        w2_put = [keep.tile([P, 2 * H], U8, name=f"w2_put{b}", align_bytes=64) for b in range(4)]
+        w2_put = [keep.tile([P, 2 * H], U8, name=f"w2_put{b}", align_bytes=64)[:] for b in range(2)]
         w2s_raw = keep.tile([P, H], U8, name="w2s_raw", align_bytes=64)
         w2s_put = [keep.tile([P, H], U8, name=f"w2s_put{b}", align_bytes=64) for b in range(4)]
         w13 = [keep.tile([P, 4, 2 * K], U8, name=f"w13_{b}", align_bytes=64) for b in range(2)]
@@ -89,32 +89,30 @@ def tile_moe_bdx_glu_sigmoid_kernel(
                     in_=w2s_put[0][32 * q + 4 * b:32 * q + 4 * b + 4, :].bitcast(I32),
                 )
 
-        def load_plane(k):
-            b, t = divmod(k, PACK)
-            load_saved(a1, a1_t, b, t, t + 1)
-            load_saved(a3, a3_t, b, t, t + 1)
+        def load_half(src, dst, b, half):
+            load_saved(src, dst, b, 2 * half, 2 * half + 2)
 
         load_w2(0)
         nc.sync.dma_start(offsets[:], offs)
-        load_w2(1)
-        nc.sync.dma_start(out=gates[:], in_=gate[0:P, 0:C])
         load_dy(0)
+        nc.sync.dma_start(out=gates[:], in_=gate[0:P, 0:C])
+        load_w2(1)
         load_dy(1)
-        load_plane(0)
         for q in range(4):
             nc.sync.dma_start(
                 out=w2s_raw[32 * q:32 * q + 16, :].bitcast(I32),
                 in_=w2_scales[:, :, 4 * q:4 * q + 4, :].bitcast(I32).rearrange("e s q i -> (e s) q i"),
             )
-        load_dy(2)
-        load_plane(1)
         nc.sync.dma_start(out=gate_rows[0:C // P, :], in_=gate[0, C:].rearrange("(c m) -> c m", m=P))
+        load_half(a1, a1_t, 0, 0)
+        load_dy(2)
+        load_half(a3, a3_t, 0, 0)
         load_dy(3)
-        load_plane(2)
+        load_half(a1, a1_t, 0, 1)
 
         def permute_w2(b):
             nc.vector.tensor_copy(
-                out=w2_put[b][:].bitcast(U16).rearrange("p (h t m) -> p h t m", h=2, t=PACK),
+                out=w2_put[b].bitcast(U16).rearrange("p (h t m) -> p h t m", h=2, t=PACK),
                 in_=w2_raw[b][:].bitcast(U16).rearrange("p (h m t) -> p h t m", h=2, t=PACK),
             )
 
@@ -125,17 +123,17 @@ def tile_moe_bdx_glu_sigmoid_kernel(
             in_=w2s_raw[:].rearrange("p (h m t) -> p h t m", h=2, t=PACK),
         )
         load_dy(4)
-        load_plane(3)
+        load_half(a3, a3_t, 0, 1)
         load_dy(5)
-        load_plane(4)
         move_scales(1)
+        load_half(a1, a1_t, 1, 0)
         load_dy(6)
-        load_plane(5)
+        load_half(a3, a3_t, 1, 0)
         load_dy(7)
-        load_plane(6)
-        load_plane(7)
         load_w2(2)
         load_w2(3)
+        load_half(a1, a1_t, 1, 1)
+        load_half(a3, a3_t, 1, 1)
         load_saved(a1, a1_t, 2)
         load_w13(0, w1_words, w1_scales)
         load_saved(a3, a3_t, 2)
@@ -153,17 +151,24 @@ def tile_moe_bdx_glu_sigmoid_kernel(
 
         rest = [[a1_t[b][:, t, :] for t in range(PACK)] for b in range(4)]
 
-        def gather(s):
-            g4 = [keep.tile([P, PACK, C], F32, name=f"g4_{e}{s}") for e in range(E)]
-            for j in range(PACK):
-                k = s * PACK + j
-                nc.vector.tensor_tensor(out=g4[0][:, j, :], in0=dy[k][:].indirect(offsets[:, 0:C // 16]), in1=gates[:], op=MULT)
-                nc.vector.tensor_copy(out=g4[1][:, j, :], in_=dy[k][:].indirect(offsets[:, C // 16:]))
-                rest[s][j] = keep.tile([P, C], F32, name=f"dy{k}")[:]
-                nc.scalar.activation(out=rest[s][j], in_=a1_t[s][:, j, :], func=ACT.Sigmoid, scale=-1.0)
-                engine = nc.gpsimd if k < 7 else nc.vector
-                engine.tensor_tensor(out=a3_t[s][:, j, :], in0=rest[s][j], in1=a3_t[s][:, j, :], op=MULT)
-            return g4
+        g4 = {(e, s): keep.tile([P, PACK, C], F32, name=f"g4_{e}{s}") for e in range(E) for s in range(2)}
+
+        def gather_weighed(k):
+            s, j = divmod(k, PACK)
+            nc.vector.tensor_tensor(out=g4[0, s][:, j, :], in0=dy[k][:].indirect(offsets[:, 0:C // 16]), in1=gates[:], op=MULT)
+
+        def gather_plain(k):
+            s, j = divmod(k, PACK)
+            nc.vector.tensor_copy(out=g4[1, s][:, j, :], in_=dy[k][:].indirect(offsets[:, C // 16:]))
+
+        def slope_beside(b, first, last, landing):
+            nc.scalar.activation(out=landing, in_=a1_t[b][:, first:last, :], func=ACT.Sigmoid, scale=-1.0)
+            for t in range(first, last):
+                rest[b][t] = landing[:, t - first, :]
+            nc.gpsimd.tensor_tensor(out=a3_t[b][:, first:last, :], in0=landing, in1=a3_t[b][:, first:last, :], op=MULT)
+
+        def in_dy_slot(k, count):
+            return keep.tile([P, count, C], F32, name=f"dy{k}", align_bytes=64)[:]
 
         def interleaved(dst):
             return dst.rearrange("p (c i) t -> p c t i", i=4)
@@ -179,34 +184,38 @@ def tile_moe_bdx_glu_sigmoid_kernel(
             )
             return codes, scales
 
-        def round_g(g4):
-            gb = ring2.tile([P, C, PACK], BF16, name="gb", align_bytes=64)
+        def round_g(g4, pool, slot):
+            gb = pool.tile([P, C, PACK], BF16, name=slot, align_bytes=64)
             nc.scalar.copy(out=interleaved(gb[:]), in_=planes(g4[:]))
             return gb
 
-        def weigh(g4):
-            gb = ring2.tile([P, C, PACK], BF16, name="gb", align_bytes=64)
-            words = gb[:].rearrange("p c t -> p (c t)").bitcast(F32).rearrange("p (a c u) -> p a c u", a=PACK, u=2)
+        def weigh(s, u, back):
             for half in range(2):
-                back = sums.tile([P, C], F32, name="dx1")
-                back4 = back[:].rearrange("p (a u c) -> p a u c", a=2, u=2)
+                across = turns.tile([P, 2, 2, P], F32, name="across")
                 for a in range(2):
                     tile = 2 * half + a
-                    across = turns.tile([P, C], F32, name="across")
-                    for j in reversed(range(PACK)):
-                        nc.tensor.transpose(across[:, j * P:(j + 1) * P], g4[:, j, tile * P:(tile + 1) * P], ident[:])
-                    rounded = ring4.tile([P, PASS], BF16, name="rounded")
+                    for v in (1, 0):
+                        nc.tensor.transpose(across[:, a, v, :], g4[1, s][:, 2 * u + v, tile * P:(tile + 1) * P], ident[:])
+                for a in range(2):
+                    tile = 2 * half + a
+                    rounded = ring4.tile([P, P, 2], BF16, name="rounded")
                     nc.scalar.activation(
-                        out=rounded[:].rearrange("c (u p v) -> c u p v", u=2, v=2),
-                        in_=across[:].rearrange("c (u v p) -> c u p v", u=2, v=2),
+                        out=rounded[:],
+                        in_=across[:, a].rearrange("c v p -> c p v"),
                         func=ACT.Copy,
                         scale=gate_cols[:, tile:tile + 1],
                     )
-                    pairs = rounded[:].bitcast(F32)
-                    for u in range(2):
-                        nc.tensor.transpose(back4[:, a, u, :], pairs[:, u * P:(u + 1) * P], ident[:])
-                nc.scalar.copy(out=words[:, 2 * half:2 * half + 2], in_=back4.rearrange("p a u c -> p a c u"))
+                    nc.tensor.transpose(back[half][:, a, u, :], rounded[:].rearrange("c p v -> c (p v)").bitcast(F32), ident[:])
+
+        def collect(back):
+            gb = keep.tile([P, C, PACK], BF16, name="gb", align_bytes=64)
+            words = gb[:].rearrange("p c t -> p (c t)").bitcast(F32).rearrange("p (a c u) -> p a c u", a=PACK, u=2)
+            for half in range(2):
+                nc.scalar.copy(out=words[:, 2 * half:2 * half + 2], in_=back[half][:].rearrange("p a u c -> p a c u"))
             return gb
+
+        def back_banks():
+            return [sums.tile([P, 2, 2, P], F32, name=f"dx{half}") for half in range(2)]
 
         def finish_g(e, s, gb, slot=None):
             g_codes[e, s], g_scales[e, s] = quantise(gb[:], f"g{e}{s}", slot)
@@ -218,15 +227,48 @@ def tile_moe_bdx_glu_sigmoid_kernel(
             nc.vector.tensor_tensor(out=a3_t[b][:], in0=a1_t[b][:], in1=a3_t[b][:], op=MULT)
 
 
-        g4_0 = gather(0)
-        gb00 = round_g(g4_0[0])
-        gb10 = weigh(g4_0[1])
-        g4_1 = gather(1)
-        finish_g(0, 0, gb00)
-        finish_g(0, 1, round_g(g4_1[0]))
+        for s in range(2):
+            back = back_banks()
+            for u in range(2):
+                k = s * PACK + 2 * u
+                gather_weighed(k)
+                gather_plain(k)
+                if k < 6:
+                    gather_plain(k + 1)
+                    gather_weighed(k + 1)
+                else:
+                    finish_g(0, 0, gb00, "dy6")
+                    slope_beside(1, 1, 2, keep.tile([P, 1, C], F32, name="early", align_bytes=64)[:])
+                    gather_weighed(k + 1)
+                    gather_plain(k + 1)
+                if k < 4:
+                    slope_beside(0, k, k + 2, in_dy_slot(k + 1, 2))
+                if k == 4:
+                    slope_beside(1, 0, 1, in_dy_slot(k + 1, 1))
+                if k == 2:
+                    gb00 = round_g(g4[0, 0], keep, "early")
+                if k == 6:
+                    g_codes[0, 1] = keep.tile([P, C], U32, name="g01_codes", align_bytes=64)
+                    g_scales[0, 1] = keep.tile([P, C], U8, name="g01_scales", align_bytes=64)
+                    for half in range(2):
+                        slots = slice(half * C // 2, (half + 1) * C // 2)
+                        gb = keep.tile([P, C // 2, PACK], BF16, name=f"late{half}", align_bytes=64)
+                        nc.scalar.copy(out=interleaved(gb[:]), in_=planes(g4[0, 1][:, :, slots]))
+                        nc.vector.quantize_mx(
+                            out=g_codes[0, 1][:, slots].bitcast(E5M2X4),
+                            scales=g_scales[0, 1][:, slots],
+                            in_=gb[:].rearrange("p c t -> p (c t)"),
+                        )
+                    slope_beside(1, 2, 4, keep.tile([P, 2, C], F32, name="late0", align_bytes=64)[:])
+                weigh(s, u, back)
+            if s == 0:
+                gb10 = collect(back)
         finish_g(1, 0, gb10, "gates")
-        permute_w2(2)
-        permute_w2(3)
+        w2_late = keep.tile([P, 2, 2 * H], U8, name="late1", align_bytes=64)
+        for b in range(2, 4):
+            w2_put.append(w2_late[:, b - 2, :])
+            permute_w2(b)
+        gb11 = collect(back)
 
         dx = [sums.tile([P, C], F32, name=f"dx{e}") for e in range(E)]
         held = {}
@@ -235,7 +277,10 @@ def tile_moe_bdx_glu_sigmoid_kernel(
             e, h = divmod(b, 2)
             u = ring2.tile([P, PACK, C], F32, name="u")
             for t in range(PACK):
-                dh = banks.tile([P, C], F32, name="dh")
+                if b == 1 and t < 2:
+                    dh = turns.tile([P, C], F32, name="across")
+                else:
+                    dh = banks.tile([P, C], F32, name="dh")
                 col = h * PASS + t * P
                 for s in range(2):
                     nc.tensor.matmul_mx(
@@ -266,8 +311,8 @@ def tile_moe_bdx_glu_sigmoid_kernel(
             d1 = ring2.tile([P, C, PACK], BF16, name="d1", align_bytes=64)
             d3 = ring2.tile([P, C, PACK], BF16, name="d3", align_bytes=64)
             held[b] = (u, d1[:], d3[:])
-            for first in range(0, share, 128):
-                product(nc.gpsimd, b, first, first + 128)
+            if share:
+                product(nc.gpsimd, b, 0, share)
             nc.scalar.copy(out=interleaved(d3[:]), in_=planes(u[:]))
 
         def second_products(b):
@@ -294,8 +339,6 @@ def tile_moe_bdx_glu_sigmoid_kernel(
         for b in range(4):
             share = 256 if b < 3 else 0
             gradients(b, share)
-            if b == 0:
-                gb11 = weigh(g4_1[1])
             if b == 1:
                 finish_g(1, 1, gb11)
             if b < 3:

@@ -28,25 +28,26 @@ def tile_moe_bdx_glu_sigmoid_kernel(
     nc = tc.nc
     with ExitStack() as ctx:
         keep = ctx.enter_context(tc.tile_pool(name="keep", bufs=1))
-        ring4 = ctx.enter_context(tc.tile_pool(name="ring4", bufs=4))
         ring2 = ctx.enter_context(tc.tile_pool(name="ring2", bufs=2))
         banks = ctx.enter_context(tc.psum_pool(name="banks", bufs=4))
         turns = ctx.enter_context(tc.psum_pool(name="turns", bufs=2))
         sums = ctx.enter_context(tc.psum_pool(name="sums", bufs=1))
 
         offsets = keep.tile([P, E * C // 16], U16, name="offsets")
-        gates = keep.tile([P, C], F32, name="gates", align_bytes=64)
+        gates = keep.tile([P, C], F32, name="gates")
         gate_rows = keep.tile([P, P], F32, name="gate_rows")
         gate_cols = keep.tile([P, C // P], F32, name="gate_cols")
         ident = keep.tile([P, P], F32, name="ident")
         dy = [keep.tile([P, T], F32, name=f"dy{b}", align_bytes=64) for b in range(N // P)]
-        w2_raw = [keep.tile([P, 2 * H], U8, name=f"w2_raw{b}", align_bytes=64) for b in range(4)]
-        w2_put = [keep.tile([P, 2 * H], U8, name=f"w2_put{b}", align_bytes=64)[:] for b in range(2)]
+        slopes1 = keep.tile([P, PACK * C], F32, name="slopes1", align_bytes=64)
+        a1_late = keep.tile([P, 2, C], F32, name="a1_late")
+        w2_raw = [keep.tile([P, 2 * H], U8, name=f"w2_raw{b}", align_bytes=64)[:] for b in range(4)]
+        w2_put = [keep.tile([P, 2 * H], U8, name=f"w2_put{b}", align_bytes=64)[:] for b in range(4)]
         w2s_raw = keep.tile([P, H], U8, name="w2s_raw", align_bytes=64)
         w2s_put = [keep.tile([P, H], U8, name=f"w2s_put{b}", align_bytes=64) for b in range(4)]
         w13 = [keep.tile([P, 4, 2 * K], U8, name=f"w13_{b}", align_bytes=64) for b in range(2)]
         w13s = keep.tile([P, 2, 4, K], U8, name="w13s", align_bytes=64)
-        a1_t = [keep.tile([P, PACK, C], F32, name=f"a1_{b}") for b in range(4)]
+        a1_t = [keep.tile([P, PACK if b else 2, C], F32, name=f"a1_{b}") for b in range(4)]
         a3_t = [keep.tile([P, PACK, C], F32, name=f"a3_{b}", align_bytes=64) for b in range(4)]
         result = keep.tile([P, T], F32, name="result")
 
@@ -58,7 +59,7 @@ def tile_moe_bdx_glu_sigmoid_kernel(
         nc.gpsimd.memset(w13s[:].rearrange("p w b k -> p (w b k)").bitcast(I32), 0)
 
         def load_w2(b):
-            nc.sync.dma_start(out=w2_raw[b][:].bitcast(I32), in_=w2_words[b // 2, b % 2].bitcast(I32))
+            nc.sync.dma_start(out=w2_raw[b].bitcast(I32), in_=w2_words[b // 2, b % 2].bitcast(I32))
 
         def load_dy(b):
             s, j = divmod(b, PACK)
@@ -108,16 +109,17 @@ def tile_moe_bdx_glu_sigmoid_kernel(
         load_dy(2)
         load_half(a3, a3_t, 0, 0)
         load_dy(3)
-        load_half(a1, a1_t, 0, 1)
+        nc.sync.dma_start(out=a1_late[:], in_=a1[0:PASS, 0:C].rearrange("(p j) c -> p j c", j=PACK)[:, 2:4, :])
+        load_w2(2)
 
         def permute_w2(b):
             nc.vector.tensor_copy(
                 out=w2_put[b].bitcast(U16).rearrange("p (h t m) -> p h t m", h=2, t=PACK),
-                in_=w2_raw[b][:].bitcast(U16).rearrange("p (h m t) -> p h t m", h=2, t=PACK),
+                in_=w2_raw[b].bitcast(U16).rearrange("p (h m t) -> p h t m", h=2, t=PACK),
             )
 
-        permute_w2(0)
-        permute_w2(1)
+        for b in range(3):
+            permute_w2(b)
         nc.vector.tensor_copy(
             out=w2s_put[0][:].rearrange("p (h t m) -> p h t m", h=2, t=PACK),
             in_=w2s_raw[:].rearrange("p (h m t) -> p h t m", h=2, t=PACK),
@@ -128,10 +130,10 @@ def tile_moe_bdx_glu_sigmoid_kernel(
         move_scales(1)
         load_half(a1, a1_t, 1, 0)
         load_dy(6)
-        load_half(a3, a3_t, 1, 0)
-        load_dy(7)
-        load_w2(2)
         load_w2(3)
+        permute_w2(3)
+        load_dy(7)
+        load_half(a3, a3_t, 1, 0)
         load_half(a1, a1_t, 1, 1)
         load_half(a3, a3_t, 1, 1)
         load_saved(a1, a1_t, 2)
@@ -149,26 +151,27 @@ def tile_moe_bdx_glu_sigmoid_kernel(
         nc.tensor.transpose(turned[:, 0:P], gate_rows[:], ident[:])
         nc.scalar.copy(out=gate_cols[:], in_=turned[:, 0:C // P])
 
-        rest = [[a1_t[b][:, t, :] for t in range(PACK)] for b in range(4)]
-
-        g4 = {(e, s): keep.tile([P, PACK, C], F32, name=f"g4_{e}{s}") for e in range(E) for s in range(2)}
+        weighed = [keep.tile([P, PACK, C], F32, name=f"weighed{s}") for s in range(2)]
+        plain = [None] * (2 * PACK)
+        slopes = [None, slopes1[:].rearrange("p (t c) -> p t c", t=PACK), a3_t[2][:], a3_t[3][:]]
+        rest = [[a1_t[b][:, t % a1_t[b].shape[1], :] for t in range(PACK)] for b in range(4)]
 
         def gather_weighed(k):
             s, j = divmod(k, PACK)
-            nc.vector.tensor_tensor(out=g4[0, s][:, j, :], in0=dy[k][:].indirect(offsets[:, 0:C // 16]), in1=gates[:], op=MULT)
+            nc.vector.tensor_tensor(out=weighed[s][:, j, :], in0=dy[k][:].indirect(offsets[:, 0:C // 16]), in1=gates[:], op=MULT)
 
-        def gather_plain(k):
-            s, j = divmod(k, PACK)
-            nc.vector.tensor_copy(out=g4[1, s][:, j, :], in_=dy[k][:].indirect(offsets[:, C // 16:]))
+        def gather_plain(k, slot):
+            plain[k] = keep.tile([P, C], F32, name=slot)
+            nc.vector.tensor_copy(out=plain[k][:], in_=dy[k][:].indirect(offsets[:, C // 16:]))
 
-        def slope_beside(b, first, last, landing):
-            nc.scalar.activation(out=landing, in_=a1_t[b][:, first:last, :], func=ACT.Sigmoid, scale=-1.0)
-            for t in range(first, last):
-                rest[b][t] = landing[:, t - first, :]
-            nc.gpsimd.tensor_tensor(out=a3_t[b][:, first:last, :], in0=landing, in1=a3_t[b][:, first:last, :], op=MULT)
+        def slope_beside(b, half, src, dst):
+            pair = slice(2 * half, 2 * half + 2)
+            nc.scalar.activation(out=dst, in_=src, func=ACT.Sigmoid, scale=-1.0)
+            rest[b][2 * half], rest[b][2 * half + 1] = dst[:, 0, :], dst[:, 1, :]
+            nc.gpsimd.tensor_tensor(out=slopes[b][:, pair, :], in0=dst, in1=a3_t[b][:, pair, :], op=MULT)
 
-        def in_dy_slot(k, count):
-            return keep.tile([P, count, C], F32, name=f"dy{k}", align_bytes=64)[:]
+        def staging(half):
+            return slopes1[:, 2 * half * C:2 * (half + 1) * C].bitcast(BF16).rearrange("p (c t) -> p c t", t=PACK)
 
         def interleaved(dst):
             return dst.rearrange("p (c i) t -> p c t i", i=4)
@@ -184,41 +187,34 @@ def tile_moe_bdx_glu_sigmoid_kernel(
             )
             return codes, scales
 
-        def round_g(g4, pool, slot):
-            gb = pool.tile([P, C, PACK], BF16, name=slot, align_bytes=64)
-            nc.scalar.copy(out=interleaved(gb[:]), in_=planes(g4[:]))
-            return gb
-
-        def weigh(s, u, back):
+        def weigh(s, u, back, slot):
+            rounded = keep.tile([P, PACK, P, 2], BF16, name=slot)
             for half in range(2):
                 across = turns.tile([P, 2, 2, P], F32, name="across")
                 for a in range(2):
                     tile = 2 * half + a
                     for v in (1, 0):
-                        nc.tensor.transpose(across[:, a, v, :], g4[1, s][:, 2 * u + v, tile * P:(tile + 1) * P], ident[:])
+                        nc.tensor.transpose(across[:, a, v, :], plain[s * PACK + 2 * u + v][:, tile * P:(tile + 1) * P], ident[:])
                 for a in range(2):
                     tile = 2 * half + a
-                    rounded = ring4.tile([P, P, 2], BF16, name="rounded")
                     nc.scalar.activation(
-                        out=rounded[:],
+                        out=rounded[:, tile],
                         in_=across[:, a].rearrange("c v p -> c p v"),
                         func=ACT.Copy,
                         scale=gate_cols[:, tile:tile + 1],
                     )
-                    nc.tensor.transpose(back[half][:, a, u, :], rounded[:].rearrange("c p v -> c (p v)").bitcast(F32), ident[:])
+                    nc.tensor.transpose(back[half][:, a, u, :], rounded[:, tile].rearrange("c p v -> c (p v)").bitcast(F32), ident[:])
 
-        def collect(back):
-            gb = keep.tile([P, C, PACK], BF16, name="gb", align_bytes=64)
-            words = gb[:].rearrange("p c t -> p (c t)").bitcast(F32).rearrange("p (a c u) -> p a c u", a=PACK, u=2)
+        def collect(back, gb):
+            words = gb.rearrange("p c t -> p (c t)").bitcast(F32).rearrange("p (a c u) -> p a c u", a=PACK, u=2)
             for half in range(2):
                 nc.scalar.copy(out=words[:, 2 * half:2 * half + 2], in_=back[half][:].rearrange("p a u c -> p a c u"))
-            return gb
 
         def back_banks():
             return [sums.tile([P, 2, 2, P], F32, name=f"dx{half}") for half in range(2)]
 
         def finish_g(e, s, gb, slot=None):
-            g_codes[e, s], g_scales[e, s] = quantise(gb[:], f"g{e}{s}", slot)
+            g_codes[e, s], g_scales[e, s] = quantise(gb, f"g{e}{s}", slot)
 
         def sigmoid(b):
             nc.scalar.activation(out=a1_t[b][:], in_=a1_t[b][:], func=ACT.Sigmoid, scale=-1.0)
@@ -227,48 +223,44 @@ def tile_moe_bdx_glu_sigmoid_kernel(
             nc.vector.tensor_tensor(out=a3_t[b][:], in0=a1_t[b][:], in1=a3_t[b][:], op=MULT)
 
 
-        for s in range(2):
-            back = back_banks()
-            for u in range(2):
-                k = s * PACK + 2 * u
-                gather_weighed(k)
-                gather_plain(k)
-                if k < 6:
-                    gather_plain(k + 1)
-                    gather_weighed(k + 1)
-                else:
-                    finish_g(0, 0, gb00, "dy6")
-                    slope_beside(1, 1, 2, keep.tile([P, 1, C], F32, name="early", align_bytes=64)[:])
-                    gather_weighed(k + 1)
-                    gather_plain(k + 1)
-                if k < 4:
-                    slope_beside(0, k, k + 2, in_dy_slot(k + 1, 2))
-                if k == 4:
-                    slope_beside(1, 0, 1, in_dy_slot(k + 1, 1))
-                if k == 2:
-                    gb00 = round_g(g4[0, 0], keep, "early")
-                if k == 6:
-                    g_codes[0, 1] = keep.tile([P, C], U32, name="g01_codes", align_bytes=64)
-                    g_scales[0, 1] = keep.tile([P, C], U8, name="g01_scales", align_bytes=64)
-                    for half in range(2):
-                        slots = slice(half * C // 2, (half + 1) * C // 2)
-                        gb = keep.tile([P, C // 2, PACK], BF16, name=f"late{half}", align_bytes=64)
-                        nc.scalar.copy(out=interleaved(gb[:]), in_=planes(g4[0, 1][:, :, slots]))
-                        nc.vector.quantize_mx(
-                            out=g_codes[0, 1][:, slots].bitcast(E5M2X4),
-                            scales=g_scales[0, 1][:, slots],
-                            in_=gb[:].rearrange("p c t -> p (c t)"),
-                        )
-                    slope_beside(1, 2, 4, keep.tile([P, 2, C], F32, name="late0", align_bytes=64)[:])
-                weigh(s, u, back)
-            if s == 0:
-                gb10 = collect(back)
-        finish_g(1, 0, gb10, "gates")
-        w2_late = keep.tile([P, 2, 2 * H], U8, name="late1", align_bytes=64)
-        for b in range(2, 4):
-            w2_put.append(w2_late[:, b - 2, :])
-            permute_w2(b)
-        gb11 = collect(back)
+        back = back_banks()
+        for k in (0, 2, 4):
+            gather_weighed(k)
+            gather_plain(k, f"plain{k}")
+            gather_plain(k + 1, f"plain{k + 1}")
+            gather_weighed(k + 1)
+            if k == 0:
+                slopes[0] = keep.tile([P, PACK, C], F32, name="dy1", align_bytes=64)[:]
+                slope_beside(0, 0, a1_t[0][:], a1_t[0][:])
+            if k == 2:
+                slope_beside(0, 1, a1_late[:], keep.tile([P, 2, C], F32, name="dy3", align_bytes=64)[:])
+                nc.scalar.copy(out=interleaved(staging(0)), in_=planes(weighed[0][:]))
+            weigh(k // 4, k // 2 % 2, back, "a1_late" if k == 2 else "rounded")
+            if k == 2:
+                collect(back, staging(1))
+                back = back_banks()
+        gather_weighed(6)
+        finish_g(0, 0, staging(0), "w2_raw3")
+        slope_beside(1, 0, a1_t[1][:, 0:2, :], a1_t[1][:, 0:2, :])
+        gather_weighed(7)
+        gather_plain(6, "gates")
+        gather_plain(7, "plain7")
+        g_codes[0, 1] = keep.tile([P, C], U32, name="g01_codes", align_bytes=64)
+        g_scales[0, 1] = keep.tile([P, C], U8, name="g01_scales", align_bytes=64)
+        for half in range(2):
+            slots = slice(half * C // 2, (half + 1) * C // 2)
+            gb = keep.tile([P, C // 2, PACK], BF16, name=f"late{half}", align_bytes=64)
+            nc.scalar.copy(out=interleaved(gb[:]), in_=planes(weighed[1][:, :, slots]))
+            nc.vector.quantize_mx(
+                out=g_codes[0, 1][:, slots].bitcast(E5M2X4),
+                scales=g_scales[0, 1][:, slots],
+                in_=gb[:].rearrange("p c t -> p (c t)"),
+            )
+        finish_g(1, 0, staging(1), "late1")
+        slope_beside(1, 1, a1_t[1][:, 2:4, :], a1_t[1][:, 2:4, :])
+        weigh(1, 1, back, "rounded")
+        gb11 = keep.tile([P, C, PACK], BF16, name="dy0", align_bytes=64)[:]
+        collect(back, gb11)
 
         dx = [sums.tile([P, C], F32, name=f"dx{e}") for e in range(E)]
         held = {}
@@ -302,7 +294,7 @@ def tile_moe_bdx_glu_sigmoid_kernel(
             engine.tensor_tensor(
                 out=interleaved(d1[:, first:last, :]),
                 in0=planes(u[:, :, first:last]),
-                in1=planes(a3_t[b][:, :, first:last]),
+                in1=planes(slopes[b][:, :, first:last]),
                 op=MULT,
             )
 
@@ -311,8 +303,8 @@ def tile_moe_bdx_glu_sigmoid_kernel(
             d1 = ring2.tile([P, C, PACK], BF16, name="d1", align_bytes=64)
             d3 = ring2.tile([P, C, PACK], BF16, name="d3", align_bytes=64)
             held[b] = (u, d1[:], d3[:])
-            if share:
-                product(nc.gpsimd, b, 0, share)
+            for first in range(0, share, 128):
+                product(nc.gpsimd, b, first, first + 128)
             nc.scalar.copy(out=interleaved(d3[:]), in_=planes(u[:]))
 
         def second_products(b):

@@ -1,4 +1,5 @@
 from contextlib import ExitStack
+from itertools import product
 
 import concourse.mybir as mybir
 from concourse.masks import make_identity
@@ -19,6 +20,7 @@ P = 128
 PACK = 4
 PASS = P * PACK
 K, T, E, C, H, N = 128, 1024, 2, 512, 1024, 1024
+GROUPS = C // P
 FLOPS = 2 * E * C * (N * H + 2 * H * K)
 
 
@@ -28,53 +30,54 @@ def tile_moe_bdx_glu_sigmoid_kernel(
     nc = tc.nc
     with ExitStack() as ctx:
         keep = ctx.enter_context(tc.tile_pool(name="keep", bufs=1))
-        ring2 = ctx.enter_context(tc.tile_pool(name="ring2", bufs=2))
-        banks = ctx.enter_context(tc.psum_pool(name="banks", bufs=4))
+        ring = ctx.enter_context(tc.psum_pool(name="ring", bufs=6))
         turns = ctx.enter_context(tc.psum_pool(name="turns", bufs=2))
-        sums = ctx.enter_context(tc.psum_pool(name="sums", bufs=1))
+
+        def held(shape, dtype, slot):
+            return keep.tile(shape, dtype, name=slot, align_bytes=64)
 
         offsets = keep.tile([P, E * C // 16], U16, name="offsets")
-        gates = keep.tile([P, C], F32, name="gates")
-        gate_rows = keep.tile([P, P], F32, name="gate_rows")
-        gate_cols = keep.tile([P, C // P], F32, name="gate_cols")
-        ident = keep.tile([P, P], F32, name="ident")
-        dy = [keep.tile([P, T], F32, name=f"dy{b}", align_bytes=64) for b in range(N // P)]
-        slopes1 = keep.tile([P, PACK * C], F32, name="slopes1", align_bytes=64)
-        a1_late = keep.tile([P, 2, C], F32, name="a1_late")
-        w2_raw = [keep.tile([P, 2 * H], U8, name=f"w2_raw{b}", align_bytes=64)[:] for b in range(4)]
-        w2_put = [keep.tile([P, 2 * H], U8, name=f"w2_put{b}", align_bytes=64)[:] for b in range(4)]
-        w2s_raw = keep.tile([P, H], U8, name="w2s_raw", align_bytes=64)
-        w2s_put = [keep.tile([P, H], U8, name=f"w2s_put{b}", align_bytes=64) for b in range(4)]
-        w13 = [keep.tile([P, 4, 2 * K], U8, name=f"w13_{b}", align_bytes=64) for b in range(2)]
-        w13s = keep.tile([P, 2, 4, K], U8, name="w13s", align_bytes=64)
-        a1_t = [keep.tile([P, PACK if b else 2, C], F32, name=f"a1_{b}") for b in range(4)]
-        a3_t = [keep.tile([P, PACK, C], F32, name=f"a3_{b}", align_bytes=64) for b in range(4)]
-        result = keep.tile([P, T], F32, name="result")
+        ident = held([P, P], F32, "ident")
+        gates = [held([P, C], F32, f"gate{e}") for e in range(E)]
+        dy = [held([P, T], F32, f"dy{k}") for k in range(N // P)]
+        w2 = [held([P, 2, 2 * H], U8, f"w2_{e}") for e in range(E)]
+        w2s = held([P, 2 * E, H], U8, "w2s")
+        w13 = [held([P, 4, 2 * K], U8, f"w13_{w}") for w in range(2)]
+        w13s = held([P, 2, 4, K], U8, "w13s")
+        a1_t = [held([P, PACK, C], F32, f"a1_{b}") for b in range(4)]
+        a3_t = [held([P, PACK, C], F32, f"a3_{b}") for b in range(4)]
+        across = [held([P, GROUPS, PACK, P], F32, f"across{b}") for b in range(4)]
+        result = held([P, T], F32, "result")
 
-        nc.gpsimd.memset(w2s_raw[:].bitcast(I32), 0)
-        nc.gpsimd.memset(gate_rows[:], 0.0)
         make_identity(nc, ident[:])
-        for b in range(1, 4):
-            nc.gpsimd.memset(w2s_put[b][:].bitcast(I32), 0)
-        nc.gpsimd.memset(w13s[:].rearrange("p w b k -> p (w b k)").bitcast(I32), 0)
+        nc.vector.memset(w2s[:].rearrange("p b i -> p (b i)").bitcast(I32), 0)
+        nc.vector.memset(w13s[:].rearrange("p w b k -> p (w b k)").bitcast(I32), 0)
 
-        def load_w2(b):
-            nc.sync.dma_start(out=w2_raw[b].bitcast(I32), in_=w2_words[b // 2, b % 2].bitcast(I32))
+        def load_gate(e):
+            nc.sync.dma_start(out=gates[e][:], in_=gate[0:P, e * C:(e + 1) * C])
 
-        def load_dy(b):
-            s, j = divmod(b, PACK)
-            nc.sync.dma_start(out=dy[b][:], in_=dyT[s * PASS:(s + 1) * PASS].rearrange("(p j) w -> p j w", j=PACK)[:, j, :])
+        def load_dy(k):
+            s, j = divmod(k, PACK)
+            nc.sync.dma_start(out=dy[k][:], in_=dyT[s * PASS:(s + 1) * PASS].rearrange("(p j) w -> p j w", j=PACK)[:, j, :])
 
-        def load_w13(w, words, scales):
+        def load_words(dst, words, n):
             nc.sync.dma_start(
-                out=w13[w][:].rearrange("p b i -> p (b i)").bitcast(I32).rearrange("p (b i) -> p b i", b=4),
-                in_=words.bitcast(I32).rearrange("e s p i -> p (e s) i"),
+                out=dst[:].rearrange("p b i -> p (b i)").bitcast(I32).rearrange("p (b i) -> p b i", b=n),
+                in_=words,
             )
+
+        def load_scales(dst, scales):
             for q in range(4):
                 nc.sync.dma_start(
-                    out=w13s[32 * q:32 * q + 4, w].rearrange("p b i -> p (b i)").bitcast(I32).rearrange("p (b i) -> p b i", b=4),
+                    out=dst[32 * q:32 * q + 4].rearrange("p b i -> p (b i)").bitcast(I32).rearrange("p (b i) -> p b i", b=4),
                     in_=scales[:, :, 4 * q:4 * q + 4, :].bitcast(I32).rearrange("e s q i -> q (e s) i"),
                 )
+
+        def load_w2(e):
+            load_words(w2[e], w2_words[e].bitcast(I32).rearrange("s p i -> p s i"), 2)
+
+        def load_w13(w, words):
+            load_words(w13[w], words.bitcast(I32).rearrange("e s p i -> p (e s) i"), 4)
 
         def load_saved(src, dst, b, first=0, last=PACK):
             e, h = divmod(b, 2)
@@ -83,95 +86,30 @@ def tile_moe_bdx_glu_sigmoid_kernel(
                 in_=src[h * PASS:(h + 1) * PASS, e * C:(e + 1) * C].rearrange("(p j) c -> p j c", j=PACK)[:, first:last, :],
             )
 
-        def move_scales(b):
-            for q in range(4):
-                nc.sync.dma_start(
-                    out=w2s_put[b][32 * q:32 * q + 4, :].bitcast(I32),
-                    in_=w2s_put[0][32 * q + 4 * b:32 * q + 4 * b + 4, :].bitcast(I32),
-                )
-
-        def load_half(src, dst, b, half):
-            load_saved(src, dst, b, 2 * half, 2 * half + 2)
-
-        load_w2(0)
         nc.sync.dma_start(offsets[:], offs)
+        load_gate(0)
         load_dy(0)
-        nc.sync.dma_start(out=gates[:], in_=gate[0:P, 0:C])
-        load_w2(1)
+        load_gate(1)
         load_dy(1)
-        for q in range(4):
-            nc.sync.dma_start(
-                out=w2s_raw[32 * q:32 * q + 16, :].bitcast(I32),
-                in_=w2_scales[:, :, 4 * q:4 * q + 4, :].bitcast(I32).rearrange("e s q i -> (e s) q i"),
-            )
-        nc.sync.dma_start(out=gate_rows[0:C // P, :], in_=gate[0, C:].rearrange("(c m) -> c m", m=P))
-        load_half(a1, a1_t, 0, 0)
+        load_saved(a1, a1_t, 0, 0, 2)
         load_dy(2)
-        load_half(a3, a3_t, 0, 0)
-        load_dy(3)
-        nc.sync.dma_start(out=a1_late[:], in_=a1[0:PASS, 0:C].rearrange("(p j) c -> p j c", j=PACK)[:, 2:4, :])
-        load_w2(2)
-
-        def permute_w2(b):
-            nc.vector.tensor_copy(
-                out=w2_put[b].bitcast(U16).rearrange("p (h t m) -> p h t m", h=2, t=PACK),
-                in_=w2_raw[b].bitcast(U16).rearrange("p (h m t) -> p h t m", h=2, t=PACK),
-            )
-
-        for b in range(3):
-            permute_w2(b)
-        nc.vector.tensor_copy(
-            out=w2s_put[0][:].rearrange("p (h t m) -> p h t m", h=2, t=PACK),
-            in_=w2s_raw[:].rearrange("p (h m t) -> p h t m", h=2, t=PACK),
-        )
-        load_dy(4)
-        load_half(a3, a3_t, 0, 1)
-        load_dy(5)
-        move_scales(1)
-        load_half(a1, a1_t, 1, 0)
-        load_dy(6)
-        load_w2(3)
-        permute_w2(3)
-        load_dy(7)
-        load_half(a3, a3_t, 1, 0)
-        load_half(a1, a1_t, 1, 1)
-        load_half(a3, a3_t, 1, 1)
+        load_saved(a1, a1_t, 0, 2, 4)
+        for k in range(3, 8):
+            load_dy(k)
+        load_saved(a1, a1_t, 1)
+        load_scales(w2s, w2_scales)
+        load_w2(0)
+        load_saved(a3, a3_t, 0)
+        load_w2(1)
         load_saved(a1, a1_t, 2)
-        load_w13(0, w1_words, w1_scales)
-        load_saved(a3, a3_t, 2)
-        load_w13(1, w3_words, w3_scales)
+        load_scales(w13s[:, 0], w1_scales)
+        load_saved(a3, a3_t, 1)
         load_saved(a1, a1_t, 3)
-        move_scales(2)
+        load_scales(w13s[:, 1], w3_scales)
+        load_w13(0, w1_words)
+        load_w13(1, w3_words)
+        load_saved(a3, a3_t, 2)
         load_saved(a3, a3_t, 3)
-        move_scales(3)
-
-        g_codes, g_scales = {}, {}
-
-        turned = turns.tile([P, C], F32, name="across")
-        nc.tensor.transpose(turned[:, 0:P], gate_rows[:], ident[:])
-        nc.scalar.copy(out=gate_cols[:], in_=turned[:, 0:C // P])
-
-        weighed = [keep.tile([P, PACK, C], F32, name=f"weighed{s}") for s in range(2)]
-        plain = [None] * (2 * PACK)
-        slopes = [None, slopes1[:].rearrange("p (t c) -> p t c", t=PACK), a3_t[2][:], a3_t[3][:]]
-        rest = [[a1_t[b][:, t % a1_t[b].shape[1], :] for t in range(PACK)] for b in range(4)]
-
-        def gather_weighed(k):
-            s, j = divmod(k, PACK)
-            nc.vector.tensor_tensor(out=weighed[s][:, j, :], in0=dy[k][:].indirect(offsets[:, 0:C // 16]), in1=gates[:], op=MULT)
-
-        def gather_plain(k, slot):
-            plain[k] = keep.tile([P, C], F32, name=slot)
-            nc.vector.tensor_copy(out=plain[k][:], in_=dy[k][:].indirect(offsets[:, C // 16:]))
-
-        def slope_beside(b, half, src, dst):
-            pair = slice(2 * half, 2 * half + 2)
-            nc.scalar.activation(out=dst, in_=src, func=ACT.Sigmoid, scale=-1.0)
-            rest[b][2 * half], rest[b][2 * half + 1] = dst[:, 0, :], dst[:, 1, :]
-            nc.gpsimd.tensor_tensor(out=slopes[b][:, pair, :], in0=dst, in1=a3_t[b][:, pair, :], op=MULT)
-
-        def staging(half):
-            return slopes1[:, 2 * half * C:2 * (half + 1) * C].bitcast(BF16).rearrange("p (c t) -> p c t", t=PACK)
 
         def interleaved(dst):
             return dst.rearrange("p (c i) t -> p c t i", i=4)
@@ -179,169 +117,173 @@ def tile_moe_bdx_glu_sigmoid_kernel(
         def planes(src):
             return src.rearrange("p t (c i) -> p c t i", i=4)
 
-        def quantise(src, name, slot=None):
-            codes = keep.tile([P, C], U32, name=slot or name + "_codes", align_bytes=64)
-            scales = keep.tile([P, C], U8, name=name + "_scales", align_bytes=64)
-            nc.vector.quantize_mx(
-                out=codes[:].bitcast(E5M2X4), scales=scales[:], in_=src.rearrange("p c t -> p (c t)")
-            )
+        def quantise(src, slot, name):
+            width = src.shape[1]
+            codes = held([P, width], U32, slot)
+            scales = held([P, width], U8, name)
+            nc.vector.quantize_mx(out=codes[:].bitcast(E5M2X4), scales=scales[:], in_=src.rearrange("p c t -> p (c t)"))
             return codes, scales
 
-        def weigh(s, u, back, slot):
-            rounded = keep.tile([P, PACK, P, 2], BF16, name=slot)
-            for half in range(2):
-                across = turns.tile([P, 2, 2, P], F32, name="across")
-                for a in range(2):
-                    tile = 2 * half + a
-                    for v in (1, 0):
-                        nc.tensor.transpose(across[:, a, v, :], plain[s * PACK + 2 * u + v][:, tile * P:(tile + 1) * P], ident[:])
-                for a in range(2):
-                    tile = 2 * half + a
-                    nc.scalar.activation(
-                        out=rounded[:, tile],
-                        in_=across[:, a].rearrange("c v p -> c p v"),
-                        func=ACT.Copy,
-                        scale=gate_cols[:, tile:tile + 1],
-                    )
-                    nc.tensor.transpose(back[half][:, a, u, :], rounded[:, tile].rearrange("c p v -> c (p v)").bitcast(F32), ident[:])
-
-        def collect(back, gb):
-            words = gb.rearrange("p c t -> p (c t)").bitcast(F32).rearrange("p (a c u) -> p a c u", a=PACK, u=2)
-            for half in range(2):
-                nc.scalar.copy(out=words[:, 2 * half:2 * half + 2], in_=back[half][:].rearrange("p a u c -> p a c u"))
-
-        def back_banks():
-            return [sums.tile([P, 2, 2, P], F32, name=f"dx{half}") for half in range(2)]
-
-        def finish_g(e, s, gb, slot=None):
-            g_codes[e, s], g_scales[e, s] = quantise(gb, f"g{e}{s}", slot)
-
-        def sigmoid(b):
-            nc.scalar.activation(out=a1_t[b][:], in_=a1_t[b][:], func=ACT.Sigmoid, scale=-1.0)
-
-        def slope(b):
-            nc.vector.tensor_tensor(out=a3_t[b][:], in0=a1_t[b][:], in1=a3_t[b][:], op=MULT)
-
-
-        back = back_banks()
-        for k in (0, 2, 4):
-            gather_weighed(k)
-            gather_plain(k, f"plain{k}")
-            gather_plain(k + 1, f"plain{k + 1}")
-            gather_weighed(k + 1)
-            if k == 0:
-                slopes[0] = keep.tile([P, PACK, C], F32, name="dy1", align_bytes=64)[:]
-                slope_beside(0, 0, a1_t[0][:], a1_t[0][:])
-            if k == 2:
-                slope_beside(0, 1, a1_late[:], keep.tile([P, 2, C], F32, name="dy3", align_bytes=64)[:])
-                nc.scalar.copy(out=interleaved(staging(0)), in_=planes(weighed[0][:]))
-            weigh(k // 4, k // 2 % 2, back, "a1_late" if k == 2 else "rounded")
-            if k == 2:
-                collect(back, staging(1))
-                back = back_banks()
-        gather_weighed(6)
-        finish_g(0, 0, staging(0), "w2_raw3")
-        slope_beside(1, 0, a1_t[1][:, 0:2, :], a1_t[1][:, 0:2, :])
-        gather_weighed(7)
-        gather_plain(6, "gates")
-        gather_plain(7, "plain7")
-        g_codes[0, 1] = keep.tile([P, C], U32, name="g01_codes", align_bytes=64)
-        g_scales[0, 1] = keep.tile([P, C], U8, name="g01_scales", align_bytes=64)
-        for half in range(2):
-            slots = slice(half * C // 2, (half + 1) * C // 2)
-            gb = keep.tile([P, C // 2, PACK], BF16, name=f"late{half}", align_bytes=64)
-            nc.scalar.copy(out=interleaved(gb[:]), in_=planes(weighed[1][:, :, slots]))
-            nc.vector.quantize_mx(
-                out=g_codes[0, 1][:, slots].bitcast(E5M2X4),
-                scales=g_scales[0, 1][:, slots],
-                in_=gb[:].rearrange("p c t -> p (c t)"),
+        def gather(e, k, dst):
+            nc.vector.tensor_tensor(
+                out=dst[:, k % PACK, :],
+                in0=dy[k][:].indirect(offsets[:, e * C // 16:(e + 1) * C // 16]),
+                in1=gates[e][:],
+                op=MULT,
             )
-        finish_g(1, 0, staging(1), "late1")
-        slope_beside(1, 1, a1_t[1][:, 2:4, :], a1_t[1][:, 2:4, :])
-        weigh(1, 1, back, "rounded")
-        gb11 = keep.tile([P, C, PACK], BF16, name="dy0", align_bytes=64)[:]
-        collect(back, gb11)
 
-        dx = [sums.tile([P, C], F32, name=f"dx{e}") for e in range(E)]
-        held = {}
+        def round_g(weighed, staged):
+            nc.scalar.copy(out=interleaved(staged), in_=planes(weighed))
+
+        def rest_across(b, pairs, halves):
+            for pair, half in product(pairs, halves):
+                bank = turns.tile([P, 2, 2, P], F32, name="turned")
+                for a in range(2):
+                    for t in range(2):
+                        first = (2 * pair + a) * P
+                        nc.tensor.transpose(bank[:, a, t, :], a1_t[b][:, 2 * half + t, first:first + P], ident[:])
+                nc.scalar.activation(
+                    out=across[b][:, 2 * pair:2 * pair + 2, 2 * half:2 * half + 2, :],
+                    in_=bank[:],
+                    func=ACT.Sigmoid,
+                    scale=-1.0,
+                )
+
+        def rest(part):
+            nc.scalar.activation(out=part, in_=part, func=ACT.Sigmoid, scale=-1.0)
+
+        g_codes, d_codes, slopes, grads = {}, {}, {}, {}
+
+        def slope(b, slot):
+            slopes[b] = held([P, PACK, C], F32, slot)
+            for a in range(GROUPS):
+                cols = slice(a * P, (a + 1) * P)
+                nc.gpsimd.tensor_tensor(out=slopes[b][:, :, cols], in0=a1_t[b][:, :, cols], in1=a3_t[b][:, :, cols], op=MULT)
 
         def first_products(b):
             e, h = divmod(b, 2)
-            u = ring2.tile([P, PACK, C], F32, name="u")
-            for t in range(PACK):
-                if b == 1 and t < 2:
-                    dh = turns.tile([P, C], F32, name="across")
-                else:
-                    dh = banks.tile([P, C], F32, name="dh")
-                col = h * PASS + t * P
+            for a in range(GROUPS):
+                dh = ring.tile([P, PASS], F32, name="bank")
                 for s in range(2):
+                    codes, scales = g_codes[e, s]
                     nc.tensor.matmul_mx(
                         out=dh[:],
-                        lhsT=w2_put[2 * e + s][:, 2 * col:2 * (col + P)].bitcast(E2M1X4),
-                        lhsT_scale=w2s_put[2 * e + s][:, col:col + P],
-                        rhs=g_codes[e, s][:].bitcast(E5M2X4),
-                        rhs_scale=g_scales[e, s][:],
+                        lhsT=codes[:, a * P:(a + 1) * P].bitcast(E5M2X4),
+                        lhsT_scale=scales[:, a * P:(a + 1) * P],
+                        rhs=w2[e][:, s, 2 * h * PASS:2 * (h + 1) * PASS].bitcast(E2M1X4),
+                        rhs_scale=w2s[:, 2 * e + s, h * PASS:(h + 1) * PASS],
                         start=(s == 0),
                         stop=(s == 1),
                     )
                 nc.vector.scalar_tensor_tensor(
-                    out=u[:, t, :], in0=rest[b][t], scalar=1.0, in1=dh[:], op0=SUB, op1=MULT
+                    out=across[b][:, a],
+                    in0=across[b][:, a],
+                    scalar=1.0,
+                    in1=dh[:].rearrange("p (m t) -> p t m", t=PACK),
+                    op0=SUB,
+                    op1=MULT,
                 )
-            held[b] = u
 
-        def product(engine, b, first, last):
-            u, d1, d3 = held[b]
-            engine.tensor_tensor(
-                out=interleaved(d1[:, first:last, :]),
-                in0=planes(u[:, :, first:last]),
-                in1=planes(slopes[b][:, :, first:last]),
-                op=MULT,
-            )
+        def gradients(b, slot):
+            grads[b] = [held([P, C, PACK], BF16, "da1"), held([P, C, PACK], BF16, slot)]
+            for a in range(GROUPS):
+                cols = slice(a * P, (a + 1) * P)
+                u = ring.tile([P, PACK, P], F32, name="bank")
+                for t in range(PACK):
+                    nc.tensor.transpose(u[:, t, :], across[b][:, a, t, :], ident[:])
+                nc.vector.tensor_tensor(
+                    out=interleaved(grads[b][0][:, cols, :]), in0=planes(u[:]), in1=planes(slopes[b][:, :, cols]), op=MULT
+                )
+                nc.scalar.copy(out=grads[b][1][:, cols, :], in_=u[:].rearrange("p t c -> p c t"))
 
-        def gradients(b, share):
-            u = held[b]
-            d1 = ring2.tile([P, C, PACK], BF16, name="d1", align_bytes=64)
-            d3 = ring2.tile([P, C, PACK], BF16, name="d3", align_bytes=64)
-            held[b] = (u, d1[:], d3[:])
-            for first in range(0, share, 128):
-                product(nc.gpsimd, b, first, first + 128)
-            nc.scalar.copy(out=interleaved(d3[:]), in_=planes(u[:]))
+        def finish_gradients(b):
+            for w in (1, 0):
+                d_codes[b, w] = quantise(grads[b][w][:], f"dy{2 * b + w}", f"d_scales{2 * b + w}")
 
-        def second_products(b):
-            e, h = divmod(b, 2)
-            for w in range(2):
-                codes, scales = quantise(held[b][1 + w], f"d{w}_{b}")
+        def second_products(b, dx):
+            h = b % 2
+            for w in (1, 0):
+                codes, scales = d_codes[b, w]
                 nc.tensor.matmul_mx(
-                    out=dx[e][:],
+                    out=dx[:],
                     lhsT=w13[w][:, b, :].bitcast(E2M1X4),
                     lhsT_scale=w13s[:, w, b, :],
                     rhs=codes[:].bitcast(E5M2X4),
                     rhs_scale=scales[:],
-                    start=(h == 0 and w == 0),
-                    stop=(h == 1 and w == 1),
+                    start=(h == 0 and w == 1),
+                    stop=(h == 1 and w == 0),
                 )
 
-        def finish(e, dx_sb):
-            nc.scalar.activation(out=dx_sb[:, 0, :], in_=dx[e][:], func=ACT.Copy, scale=-1.0)
+        def land(dx, first, last, slot):
+            landing = held([P, last - first], F32, slot)
+            nc.scalar.activation(out=landing[:], in_=dx[:, first:last], func=ACT.Copy, scale=-1.0)
+            return landing
 
-        def scatter(e, dx_sb):
-            nc.vector.tensor_copy(result[:].indirect(offsets[:, e * C // 16:(e + 1) * C // 16]), dx_sb[:, 0, :])
+        def scatter(landing, first):
+            count = landing.shape[1]
+            nc.vector.tensor_copy(result[:].indirect(offsets[:, first // 16:(first + count) // 16]), landing[:])
 
-        first_products(0)
-        for b in range(4):
-            share = 256 if b < 3 else 0
-            gradients(b, share)
-            if b == 1:
-                finish_g(1, 1, gb11)
-            if b < 3:
-                first_products(b + 1)
-            product(nc.vector, b, share, C)
-            if b < 2:
-                sigmoid(b + 2)
-                slope(b + 2)
-            second_products(b)
-        landing = [ring2.tile([P, PACK, C], F32, name="u") for z in range(2)]
+        weighed = {(e, 0): held([P, PACK, C], F32, f"weighed{e}0")[:] for e in range(E)}
+        weighed[0, 1] = held([P, PACK, C], F32, "weighed01")[:]
+        for k in range(PACK):
+            for e in range(E):
+                gather(e, k, weighed[e, 0])
+        for half in range(2):
+            rest_across(0, [0, 1], [half])
+            rest(a1_t[0][:, 2 * half:2 * half + 2, :])
+        staged = {(e, 0): held([P, C, PACK], BF16, f"staged{e}0")[:] for e in range(E)}
         for e in range(E):
-            finish(e, landing[1 - e])
-            scatter(e, landing[1 - e])
+            round_g(weighed[e, 0], staged[e, 0])
+        for k in range(PACK, 2 * PACK):
+            gather(0, k, weighed[0, 1])
+        g_codes[0, 0] = quantise(staged[0, 0], "g00", "g_scales00")
+        last = held([P, PACK * C], F32, "gate0")
+        weighed[1, 1] = last[:].rearrange("p (t c) -> p t c", t=PACK)
+        staged[0, 1] = last[:, 2 * C:].bitcast(BF16).rearrange("p (c t) -> p c t", t=PACK)
+        rest_across(1, [0, 1], [0])
+        round_g(weighed[0, 1], staged[0, 1])
+        gather(1, PACK, weighed[1, 1])
+        gather(1, PACK + 1, weighed[1, 1])
+        g_codes[1, 0] = quantise(staged[1, 0], "g10", "g_scales10")
+        g_codes[0, 1] = quantise(staged[0, 1], "g01", "g_scales01")
+        gather(1, PACK + 2, weighed[1, 1])
+        gather(1, PACK + 3, weighed[1, 1])
+        rest_across(1, [0, 1], [1])
+        rest(a1_t[1][:])
+        staged[1, 1] = held([P, C, PACK], BF16, "staged11")[:]
+        round_g(weighed[1, 1], staged[1, 1])
+
+        slope(0, "gate1")
+        first_products(0)
+        first_products(1)
+        g_codes[1, 1] = quantise(staged[1, 1], "g11", "g_scales11")
+        rest_across(2, [0, 1], [0, 1])
+        slope(1, "staged11")
+        gradients(0, "weighed01")
+        first_products(2)
+        finish_gradients(0)
+        for pair in range(GROUPS // 2):
+            rest_across(3, [pair], [0, 1])
+        for pair in range(GROUPS // 2):
+            rest(a1_t[2][:, :, 2 * pair * P:2 * (pair + 1) * P])
+        slope(2, "weighed01")
+        gradients(1, "grads1")
+        rest(a1_t[3][:])
+        first_products(3)
+        finish_gradients(1)
+        dx = [turns.tile([P, C], F32, name="turned") for e in range(E)]
+        second_products(0, dx[0])
+        second_products(1, dx[0])
+        slope(3, "grads1")
+        early = land(dx[0], 0, C // 2, "staged00")
+        gradients(2, "weighed00")
+        scatter(early, 0)
+        finish_gradients(2)
+        second_products(2, dx[1])
+        gradients(3, "weighed10")
+        finish_gradients(3)
+        second_products(3, dx[1])
+        late = land(dx[0], C // 2, C, "grads1")
+        scatter(late, C // 2)
+        scatter(land(dx[1], 0, C, "staged10"), C)
         nc.sync.dma_start(out=out, in_=result[:])

@@ -86,29 +86,31 @@ def tile_moe_bdx_glu_sigmoid_kernel(
                 in_=src[h * PASS:(h + 1) * PASS, e * C:(e + 1) * C].rearrange("(p j) c -> p j c", j=PACK)[:, first:last, :],
             )
 
+        def load_a1_half(half):
+            load_saved(a1, a1_t, half // 2, 2 * (half % 2), 2 * (half % 2) + 2)
+
         nc.sync.dma_start(offsets[:], offs)
         load_gate(0)
         load_dy(0)
         load_gate(1)
-        load_dy(1)
-        load_saved(a1, a1_t, 0, 0, 2)
-        load_dy(2)
-        load_saved(a1, a1_t, 0, 2, 4)
-        for k in range(3, 8):
+        for k in range(1, PACK):
             load_dy(k)
-        load_saved(a1, a1_t, 1)
+            load_a1_half(k - 1)
+        for k in range(PACK, 2 * PACK):
+            load_dy(k)
+        load_a1_half(3)
+        load_saved(a1, a1_t, 2)
         load_scales(w2s, w2_scales)
         load_w2(0)
+        load_saved(a1, a1_t, 3)
         load_saved(a3, a3_t, 0)
         load_w2(1)
-        load_saved(a1, a1_t, 2)
         load_scales(w13s[:, 0], w1_scales)
         load_saved(a3, a3_t, 1)
-        load_saved(a1, a1_t, 3)
         load_scales(w13s[:, 1], w3_scales)
+        load_saved(a3, a3_t, 2)
         load_w13(0, w1_words)
         load_w13(1, w3_words)
-        load_saved(a3, a3_t, 2)
         load_saved(a3, a3_t, 3)
 
         def interleaved(dst):
@@ -151,6 +153,10 @@ def tile_moe_bdx_glu_sigmoid_kernel(
 
         def rest(part):
             nc.scalar.activation(out=part, in_=part, func=ACT.Sigmoid, scale=-1.0)
+
+        def rest_by_pairs(b):
+            for pair in range(GROUPS // 2):
+                rest(a1_t[b][:, :, 2 * pair * P:2 * (pair + 1) * P])
 
         g_codes, d_codes, slopes, grads = {}, {}, {}, {}
 
@@ -228,9 +234,9 @@ def tile_moe_bdx_glu_sigmoid_kernel(
         for k in range(PACK):
             for e in range(E):
                 gather(e, k, weighed[e, 0])
-        for half in range(2):
-            rest_across(0, [0, 1], [half])
-            rest(a1_t[0][:, 2 * half:2 * half + 2, :])
+        for b, half in ((0, 0), (0, 1), (1, 0)):
+            rest_across(b, [0, 1], [half])
+            rest(a1_t[b][:, 2 * half:2 * half + 2, :])
         staged = {(e, 0): held([P, C, PACK], BF16, f"staged{e}0")[:] for e in range(E)}
         for e in range(E):
             round_g(weighed[e, 0], staged[e, 0])
@@ -240,7 +246,7 @@ def tile_moe_bdx_glu_sigmoid_kernel(
         last = held([P, PACK * C], F32, "gate0")
         weighed[1, 1] = last[:].rearrange("p (t c) -> p t c", t=PACK)
         staged[0, 1] = last[:, 2 * C:].bitcast(BF16).rearrange("p (c t) -> p c t", t=PACK)
-        rest_across(1, [0, 1], [0])
+        rest_across(1, [0, 1], [1])
         round_g(weighed[0, 1], staged[0, 1])
         gather(1, PACK, weighed[1, 1])
         gather(1, PACK + 1, weighed[1, 1])
@@ -248,27 +254,24 @@ def tile_moe_bdx_glu_sigmoid_kernel(
         g_codes[0, 1] = quantise(staged[0, 1], "g01", "g_scales01")
         gather(1, PACK + 2, weighed[1, 1])
         gather(1, PACK + 3, weighed[1, 1])
-        rest_across(1, [0, 1], [1])
-        rest(a1_t[1][:])
+        rest(a1_t[1][:, 2:4, :])
+        rest_across(2, [0, 1], [0, 1])
+        rest_across(3, [0, 1], [0, 1])
         staged[1, 1] = held([P, C, PACK], BF16, "staged11")[:]
         round_g(weighed[1, 1], staged[1, 1])
+        rest_by_pairs(2)
 
         slope(0, "gate1")
         first_products(0)
         first_products(1)
         g_codes[1, 1] = quantise(staged[1, 1], "g11", "g_scales11")
-        rest_across(2, [0, 1], [0, 1])
         slope(1, "staged11")
         gradients(0, "weighed01")
+        rest_by_pairs(3)
         first_products(2)
         finish_gradients(0)
-        for pair in range(GROUPS // 2):
-            rest_across(3, [pair], [0, 1])
-        for pair in range(GROUPS // 2):
-            rest(a1_t[2][:, :, 2 * pair * P:2 * (pair + 1) * P])
         slope(2, "weighed01")
         gradients(1, "grads1")
-        rest(a1_t[3][:])
         first_products(3)
         finish_gradients(1)
         dx = [turns.tile([P, C], F32, name="turned") for e in range(E)]

@@ -21,6 +21,7 @@ PACK = 4
 PASS = P * PACK
 K, T, E, C, H, N = 128, 1024, 2, 512, 1024, 1024
 GROUPS = C // P
+EARLY = 128
 FLOPS = 2 * E * C * (N * H + 2 * H * K)
 
 
@@ -30,8 +31,7 @@ def tile_moe_bdx_glu_sigmoid_kernel(
     nc = tc.nc
     with ExitStack() as ctx:
         keep = ctx.enter_context(tc.tile_pool(name="keep", bufs=1))
-        ring = ctx.enter_context(tc.psum_pool(name="ring", bufs=6))
-        turns = ctx.enter_context(tc.psum_pool(name="turns", bufs=2))
+        ring = ctx.enter_context(tc.psum_pool(name="ring", bufs=8))
 
         def held(shape, dtype, slot):
             return keep.tile(shape, dtype, name=slot, align_bytes=64)
@@ -46,7 +46,7 @@ def tile_moe_bdx_glu_sigmoid_kernel(
         w13s = held([P, 2, 4, K], U8, "w13s")
         a1_t = [held([P, PACK, C], F32, f"a1_{b}") for b in range(4)]
         a3_t = [held([P, PACK, C], F32, f"a3_{b}") for b in range(4)]
-        across = [held([P, GROUPS, PACK, P], F32, f"across{b}") for b in range(4)]
+        across = [[held([P, 2, PACK, P], F32, f"across{b}{pair}") for pair in range(GROUPS // 2)] for b in range(4)]
         result = held([P, T], F32, "result")
 
         make_identity(nc, ident[:])
@@ -69,7 +69,7 @@ def tile_moe_bdx_glu_sigmoid_kernel(
         def load_scales(dst, scales):
             for q in range(4):
                 nc.sync.dma_start(
-                    out=dst[32 * q:32 * q + 4].rearrange("p b i -> p (b i)").bitcast(I32).rearrange("p (b i) -> p b i", b=4),
+                    out=dst[32 * q:32 * q + 4].rearrange("p b i -> p (b i)").bitcast(I32).rearrange("p (b i) -> p b i", b=dst.shape[1]),
                     in_=scales[:, :, 4 * q:4 * q + 4, :].bitcast(I32).rearrange("e s q i -> q (e s) i"),
                 )
 
@@ -100,18 +100,19 @@ def tile_moe_bdx_glu_sigmoid_kernel(
             load_dy(k)
         load_a1_half(3)
         load_saved(a1, a1_t, 2)
-        load_scales(w2s, w2_scales)
-        load_w2(0)
+        load_scales(w2s[:, 0:2], w2_scales[0:1])
         load_saved(a1, a1_t, 3)
+        load_w2(0)
         load_saved(a3, a3_t, 0)
-        load_w2(1)
-        load_scales(w13s[:, 0], w1_scales)
         load_saved(a3, a3_t, 1)
-        load_scales(w13s[:, 1], w3_scales)
+        load_scales(w2s[:, 2:4], w2_scales[1:2])
+        load_w2(1)
         load_saved(a3, a3_t, 2)
+        load_scales(w13s[:, 0], w1_scales)
+        load_saved(a3, a3_t, 3)
+        load_scales(w13s[:, 1], w3_scales)
         load_w13(0, w1_words)
         load_w13(1, w3_words)
-        load_saved(a3, a3_t, 3)
 
         def interleaved(dst):
             return dst.rearrange("p (c i) t -> p c t i", i=4)
@@ -139,13 +140,13 @@ def tile_moe_bdx_glu_sigmoid_kernel(
 
         def rest_across(b, pairs, halves):
             for pair, half in product(pairs, halves):
-                bank = turns.tile([P, 2, 2, P], F32, name="turned")
+                bank = ring.tile([P, 2, 2, P], F32, name="bank")
                 for a in range(2):
                     for t in range(2):
                         first = (2 * pair + a) * P
                         nc.tensor.transpose(bank[:, a, t, :], a1_t[b][:, 2 * half + t, first:first + P], ident[:])
                 nc.scalar.activation(
-                    out=across[b][:, 2 * pair:2 * pair + 2, 2 * half:2 * half + 2, :],
+                    out=across[b][pair][:, :, 2 * half:2 * half + 2, :],
                     in_=bank[:],
                     func=ACT.Sigmoid,
                     scale=-1.0,
@@ -154,22 +155,34 @@ def tile_moe_bdx_glu_sigmoid_kernel(
         def rest(part):
             nc.scalar.activation(out=part, in_=part, func=ACT.Sigmoid, scale=-1.0)
 
-        def rest_by_pairs(b):
-            for pair in range(GROUPS // 2):
-                rest(a1_t[b][:, :, 2 * pair * P:2 * (pair + 1) * P])
+        def rest_pair(b, pair, dst):
+            cols = slice(2 * pair * P, 2 * (pair + 1) * P)
+            nc.scalar.activation(out=dst, in_=a1_t[b][:, :, cols], func=ACT.Sigmoid, scale=-1.0)
+            rests[b, pair] = dst
 
-        g_codes, d_codes, slopes, grads = {}, {}, {}, {}
+        rests = {(b, pair): a1_t[b][:, :, 2 * pair * P:2 * (pair + 1) * P] for b in range(4) for pair in range(2)}
+        g_codes, slopes, firsts, backs, rooms, grads = {}, {}, {}, {}, {}, {}
 
-        def slope(b, slot):
-            slopes[b] = held([P, PACK, C], F32, slot)
-            for a in range(GROUPS):
-                cols = slice(a * P, (a + 1) * P)
-                nc.gpsimd.tensor_tensor(out=slopes[b][:, :, cols], in0=a1_t[b][:, :, cols], in1=a3_t[b][:, :, cols], op=MULT)
+        def make_slopes(cuts, slot):
+            room = held([P, cuts[-1] - cuts[0], PACK, P], F32, slot)
+            for piece in range(cuts[0], cuts[-1]):
+                slopes[piece] = room[:, piece - cuts[0]]
+            for first, last in zip(cuts, cuts[1:]):
+                b, a = divmod(first, GROUPS)
+                cols = slice(a * P, (a + last - first) * P)
+                near = slice(a % 2 * P, (a % 2 + last - first) * P)
+                nc.gpsimd.tensor_tensor(
+                    out=room[:, first - cuts[0]:last - cuts[0]],
+                    in0=rests[b, a // 2][:, :, near].rearrange("p t (a c) -> p a t c", c=P),
+                    in1=a3_t[b][:, :, cols].rearrange("p t (a c) -> p a t c", c=P),
+                    op=MULT,
+                )
 
         def first_products(b):
             e, h = divmod(b, 2)
             for a in range(GROUPS):
                 dh = ring.tile([P, PASS], F32, name="bank")
+                firsts[b, a] = across[b][a // 2][:, a % 2] if b < 2 else slopes[GROUPS * (b - 2) + a]
                 for s in range(2):
                     codes, scales = g_codes[e, s]
                     nc.tensor.matmul_mx(
@@ -182,42 +195,46 @@ def tile_moe_bdx_glu_sigmoid_kernel(
                         stop=(s == 1),
                     )
                 nc.vector.scalar_tensor_tensor(
-                    out=across[b][:, a],
-                    in0=across[b][:, a],
+                    out=firsts[b, a],
+                    in0=across[b][a // 2][:, a % 2],
                     scalar=1.0,
                     in1=dh[:].rearrange("p (m t) -> p t m", t=PACK),
                     op0=SUB,
                     op1=MULT,
                 )
 
-        def gradients(b, slot):
-            grads[b] = [held([P, C, PACK], BF16, "da1"), held([P, C, PACK], BF16, slot)]
+        def turn_back(b):
+            for a in range(GROUPS):
+                backs[b, a] = ring.tile([P, PACK, P], F32, name="bank")
+                for t in range(PACK):
+                    nc.tensor.transpose(backs[b, a][:, t, :], firsts[b, a][:, t, :], ident[:])
+
+        def gradients(b):
             for a in range(GROUPS):
                 cols = slice(a * P, (a + 1) * P)
-                u = ring.tile([P, PACK, P], F32, name="bank")
-                for t in range(PACK):
-                    nc.tensor.transpose(u[:, t, :], across[b][:, a, t, :], ident[:])
+                u = backs[b, a][:]
                 nc.vector.tensor_tensor(
-                    out=interleaved(grads[b][0][:, cols, :]), in0=planes(u[:]), in1=planes(slopes[b][:, :, cols]), op=MULT
+                    out=interleaved(grads[b, 0][:, cols, :]), in0=planes(u), in1=planes(slopes[GROUPS * b + a]), op=MULT
                 )
-                nc.scalar.copy(out=grads[b][1][:, cols, :], in_=u[:].rearrange("p t c -> p c t"))
+                nc.scalar.copy(out=grads[b, 1][:, cols, :], in_=u.rearrange("p t c -> p c t"))
 
-        def finish_gradients(b):
-            for w in (1, 0):
-                d_codes[b, w] = quantise(grads[b][w][:], f"dy{2 * b + w}", f"d_scales{2 * b + w}")
+        def room_for(parts, slot):
+            rooms[parts] = held([P, len(parts) * C, PACK], BF16, slot)[:]
+            for n, part in enumerate(parts):
+                grads[part] = rooms[parts][:, n * C:(n + 1) * C, :]
 
-        def second_products(b, dx):
-            h = b % 2
-            for w in (1, 0):
-                codes, scales = d_codes[b, w]
+        def second_products(parts, slot, start=False, stop=False):
+            codes, scales = quantise(rooms[parts], slot, f"d_scales{parts[0][0]}{parts[0][1]}")
+            for n, (b, w) in enumerate(parts):
+                cols = slice(n * C, (n + 1) * C)
                 nc.tensor.matmul_mx(
-                    out=dx[:],
+                    out=dx[b // 2][:],
                     lhsT=w13[w][:, b, :].bitcast(E2M1X4),
                     lhsT_scale=w13s[:, w, b, :],
-                    rhs=codes[:].bitcast(E5M2X4),
-                    rhs_scale=scales[:],
-                    start=(h == 0 and w == 1),
-                    stop=(h == 1 and w == 0),
+                    rhs=codes[:, cols].bitcast(E5M2X4),
+                    rhs_scale=scales[:, cols],
+                    start=(start and n == 0),
+                    stop=(stop and n == len(parts) - 1),
                 )
 
         def land(dx, first, last, slot):
@@ -254,39 +271,46 @@ def tile_moe_bdx_glu_sigmoid_kernel(
         g_codes[0, 1] = quantise(staged[0, 1], "g01", "g_scales01")
         gather(1, PACK + 2, weighed[1, 1])
         gather(1, PACK + 3, weighed[1, 1])
-        rest(a1_t[1][:, 2:4, :])
         rest_across(2, [0, 1], [0, 1])
         rest_across(3, [0, 1], [0, 1])
         staged[1, 1] = held([P, C, PACK], BF16, "staged11")[:]
         round_g(weighed[1, 1], staged[1, 1])
-        rest_by_pairs(2)
+        rest(a1_t[1][:, 2:4, :])
 
-        slope(0, "gate1")
+        make_slopes([0, 2, 4], "gate1")
         first_products(0)
         first_products(1)
         g_codes[1, 1] = quantise(staged[1, 1], "g11", "g_scales11")
-        slope(1, "staged11")
-        gradients(0, "weighed01")
-        rest_by_pairs(3)
+        room_for(((0, 0), (1, 0)), "weighed00")
+        room_for(((0, 1), (1, 1)), "weighed01")
+        turn_back(0)
+        gradients(0)
+        make_slopes([4, 6, 8], "staged11")
+        for pair in range(2):
+            rest_pair(2, pair, rests[2, pair])
+        make_slopes([8, 10, 12], "a3_0")
         first_products(2)
-        finish_gradients(0)
-        slope(2, "weighed01")
-        gradients(1, "grads1")
+        turn_back(1)
+        gradients(1)
+        for pair in range(2):
+            rest_pair(3, pair, held([P, PACK, 2 * P], F32, f"across2{pair}")[:])
         first_products(3)
-        finish_gradients(1)
-        dx = [turns.tile([P, C], F32, name="turned") for e in range(E)]
-        second_products(0, dx[0])
-        second_products(1, dx[0])
-        slope(3, "grads1")
-        early = land(dx[0], 0, C // 2, "staged00")
-        gradients(2, "weighed00")
-        scatter(early, 0)
-        finish_gradients(2)
-        second_products(2, dx[1])
-        gradients(3, "weighed10")
-        finish_gradients(3)
-        second_products(3, dx[1])
-        late = land(dx[0], C // 2, C, "grads1")
-        scatter(late, C // 2)
+        turn_back(2)
+        dx = [ring.tile([P, C], F32, name="bank")]
+        turn_back(3)
+        dx.append(ring.tile([P, C], F32, name="bank"))
+        second_products(((0, 0), (1, 0)), "across30", start=True)
+        second_products(((0, 1), (1, 1)), "across31", stop=True)
+        make_slopes([12, 14, 15, 16], "weighed01")
+        room_for(((2, 0), (2, 1)), "weighed10")
+        gradients(2)
+        scatter(land(dx[0], 0, EARLY, "staged00"), 0)
+        room_for(((3, 0),), "staged00")
+        room_for(((3, 1),), "dy3")
+        gradients(3)
+        second_products(((2, 0), (2, 1)), "weighed01", start=True)
+        second_products(((3, 1),), "dy0")
+        second_products(((3, 0),), "dy1", stop=True)
+        scatter(land(dx[0], EARLY, C, "dy3"), EARLY)
         scatter(land(dx[1], 0, C, "staged10"), C)
         nc.sync.dma_start(out=out, in_=result[:])

@@ -38,7 +38,8 @@ def tile_moe_bdx_glu_sigmoid_kernel(
 
         offsets = keep.tile([P, E * C // 16], U16, name="offsets")
         ident = held([P, P], F32, "ident")
-        gates = [held([P, C], F32, f"gate{e}") for e in range(E)]
+        second = held([P, 6 * C], F32, "weighed01")
+        gates = [second[:, 0:C], held([P, C], F32, "gate1")[:]]
         dy = [held([P, T], F32, f"dy{k}") for k in range(N // P)]
         w2 = [held([P, 2, 2 * H], U8, f"w2_{e}") for e in range(E)]
         w2s = held([P, 2 * E, H], U8, "w2s")
@@ -53,8 +54,8 @@ def tile_moe_bdx_glu_sigmoid_kernel(
         nc.vector.memset(w2s[:].rearrange("p b i -> p (b i)").bitcast(I32), 0)
         nc.vector.memset(w13s[:].rearrange("p w b k -> p (w b k)").bitcast(I32), 0)
 
-        def load_gate(e):
-            nc.sync.dma_start(out=gates[e][:], in_=gate[0:P, e * C:(e + 1) * C])
+        def load_gate(e, first, last):
+            nc.sync.dma_start(out=gates[e][:, first:last], in_=gate[0:P, e * C + first:e * C + last])
 
         def load_dy(k):
             s, j = divmod(k, PACK)
@@ -90,9 +91,10 @@ def tile_moe_bdx_glu_sigmoid_kernel(
             load_saved(a1, a1_t, half // 2, 2 * (half % 2), 2 * (half % 2) + 2)
 
         nc.sync.dma_start(offsets[:], offs)
-        load_gate(0)
+        load_gate(0, 0, C // 2)
         load_dy(0)
-        load_gate(1)
+        load_gate(0, C // 2, C)
+        load_gate(1, 0, C)
         for k in range(1, PACK):
             load_dy(k)
             load_a1_half(k - 1)
@@ -101,12 +103,12 @@ def tile_moe_bdx_glu_sigmoid_kernel(
         load_a1_half(3)
         load_saved(a1, a1_t, 2)
         load_scales(w2s[:, 0:2], w2_scales[0:1])
-        load_saved(a1, a1_t, 3)
         load_w2(0)
         load_saved(a3, a3_t, 0)
-        load_saved(a3, a3_t, 1)
         load_scales(w2s[:, 2:4], w2_scales[1:2])
         load_w2(1)
+        load_saved(a3, a3_t, 1)
+        load_saved(a1, a1_t, 3)
         load_saved(a3, a3_t, 2)
         load_scales(w13s[:, 0], w1_scales)
         load_saved(a3, a3_t, 3)
@@ -127,11 +129,11 @@ def tile_moe_bdx_glu_sigmoid_kernel(
             nc.vector.quantize_mx(out=codes[:].bitcast(E5M2X4), scales=scales[:], in_=src.rearrange("p c t -> p (c t)"))
             return codes, scales
 
-        def gather(e, k, dst):
+        def gather(e, k, dst, first=0, last=C):
             nc.vector.tensor_tensor(
-                out=dst[:, k % PACK, :],
-                in0=dy[k][:].indirect(offsets[:, e * C // 16:(e + 1) * C // 16]),
-                in1=gates[e][:],
+                out=dst[:, k % PACK, first:last],
+                in0=dy[k][:].indirect(offsets[:, (e * C + first) // 16:(e * C + last) // 16]),
+                in1=gates[e][:, first:last],
                 op=MULT,
             )
 
@@ -247,32 +249,34 @@ def tile_moe_bdx_glu_sigmoid_kernel(
             nc.vector.tensor_copy(result[:].indirect(offsets[:, first // 16:(first + count) // 16]), landing[:])
 
         weighed = {(e, 0): held([P, PACK, C], F32, f"weighed{e}0")[:] for e in range(E)}
-        weighed[0, 1] = held([P, PACK, C], F32, "weighed01")[:]
-        for k in range(PACK):
+        weighed[0, 1] = second[:, 2 * C:].rearrange("p (t c) -> p t c", t=PACK)
+        weighed[1, 1] = second[:, :PACK * C].rearrange("p (t c) -> p t c", t=PACK)
+        gather(0, 0, weighed[0, 0], 0, C // 2)
+        gather(0, 0, weighed[0, 0], C // 2, C)
+        gather(1, 0, weighed[1, 0])
+        for k in range(1, PACK):
             for e in range(E):
                 gather(e, k, weighed[e, 0])
         for b, half in ((0, 0), (0, 1), (1, 0)):
             rest_across(b, [0, 1], [half])
             rest(a1_t[b][:, 2 * half:2 * half + 2, :])
-        staged = {(e, 0): held([P, C, PACK], BF16, f"staged{e}0")[:] for e in range(E)}
+        staged = held([P, E * C, PACK], BF16, "staged0")
         for e in range(E):
-            round_g(weighed[e, 0], staged[e, 0])
+            round_g(weighed[e, 0], staged[:, e * C:(e + 1) * C, :])
         for k in range(PACK, 2 * PACK):
             gather(0, k, weighed[0, 1])
-        g_codes[0, 0] = quantise(staged[0, 0], "g00", "g_scales00")
-        last = held([P, PACK * C], F32, "gate0")
-        weighed[1, 1] = last[:].rearrange("p (t c) -> p t c", t=PACK)
-        staged[0, 1] = last[:, 2 * C:].bitcast(BF16).rearrange("p (c t) -> p c t", t=PACK)
-        rest_across(1, [0, 1], [1])
+        codes, scales = quantise(staged[:], "g0", "g_scales0")
+        for e in range(E):
+            g_codes[e, 0] = codes[:, e * C:(e + 1) * C], scales[:, e * C:(e + 1) * C]
+        staged = {(0, 1): held([P, C, PACK], BF16, "staged01")[:]}
         round_g(weighed[0, 1], staged[0, 1])
+        rest_across(1, [0, 1], [1])
         gather(1, PACK, weighed[1, 1])
         gather(1, PACK + 1, weighed[1, 1])
-        g_codes[1, 0] = quantise(staged[1, 0], "g10", "g_scales10")
         g_codes[0, 1] = quantise(staged[0, 1], "g01", "g_scales01")
         gather(1, PACK + 2, weighed[1, 1])
         gather(1, PACK + 3, weighed[1, 1])
         rest_across(2, [0, 1], [0, 1])
-        rest_across(3, [0, 1], [0, 1])
         staged[1, 1] = held([P, C, PACK], BF16, "staged11")[:]
         round_g(weighed[1, 1], staged[1, 1])
         rest(a1_t[1][:, 2:4, :])
@@ -290,6 +294,7 @@ def tile_moe_bdx_glu_sigmoid_kernel(
             rest_pair(2, pair, rests[2, pair])
         make_slopes([8, 10, 12], "a3_0")
         first_products(2)
+        rest_across(3, [0, 1], [0, 1])
         turn_back(1)
         gradients(1)
         for pair in range(2):
@@ -304,13 +309,13 @@ def tile_moe_bdx_glu_sigmoid_kernel(
         make_slopes([12, 14, 15, 16], "weighed01")
         room_for(((2, 0), (2, 1)), "weighed10")
         gradients(2)
-        scatter(land(dx[0], 0, EARLY, "staged00"), 0)
-        room_for(((3, 0),), "staged00")
+        scatter(land(dx[0], 0, EARLY, "staged01"), 0)
+        room_for(((3, 0),), "staged01")
         room_for(((3, 1),), "dy3")
         gradients(3)
         second_products(((2, 0), (2, 1)), "weighed01", start=True)
         second_products(((3, 1),), "dy0")
         second_products(((3, 0),), "dy1", stop=True)
         scatter(land(dx[0], EARLY, C, "dy3"), EARLY)
-        scatter(land(dx[1], 0, C, "staged10"), C)
+        scatter(land(dx[1], 0, C, "staged0"), C)
         nc.sync.dma_start(out=out, in_=result[:])

@@ -21,6 +21,7 @@ PACK = 4
 PASS = P * PACK
 K, T, E, C, H, N = 128, 1024, 2, 512, 1024, 1024
 GROUPS = C // P
+HALF = C // 2
 EARLY = 128
 FLOPS = 2 * E * C * (N * H + 2 * H * K)
 
@@ -47,6 +48,7 @@ def tile_moe_bdx_glu_sigmoid_kernel(
         w13s = held([P, 2, 4, K], U8, "w13s")
         a1_t = [held([P, PACK, C], F32, f"a1_{b}") for b in range(4)]
         a3_t = [held([P, PACK, C], F32, f"a3_{b}") for b in range(4)]
+        a3_p = {(b, pair): a3_t[b][:, :, pair * HALF:(pair + 1) * HALF] for b, pair in product(range(4), range(2))}
         across = [[held([P, 2, PACK, P], F32, f"across{b}{pair}") for pair in range(GROUPS // 2)] for b in range(4)]
         result = held([P, T], F32, "result")
 
@@ -163,28 +165,28 @@ def tile_moe_bdx_glu_sigmoid_kernel(
             rests[b, pair] = dst
 
         rests = {(b, pair): a1_t[b][:, :, 2 * pair * P:2 * (pair + 1) * P] for b in range(4) for pair in range(2)}
-        g_codes, slopes, firsts, backs, rooms, grads = {}, {}, {}, {}, {}, {}
+        g_codes, sums, slopes, firsts, backs, grads = {}, {}, {}, {}, {}, {}
 
-        def make_slopes(cuts, slot):
-            room = held([P, cuts[-1] - cuts[0], PACK, P], F32, slot)
-            for piece in range(cuts[0], cuts[-1]):
-                slopes[piece] = room[:, piece - cuts[0]]
-            for first, last in zip(cuts, cuts[1:]):
-                b, a = divmod(first, GROUPS)
-                cols = slice(a * P, (a + last - first) * P)
-                near = slice(a % 2 * P, (a % 2 + last - first) * P)
-                nc.gpsimd.tensor_tensor(
-                    out=room[:, first - cuts[0]:last - cuts[0]],
-                    in0=rests[b, a // 2][:, :, near].rearrange("p t (a c) -> p a t c", c=P),
-                    in1=a3_t[b][:, :, cols].rearrange("p t (a c) -> p a t c", c=P),
-                    op=MULT,
-                )
+        def pieces(room):
+            return room.rearrange("p (a t c) -> p a t c", t=PACK, c=P)
+
+        def make_slopes(b, first, last, dst):
+            near = slice(first % 2 * P, (first % 2 + last - first) * P)
+            for a in range(first, last):
+                slopes[b, a] = dst[:, a - first]
+            nc.gpsimd.tensor_tensor(
+                out=dst,
+                in0=rests[b, first // 2][:, :, near].rearrange("p t (a c) -> p a t c", c=P),
+                in1=a3_p[b, first // 2][:, :, near].rearrange("p t (a c) -> p a t c", c=P),
+                op=MULT,
+            )
 
         def first_products(b):
             e, h = divmod(b, 2)
             for a in range(GROUPS):
                 dh = ring.tile([P, PASS], F32, name="bank")
-                firsts[b, a] = across[b][a // 2][:, a % 2] if b < 2 else slopes[GROUPS * (b - 2) + a]
+                sums[b, a] = dh
+                firsts[b, a] = across[b][a // 2][:, a % 2] if b < 2 else slopes[b - 2, a]
                 for s in range(2):
                     codes, scales = g_codes[e, s]
                     nc.tensor.matmul_mx(
@@ -205,48 +207,46 @@ def tile_moe_bdx_glu_sigmoid_kernel(
                     op1=MULT,
                 )
 
-        def turn_back(b):
-            for a in range(GROUPS):
+        def turn_back(b, groups=range(GROUPS)):
+            for a in groups:
                 backs[b, a] = ring.tile([P, PACK, P], F32, name="bank")
                 for t in range(PACK):
                     nc.tensor.transpose(backs[b, a][:, t, :], firsts[b, a][:, t, :], ident[:])
 
+        def make_da1(b, a):
+            nc.vector.tensor_tensor(
+                out=interleaved(grads[b, a, 0]), in0=planes(backs[b, a][:]), in1=planes(slopes[b, a]), op=MULT
+            )
+
+        def make_da3(b, a):
+            nc.scalar.copy(out=grads[b, a, 1], in_=backs[b, a][:].rearrange("p t c -> p c t"))
+
         def gradients(b):
             for a in range(GROUPS):
-                cols = slice(a * P, (a + 1) * P)
-                u = backs[b, a][:]
-                nc.vector.tensor_tensor(
-                    out=interleaved(grads[b, 0][:, cols, :]), in0=planes(u), in1=planes(slopes[GROUPS * b + a]), op=MULT
-                )
-                nc.scalar.copy(out=grads[b, 1][:, cols, :], in_=u.rearrange("p t c -> p c t"))
+                make_da1(b, a)
+                make_da3(b, a)
 
-        def room_for(parts, slot):
-            rooms[parts] = held([P, len(parts) * C, PACK], BF16, slot)[:]
+        def lay(room, parts):
             for n, part in enumerate(parts):
-                grads[part] = rooms[parts][:, n * C:(n + 1) * C, :]
+                grads[part] = room[:, n * P:(n + 1) * P, :]
 
-        def second_products(parts, slot, start=False, stop=False):
-            codes, scales = quantise(rooms[parts], slot, f"d_scales{parts[0][0]}{parts[0][1]}")
-            for n, (b, w) in enumerate(parts):
-                cols = slice(n * C, (n + 1) * C)
-                nc.tensor.matmul_mx(
-                    out=dx[b // 2][:],
-                    lhsT=w13[w][:, b, :].bitcast(E2M1X4),
-                    lhsT_scale=w13s[:, w, b, :],
-                    rhs=codes[:, cols].bitcast(E5M2X4),
-                    rhs_scale=scales[:, cols],
-                    start=(start and n == 0),
-                    stop=(stop and n == len(parts) - 1),
-                )
+        def second_pass(dx, b, w, codes, scales, start, stop):
+            nc.tensor.matmul_mx(
+                out=dx[:],
+                lhsT=w13[w][:, b, :].bitcast(E2M1X4),
+                lhsT_scale=w13s[:, w, b, :],
+                rhs=codes.bitcast(E5M2X4),
+                rhs_scale=scales,
+                start=start,
+                stop=stop,
+            )
 
-        def land(dx, first, last, slot):
-            landing = held([P, last - first], F32, slot)
-            nc.scalar.activation(out=landing[:], in_=dx[:, first:last], func=ACT.Copy, scale=-1.0)
-            return landing
+        def land(dx, first, landing):
+            nc.scalar.activation(out=landing, in_=dx[:, first:first + landing.shape[1]], func=ACT.Copy, scale=-1.0)
 
         def scatter(landing, first):
             count = landing.shape[1]
-            nc.vector.tensor_copy(result[:].indirect(offsets[:, first // 16:(first + count) // 16]), landing[:])
+            nc.vector.tensor_copy(result[:].indirect(offsets[:, first // 16:(first + count) // 16]), landing)
 
         weighed = {(e, 0): held([P, PACK, C], F32, f"weighed{e}0")[:] for e in range(E)}
         weighed[0, 1] = second[:, 2 * C:].rearrange("p (t c) -> p t c", t=PACK)
@@ -281,41 +281,99 @@ def tile_moe_bdx_glu_sigmoid_kernel(
         round_g(weighed[1, 1], staged[1, 1])
         rest(a1_t[1][:, 2:4, :])
 
-        make_slopes([0, 2, 4], "gate1")
+        room = pieces(held([P, 4 * C], F32, "gate1")[:])
+        make_slopes(0, 0, 2, room[:, 0:2])
+        make_slopes(0, 2, 4, room[:, 2:4])
         first_products(0)
         first_products(1)
         g_codes[1, 1] = quantise(staged[1, 1], "g11", "g_scales11")
-        room_for(((0, 0), (1, 0)), "weighed00")
-        room_for(((0, 1), (1, 1)), "weighed01")
+        whole = [held([P, 2 * C, PACK], BF16, slot)[:] for slot in ("weighed00", "weighed01")]
+        for w in range(2):
+            lay(whole[w], [(b, a, w) for b, a in product(range(2), range(GROUPS))])
         turn_back(0)
         gradients(0)
-        make_slopes([4, 6, 8], "staged11")
+        room = pieces(held([P, 4 * C], F32, "staged11")[:])
+        make_slopes(1, 0, 2, room[:, 0:2])
+        make_slopes(1, 2, 4, room[:, 2:4])
         for pair in range(2):
             rest_pair(2, pair, rests[2, pair])
-        make_slopes([8, 10, 12], "a3_0")
+        room = pieces(held([P, 3 * C], F32, "a3_0")[:])
+        make_slopes(2, 0, 2, room[:, 0:2])
+        make_slopes(2, 2, 3, room[:, 2:3])
         first_products(2)
         rest_across(3, [0, 1], [0, 1])
         turn_back(1)
         gradients(1)
         for pair in range(2):
-            rest_pair(3, pair, held([P, PACK, 2 * P], F32, f"across2{pair}")[:])
+            rest_pair(3, pair, held([P, PACK, HALF], F32, f"across2{pair}")[:])
         first_products(3)
-        turn_back(2)
-        dx = [ring.tile([P, C], F32, name="bank")]
-        turn_back(3)
-        dx.append(ring.tile([P, C], F32, name="bank"))
-        second_products(((0, 0), (1, 0)), "across30", start=True)
-        second_products(((0, 1), (1, 1)), "across31", stop=True)
-        make_slopes([12, 14, 15, 16], "weighed01")
-        room_for(((2, 0), (2, 1)), "weighed10")
-        gradients(2)
-        scatter(land(dx[0], 0, EARLY, "staged01"), 0)
-        room_for(((3, 0),), "staged01")
-        room_for(((3, 1),), "dy3")
-        gradients(3)
-        second_products(((2, 0), (2, 1)), "weighed01", start=True)
-        second_products(((3, 1),), "dy0")
-        second_products(((3, 0),), "dy1", stop=True)
-        scatter(land(dx[0], EARLY, C, "dy3"), EARLY)
-        scatter(land(dx[1], 0, C, "staged0"), C)
+        turn_back(2, (0, 1, 2))
+        dx = [sums[3, GROUPS - 1]]
+        for w in range(2):
+            codes, scales = quantise(whole[w], f"across3{w}", f"d_scales{w}")
+            for b in range(2):
+                cols = slice(b * C, (b + 1) * C)
+                second_pass(dx[0], b, w, codes[:, cols], scales[:, cols], w == 0 and b == 0, w == 1 and b == 1)
+
+        turn_back(3, (0, 1, 2, 3))
+        turn_back(2, (3,))
+        dx += [ring.tile([P, C], F32, name="bank") for half in range(2)]
+        room = pieces(held([P, 5 * C], F32, "weighed01")[:])
+        make_slopes(3, 0, 2, room[:, 0:2])
+        make_slopes(3, 2, 4, room[:, 2:4])
+        make_slopes(2, 3, 4, room[:, 4:5])
+
+        def room_for(parts, slot):
+            room = held([P, len(parts) * HALF, PACK], BF16, slot)[:]
+            lay(room, [(b, 2 * half + i, w) for b, half, w in parts for i in range(2)])
+            return room
+
+        groups = [[(2, 0, 1), (3, 0, 1), (2, 0, 0), (2, 1, 1)], [(3, 0, 0), (3, 1, 1)], [(3, 1, 0)], [(2, 1, 0)]]
+        rooms = {n: room_for(groups[n], slot) for n, slot in ((0, "weighed10"), (3, "dy3"))}
+        early = held([P, EARLY], F32, "staged01")[:]
+        later = held([P, C - EARLY], F32, "dy0")[:]
+        land(dx[0], 0, early)
+        for a in range(3):
+            make_da1(2, a)
+            make_da3(2, a)
+        scatter(early, 0)
+        rooms[1] = room_for(groups[1], "staged01")
+        land(dx[0], EARLY, later)
+        for b, a in ((3, 0), (3, 1), (2, 3), (3, 2), (3, 3)):
+            make_da3(b, a)
+        for a in range(2):
+            make_da1(3, a)
+        scatter(later, EARLY)
+
+        codes = held([P, 4 * C], U32, "a3_2")
+        scales = held([P, 4 * C], U8, "a3_3")
+        parts = [part for group in groups for part in group]
+
+        def quantise_group(n):
+            first = parts.index(groups[n][0]) * HALF
+            cols = slice(first, first + len(groups[n]) * HALF)
+            nc.vector.quantize_mx(
+                out=codes[:, cols].bitcast(E5M2X4), scales=scales[:, cols], in_=rooms[n].rearrange("p c t -> p (c t)")
+            )
+
+        def padded_pass(b, half, w):
+            place = parts.index((b, half, w))
+            cols = slice((place - half) * HALF, (place - half) * HALF + C)
+            mine = [part for part in parts if part[1] == half]
+            second_pass(dx[1 + half], b, w, codes[:, cols], scales[:, cols], (b, half, w) == mine[0], (b, half, w) == mine[-1])
+
+        for n in range(2):
+            quantise_group(n)
+        for part in sorted(groups[0] + groups[1], key=lambda part: part[1]):
+            padded_pass(*part)
+        rooms[2] = room_for(groups[2], "weighed10")
+        for b, a in ((3, 2), (3, 3), (2, 3)):
+            make_da1(b, a)
+        for n in (2, 3):
+            quantise_group(n)
+            padded_pass(*groups[n][0])
+        for half, slot in enumerate(("dy1", "staged0")):
+            landing = held([P, HALF], F32, slot)[:]
+            land(dx[1 + half], half * HALF, landing)
+            scatter(landing, C + half * HALF)
         nc.sync.dma_start(out=out, in_=result[:])

@@ -309,11 +309,17 @@ def tile_moe_bdx_glu_sigmoid_kernel(
         first_products(3)
         turn_back(2, (0, 1, 2))
         dx = [sums[3, GROUPS - 1]]
-        for w in range(2):
-            codes, scales = quantise(whole[w], f"across3{w}", f"d_scales{w}")
-            for b in range(2):
-                cols = slice(b * C, (b + 1) * C)
-                second_pass(dx[0], b, w, codes[:, cols], scales[:, cols], w == 0 and b == 0, w == 1 and b == 1)
+        codes, scales = quantise(whole[0], "across30", "d_scales0")
+        for b in range(2):
+            second_pass(dx[0], b, 0, codes[:, b * C:(b + 1) * C], scales[:, b * C:(b + 1) * C], b == 0, False)
+        codes = held([P, 2 * C], U32, "across31")
+        scales = held([P, 2 * C], U8, "d_scales1")
+        for b in range(2):
+            cols = slice(b * C, (b + 1) * C)
+            nc.vector.quantize_mx(
+                out=codes[:, cols].bitcast(E5M2X4), scales=scales[:, cols], in_=whole[1][:, cols, :].rearrange("p c t -> p (c t)")
+            )
+            second_pass(dx[0], b, 1, codes[:, cols], scales[:, cols], False, b == 1)
 
         turn_back(3, (0, 1, 2, 3))
         turn_back(2, (3,))
@@ -328,22 +334,22 @@ def tile_moe_bdx_glu_sigmoid_kernel(
             lay(room, [(b, 2 * half + i, w) for b, half, w in parts for i in range(2)])
             return room
 
-        groups = [[(2, 0, 1), (3, 0, 1), (2, 0, 0), (2, 1, 1)], [(3, 0, 0), (3, 1, 1)], [(3, 1, 0)], [(2, 1, 0)]]
-        rooms = {n: room_for(groups[n], slot) for n, slot in ((0, "weighed10"), (3, "dy3"))}
+        groups = [[(2, 0, 0), (3, 0, 0)], [(2, 0, 1), (3, 0, 1)], [(2, 1, 1), (3, 1, 1)], [(3, 1, 0)], [(2, 1, 0)]]
+        rooms = {n: room_for(groups[n], slot) for n, slot in ((0, "weighed10"), (4, "dy3"))}
         early = held([P, EARLY], F32, "staged01")[:]
         later = held([P, C - EARLY], F32, "dy0")[:]
         land(dx[0], 0, early)
+        land(dx[0], EARLY, later)
         for a in range(3):
             make_da1(2, a)
-            make_da3(2, a)
         scatter(early, 0)
-        rooms[1] = room_for(groups[1], "staged01")
-        land(dx[0], EARLY, later)
-        for b, a in ((3, 0), (3, 1), (2, 3), (3, 2), (3, 3)):
+        both = room_for(groups[1] + groups[2], "staged01")
+        rooms[1], rooms[2] = both[:, :C, :], both[:, C:, :]
+        for b, a in ((3, 0), (3, 1), (2, 0), (2, 1), (2, 2), (3, 2), (3, 3), (2, 3)):
             make_da3(b, a)
+        scatter(later, EARLY)
         for a in range(2):
             make_da1(3, a)
-        scatter(later, EARLY)
 
         codes = held([P, 4 * C], U32, "a3_2")
         scales = held([P, 4 * C], U8, "a3_3")
@@ -356,22 +362,21 @@ def tile_moe_bdx_glu_sigmoid_kernel(
                 out=codes[:, cols].bitcast(E5M2X4), scales=scales[:, cols], in_=rooms[n].rearrange("p c t -> p (c t)")
             )
 
-        def padded_pass(b, half, w):
-            place = parts.index((b, half, w))
+        def padded_pass(place):
+            b, half, w = parts[place]
             cols = slice((place - half) * HALF, (place - half) * HALF + C)
-            mine = [part for part in parts if part[1] == half]
-            second_pass(dx[1 + half], b, w, codes[:, cols], scales[:, cols], (b, half, w) == mine[0], (b, half, w) == mine[-1])
+            second_pass(dx[1 + half], b, w, codes[:, cols], scales[:, cols], place % 4 == 0, place % 4 == 3)
 
-        for n in range(2):
+        for n, places in enumerate(((0,), (1, 2), (3, 4, 5))):
             quantise_group(n)
-        for part in sorted(groups[0] + groups[1], key=lambda part: part[1]):
-            padded_pass(*part)
-        rooms[2] = room_for(groups[2], "weighed10")
+            for place in places:
+                padded_pass(place)
+        rooms[3] = room_for(groups[3], "weighed10")
         for b, a in ((3, 2), (3, 3), (2, 3)):
             make_da1(b, a)
-        for n in (2, 3):
+        for n in (3, 4):
             quantise_group(n)
-            padded_pass(*groups[n][0])
+            padded_pass(3 + n)
         for half, slot in enumerate(("dy1", "staged0")):
             landing = held([P, HALF], F32, slot)[:]
             land(dx[1 + half], half * HALF, landing)

@@ -48,7 +48,6 @@ def tile_moe_bdx_glu_sigmoid_kernel(
         w13s = held([P, 2, 4, K], U8, "w13s")
         a1_t = [held([P, PACK, C], F32, f"a1_{b}") for b in range(4)]
         a3_t = [held([P, PACK, C], F32, f"a3_{b}") for b in range(4)]
-        a3_p = {(b, pair): a3_t[b][:, :, pair * HALF:(pair + 1) * HALF] for b, pair in product(range(4), range(2))}
         across = [[held([P, 2, PACK, P], F32, f"across{b}{pair}") for pair in range(GROUPS // 2)] for b in range(4)]
         result = held([P, T], F32, "result")
 
@@ -167,19 +166,12 @@ def tile_moe_bdx_glu_sigmoid_kernel(
         rests = {(b, pair): a1_t[b][:, :, 2 * pair * P:2 * (pair + 1) * P] for b in range(4) for pair in range(2)}
         g_codes, sums, slopes, firsts, backs, grads = {}, {}, {}, {}, {}, {}
 
-        def pieces(room):
-            return room.rearrange("p (a t c) -> p a t c", t=PACK, c=P)
-
         def make_slopes(b, first, last, dst):
-            near = slice(first % 2 * P, (first % 2 + last - first) * P)
+            cols = slice(first * P, last * P)
+            rested = a1_t[b][:, :, cols] if b < 3 else rests[b, first // 2]
             for a in range(first, last):
-                slopes[b, a] = dst[:, a - first]
-            nc.gpsimd.tensor_tensor(
-                out=dst,
-                in0=rests[b, first // 2][:, :, near].rearrange("p t (a c) -> p a t c", c=P),
-                in1=a3_p[b, first // 2][:, :, near].rearrange("p t (a c) -> p a t c", c=P),
-                op=MULT,
-            )
+                slopes[b, a] = dst[:, :, (a - first) * P:(a - first + 1) * P]
+            nc.gpsimd.tensor_tensor(out=dst, in0=rested, in1=a3_t[b][:, :, cols], op=MULT)
 
         def first_products(b):
             e, h = divmod(b, 2)
@@ -281,9 +273,7 @@ def tile_moe_bdx_glu_sigmoid_kernel(
         round_g(weighed[1, 1], staged[1, 1])
         rest(a1_t[1][:, 2:4, :])
 
-        room = pieces(held([P, 4 * C], F32, "gate1")[:])
-        make_slopes(0, 0, 2, room[:, 0:2])
-        make_slopes(0, 2, 4, room[:, 2:4])
+        make_slopes(0, 0, 4, held([P, PACK, C], F32, "gate1")[:])
         first_products(0)
         first_products(1)
         g_codes[1, 1] = quantise(staged[1, 1], "g11", "g_scales11")
@@ -292,14 +282,12 @@ def tile_moe_bdx_glu_sigmoid_kernel(
             lay(whole[w], [(b, a, w) for b, a in product(range(2), range(GROUPS))])
         turn_back(0)
         gradients(0)
-        room = pieces(held([P, 4 * C], F32, "staged11")[:])
-        make_slopes(1, 0, 2, room[:, 0:2])
-        make_slopes(1, 2, 4, room[:, 2:4])
+        room = held([P, 2, PACK, HALF], F32, "staged11")
+        make_slopes(1, 0, 2, room[:, 0])
+        make_slopes(1, 2, 4, room[:, 1])
         for pair in range(2):
             rest_pair(2, pair, rests[2, pair])
-        room = pieces(held([P, 3 * C], F32, "a3_0")[:])
-        make_slopes(2, 0, 2, room[:, 0:2])
-        make_slopes(2, 2, 3, room[:, 2:3])
+        make_slopes(2, 0, 3, held([P, PACK, 3 * P], F32, "a3_0")[:])
         first_products(2)
         rest_across(3, [0, 1], [0, 1])
         turn_back(1)
@@ -324,10 +312,10 @@ def tile_moe_bdx_glu_sigmoid_kernel(
         turn_back(3, (0, 1, 2, 3))
         turn_back(2, (3,))
         dx += [ring.tile([P, C], F32, name="bank") for half in range(2)]
-        room = pieces(held([P, 5 * C], F32, "weighed01")[:])
-        make_slopes(3, 0, 2, room[:, 0:2])
-        make_slopes(3, 2, 4, room[:, 2:4])
-        make_slopes(2, 3, 4, room[:, 4:5])
+        room = held([P, 2, PACK, HALF], F32, "weighed01")
+        make_slopes(3, 0, 2, room[:, 0])
+        make_slopes(3, 2, 4, room[:, 1])
+        make_slopes(2, 3, 4, held([P, PACK, P], F32, "across20")[:])
 
         def room_for(parts, slot):
             room = held([P, len(parts) * HALF, PACK], BF16, slot)[:]

@@ -69,7 +69,7 @@ def tile_moe_bdx_glu_sigmoid_kernel(
             )
 
         def load_scales(dst, scales):
-            for q in range(4):
+            for q in (0, 2, 1, 3):
                 nc.sync.dma_start(
                     out=dst[32 * q:32 * q + 4].rearrange("p b i -> p (b i)").bitcast(I32).rearrange("p (b i) -> p b i", b=dst.shape[1]),
                     in_=scales[:, :, 4 * q:4 * q + 4, :].bitcast(I32).rearrange("e s q i -> q (e s) i"),
@@ -109,7 +109,8 @@ def tile_moe_bdx_glu_sigmoid_kernel(
         load_scales(w2s[:, 2:4], w2_scales[1:2])
         load_w2(1)
         load_saved(a3, a3_t, 1)
-        load_saved(a1, a1_t, 3)
+        load_saved(a1, a1_t, 3, 0, 2)
+        load_saved(a1, a1_t, 3, 2, 4)
         load_saved(a3, a3_t, 2)
         load_scales(w13s[:, 0], w1_scales)
         load_saved(a3, a3_t, 3)
@@ -142,7 +143,7 @@ def tile_moe_bdx_glu_sigmoid_kernel(
             nc.scalar.copy(out=interleaved(staged), in_=planes(weighed))
 
         def rest_across(b, pairs, halves):
-            for pair, half in product(pairs, halves):
+            for half, pair in product(halves, pairs):
                 bank = ring.tile([P, 2, 2, P], F32, name="bank")
                 for a in range(2):
                     for t in range(2):
@@ -322,8 +323,8 @@ def tile_moe_bdx_glu_sigmoid_kernel(
             lay(room, [(b, 2 * half + i, w) for b, half, w in parts for i in range(2)])
             return room
 
-        groups = [[(2, 0, 0), (3, 0, 0)], [(2, 0, 1), (3, 0, 1)], [(2, 1, 1), (3, 1, 1)], [(3, 1, 0)], [(2, 1, 0)]]
-        rooms = {n: room_for(groups[n], slot) for n, slot in ((0, "weighed10"), (4, "dy3"))}
+        groups = [[(2, 0, 1), (3, 0, 1)], [(2, 0, 0), (3, 0, 0)], [(2, 1, 1), (3, 1, 1)], [(3, 1, 0)], [(2, 1, 0)]]
+        rooms = {n: room_for(groups[n], slot) for n, slot in ((1, "weighed10"), (4, "dy3"))}
         early = held([P, EARLY], F32, "staged01")[:]
         later = held([P, C - EARLY], F32, "dy0")[:]
         land(dx[0], 0, early)
@@ -331,8 +332,8 @@ def tile_moe_bdx_glu_sigmoid_kernel(
         for a in range(3):
             make_da1(2, a)
         scatter(early, 0)
-        both = room_for(groups[1] + groups[2], "staged01")
-        rooms[1], rooms[2] = both[:, :C, :], both[:, C:, :]
+        both = room_for(groups[0] + groups[2], "staged01")
+        rooms[0], rooms[2] = both[:, :C, :], both[:, C:, :]
         for b, a in ((3, 0), (3, 1), (2, 0), (2, 1), (2, 2), (3, 2), (3, 3), (2, 3)):
             make_da3(b, a)
         scatter(later, EARLY)

@@ -75,8 +75,8 @@ def tile_moe_bdx_glu_sigmoid_kernel(
                     in_=scales[:, :, 4 * q:4 * q + 4, :].bitcast(I32).rearrange("e s q i -> q (e s) i"),
                 )
 
-        def load_w2(e):
-            load_words(w2[e], w2_words[e].bitcast(I32).rearrange("s p i -> p s i"), 2)
+        def load_w2(e, s):
+            nc.sync.dma_start(out=w2[e][:, s, :].bitcast(I32), in_=w2_words[e, s].bitcast(I32))
 
         def load_w13(w, words):
             load_words(w13[w], words.bitcast(I32).rearrange("e s p i -> p (e s) i"), 4)
@@ -102,12 +102,15 @@ def tile_moe_bdx_glu_sigmoid_kernel(
         for k in range(PACK, 2 * PACK):
             load_dy(k)
         load_a1_half(3)
-        load_saved(a1, a1_t, 2)
+        load_saved(a1, a1_t, 2, 0, 2)
+        load_saved(a1, a1_t, 2, 2, 4)
         load_scales(w2s[:, 0:2], w2_scales[0:1])
-        load_w2(0)
+        for s in range(2):
+            load_w2(0, s)
         load_saved(a3, a3_t, 0)
         load_scales(w2s[:, 2:4], w2_scales[1:2])
-        load_w2(1)
+        for s in range(2):
+            load_w2(1, s)
         load_saved(a3, a3_t, 1)
         load_saved(a1, a1_t, 3, 0, 2)
         load_saved(a1, a1_t, 3, 2, 4)

@@ -22,7 +22,7 @@ PASS = P * PACK
 K, T, E, C, H, N = 128, 1024, 2, 512, 1024, 1024
 GROUPS = C // P
 HALF = C // 2
-EARLY = 128
+BLOCKS = 4
 FLOPS = 2 * E * C * (N * H + 2 * H * K)
 
 
@@ -32,41 +32,32 @@ def tile_moe_bdx_glu_sigmoid_kernel(
     nc = tc.nc
     with ExitStack() as ctx:
         keep = ctx.enter_context(tc.tile_pool(name="keep", bufs=1))
-        ring = ctx.enter_context(tc.psum_pool(name="ring", bufs=8))
+        psum = ctx.enter_context(tc.psum_pool(name="psum", bufs=7))
+        pinned = ctx.enter_context(tc.psum_pool(name="pinned", bufs=1))
 
         def held(shape, dtype, slot):
             return keep.tile(shape, dtype, name=slot, align_bytes=64)
 
         offsets = keep.tile([P, E * C // 16], U16, name="offsets")
         ident = held([P, P], F32, "ident")
-        second = held([P, 6 * C], F32, "weighed01")
-        gates = [second[:, 0:C], held([P, C], F32, "gate1")[:]]
+        gate0 = held([P, C], F32, "gate0")
+        gate_col = held([P, GROUPS], F32, "gate_col")
         dy = [held([P, T], F32, f"dy{k}") for k in range(N // P)]
         w2 = [held([P, 2, 2 * H], U8, f"w2_{e}") for e in range(E)]
         w2s = held([P, 2 * E, H], U8, "w2s")
         w13 = [held([P, 4, 2 * K], U8, f"w13_{w}") for w in range(2)]
         w13s = held([P, 2, 4, K], U8, "w13s")
-        a1_t = [held([P, PACK, C], F32, f"a1_{b}") for b in range(4)]
-        a3_t = [held([P, PACK, C], F32, f"a3_{b}") for b in range(4)]
-        across = [[held([P, 2, PACK, P], F32, f"across{b}{pair}") for pair in range(GROUPS // 2)] for b in range(4)]
+        a1_t = [held([P, PACK, C], F32, f"a1_{b}") for b in range(BLOCKS)]
+        a3_t = [held([P, PACK, C], F32, f"a3_{b}") for b in range(BLOCKS)]
         result = held([P, T], F32, "result")
 
         make_identity(nc, ident[:])
         nc.vector.memset(w2s[:].rearrange("p b i -> p (b i)").bitcast(I32), 0)
         nc.vector.memset(w13s[:].rearrange("p w b k -> p (w b k)").bitcast(I32), 0)
 
-        def load_gate(e, first, last):
-            nc.sync.dma_start(out=gates[e][:, first:last], in_=gate[0:P, e * C + first:e * C + last])
-
         def load_dy(k):
             s, j = divmod(k, PACK)
             nc.sync.dma_start(out=dy[k][:], in_=dyT[s * PASS:(s + 1) * PASS].rearrange("(p j) w -> p j w", j=PACK)[:, j, :])
-
-        def load_words(dst, words, n):
-            nc.sync.dma_start(
-                out=dst[:].rearrange("p b i -> p (b i)").bitcast(I32).rearrange("p (b i) -> p b i", b=n),
-                in_=words,
-            )
 
         def load_scales(dst, scales):
             for q in (0, 2, 1, 3):
@@ -75,51 +66,50 @@ def tile_moe_bdx_glu_sigmoid_kernel(
                     in_=scales[:, :, 4 * q:4 * q + 4, :].bitcast(I32).rearrange("e s q i -> q (e s) i"),
                 )
 
-        def load_w2(e, s):
-            nc.sync.dma_start(out=w2[e][:, s, :].bitcast(I32), in_=w2_words[e, s].bitcast(I32))
+        def load_w2(e):
+            load_scales(w2s[:, 2 * e:2 * e + 2], w2_scales[e:e + 1])
+            for s in range(2):
+                nc.sync.dma_start(out=w2[e][:, s, :].bitcast(I32), in_=w2_words[e, s].bitcast(I32))
 
         def load_w13(w, words):
-            load_words(w13[w], words.bitcast(I32).rearrange("e s p i -> p (e s) i"), 4)
-
-        def load_saved(src, dst, b, first=0, last=PACK):
-            e, h = divmod(b, 2)
             nc.sync.dma_start(
-                out=dst[b][:, first:last, :],
-                in_=src[h * PASS:(h + 1) * PASS, e * C:(e + 1) * C].rearrange("(p j) c -> p j c", j=PACK)[:, first:last, :],
+                out=w13[w][:].rearrange("p b i -> p (b i)").bitcast(I32).rearrange("p (b i) -> p b i", b=4),
+                in_=words.bitcast(I32).rearrange("e s p i -> p (e s) i"),
             )
 
-        def load_a1_half(half):
-            load_saved(a1, a1_t, half // 2, 2 * (half % 2), 2 * (half % 2) + 2)
+        def load_saved(src, dst, b):
+            e, h = divmod(b, 2)
+            nc.sync.dma_start(
+                out=dst[b][:],
+                in_=src[h * PASS:(h + 1) * PASS, e * C:(e + 1) * C].rearrange("(p j) c -> p j c", j=PACK),
+            )
 
+        early = held([P, PACK, P], F32, "early")
         nc.sync.dma_start(offsets[:], offs)
-        load_gate(0, 0, C // 2)
+        nc.sync.dma_start(out=early[:], in_=a1[0:PASS, 0:P].rearrange("(p j) c -> p j c", j=PACK))
+        nc.sync.dma_start(out=gate0[:, :HALF], in_=gate[0:P, 0:HALF])
         load_dy(0)
-        load_gate(0, C // 2, C)
-        load_gate(1, 0, C)
-        for k in range(1, PACK):
+        nc.sync.dma_start(out=gate0[:, HALF:], in_=gate[0:P, HALF:C])
+        for k in range(1, 2 * PACK - 2):
             load_dy(k)
-            load_a1_half(k - 1)
-        for k in range(PACK, 2 * PACK):
+        with nc.allow_non_contiguous_dma(reason="one gate a partition"):
+            nc.sync.dma_start(out=gate_col[:], in_=gate[0, C:].rearrange("(a j) -> j a", j=P))
+        nc.sync.dma_start(out=a1_t[0][:, :, P:], in_=a1[0:PASS, P:C].rearrange("(p j) c -> p j c", j=PACK))
+        for k in range(2 * PACK - 2, 2 * PACK):
             load_dy(k)
-        load_a1_half(3)
-        load_saved(a1, a1_t, 2, 0, 2)
-        load_saved(a1, a1_t, 2, 2, 4)
-        load_scales(w2s[:, 0:2], w2_scales[0:1])
-        for s in range(2):
-            load_w2(0, s)
+        load_w2(0)
+        load_saved(a1, a1_t, 1)
+        load_saved(a1, a1_t, 2)
         load_saved(a3, a3_t, 0)
-        load_scales(w2s[:, 2:4], w2_scales[1:2])
-        for s in range(2):
-            load_w2(1, s)
+        load_w2(1)
+        load_saved(a1, a1_t, 3)
         load_saved(a3, a3_t, 1)
-        load_saved(a1, a1_t, 3, 0, 2)
-        load_saved(a1, a1_t, 3, 2, 4)
-        load_saved(a3, a3_t, 2)
         load_scales(w13s[:, 0], w1_scales)
-        load_saved(a3, a3_t, 3)
         load_scales(w13s[:, 1], w3_scales)
         load_w13(0, w1_words)
         load_w13(1, w3_words)
+        load_saved(a3, a3_t, 2)
+        load_saved(a3, a3_t, 3)
 
         def interleaved(dst):
             return dst.rearrange("p (c i) t -> p c t i", i=4)
@@ -127,250 +117,210 @@ def tile_moe_bdx_glu_sigmoid_kernel(
         def planes(src):
             return src.rearrange("p t (c i) -> p c t i", i=4)
 
-        def quantise(src, slot, name):
-            width = src.shape[1]
-            codes = held([P, width], U32, slot)
-            scales = held([P, width], U8, name)
-            nc.vector.quantize_mx(out=codes[:].bitcast(E5M2X4), scales=scales[:], in_=src.rearrange("p c t -> p (c t)"))
-            return codes, scales
+        def quantise(codes, scales, src):
+            nc.vector.quantize_mx(out=codes.bitcast(E5M2X4), scales=scales, in_=src.rearrange("p c t -> p (c t)"))
 
-        def gather(e, k, dst, first=0, last=C):
+        def slots(e, first=0, last=C):
+            return offsets[:, (e * C + first) // 16:(e * C + last) // 16]
+
+        def gather_weighed(k, dst, first=0, last=C):
             nc.vector.tensor_tensor(
-                out=dst[:, k % PACK, first:last],
-                in0=dy[k][:].indirect(offsets[:, (e * C + first) // 16:(e * C + last) // 16]),
-                in1=gates[e][:, first:last],
-                op=MULT,
+                out=dst[:, k % PACK, first:last], in0=dy[k][:].indirect(slots(0, first, last)), in1=gate0[:, first:last], op=MULT
             )
 
-        def round_g(weighed, staged):
-            nc.scalar.copy(out=interleaved(staged), in_=planes(weighed))
+        def gather_plain(k, dst):
+            nc.scalar.activation(dst[:, k % PACK, :], dy[k][:].indirect(slots(1)), ACT.Copy)
 
-        def rest_across(b, pairs, halves):
-            for half, pair in product(halves, pairs):
-                bank = ring.tile([P, 2, 2, P], F32, name="bank")
-                for a in range(2):
-                    for t in range(2):
-                        first = (2 * pair + a) * P
-                        nc.tensor.transpose(bank[:, a, t, :], a1_t[b][:, 2 * half + t, first:first + P], ident[:])
-                nc.scalar.activation(
-                    out=across[b][pair][:, :, 2 * half:2 * half + 2, :],
-                    in_=bank[:],
-                    func=ACT.Sigmoid,
-                    scale=-1.0,
-                )
-
-        def rest(part):
-            nc.scalar.activation(out=part, in_=part, func=ACT.Sigmoid, scale=-1.0)
-
-        def rest_pair(b, pair, dst):
-            cols = slice(2 * pair * P, 2 * (pair + 1) * P)
-            nc.scalar.activation(out=dst, in_=a1_t[b][:, :, cols], func=ACT.Sigmoid, scale=-1.0)
-            rests[b, pair] = dst
-
-        rests = {(b, pair): a1_t[b][:, :, 2 * pair * P:2 * (pair + 1) * P] for b in range(4) for pair in range(2)}
-        g_codes, sums, slopes, firsts, backs, grads = {}, {}, {}, {}, {}, {}
-
-        def make_slopes(b, first, last, dst):
-            cols = slice(first * P, last * P)
-            rested = a1_t[b][:, :, cols] if b < 3 else rests[b, first // 2]
-            for a in range(first, last):
-                slopes[b, a] = dst[:, :, (a - first) * P:(a - first + 1) * P]
-            nc.gpsimd.tensor_tensor(out=dst, in0=rested, in1=a3_t[b][:, :, cols], op=MULT)
-
-        def first_products(b):
-            e, h = divmod(b, 2)
+        def weigh(src, dst):
+            gate1 = pinned.tile([P, C], F32, name="pin")
             for a in range(GROUPS):
-                dh = ring.tile([P, PASS], F32, name="bank")
-                sums[b, a] = dh
-                firsts[b, a] = across[b][a // 2][:, a % 2] if b < 2 else slopes[b - 2, a]
+                nc.tensor.transpose(gate1[:, a * P:(a + 1) * P], gate_col[:, a:a + 1].to_broadcast([P, P]), ident[:])
+            spread = gate1[:].rearrange("p (c i) -> p c i", i=4).unsqueeze(2).to_broadcast([P, C // 4, PACK, 4])
+            nc.vector.tensor_tensor(out=interleaved(dst), in0=planes(src), in1=spread, op=MULT)
+
+        g_codes, rests, firsts, seconds, staged, d_codes = {}, {}, {}, {}, {}, {}
+        rest_slots = ("r00", "r01", "r10", "r11", "weighed0", "r21", "plain0", "r31")
+
+        def turn(src):
+            bank = psum.tile([P, PACK, P], F32, name="bank")
+            for t in range(PACK):
+                nc.tensor.transpose(bank[:, t, :], src[:, t, :], ident[:])
+            return bank
+
+        def make_rest(b, pair, groups=range(2)):
+            if 0 in groups:
+                rests[b, pair] = held([P, 2, PACK, P], F32, rest_slots[2 * b + pair])
+            for a in groups:
+                first = (2 * pair + a) * P
+                bank = turn(early[:] if (b, pair, a) == (0, 0, 0) else a1_t[b][:, :, first:first + P])
+                nc.scalar.activation(out=rests[b, pair][:, a], in_=bank[:], func=ACT.Sigmoid, scale=-1.0)
+
+        def make_first(b, pair):
+            e, h = divmod(b, 2)
+            firsts[b, pair] = held([P, 2, PACK, P], F32, f"dy{2 * b + pair}")
+            for a in range(2):
+                cols = slice((2 * pair + a) * P, (2 * pair + a + 1) * P)
+                if (b, pair, a) == (0, 0, 1):
+                    dh = pinned.tile([P, PASS], F32, name="pin")
+                else:
+                    dh = psum.tile([P, PASS], F32, name="bank")
                 for s in range(2):
                     codes, scales = g_codes[e, s]
                     nc.tensor.matmul_mx(
                         out=dh[:],
-                        lhsT=codes[:, a * P:(a + 1) * P].bitcast(E5M2X4),
-                        lhsT_scale=scales[:, a * P:(a + 1) * P],
+                        lhsT=codes[:, cols].bitcast(E5M2X4),
+                        lhsT_scale=scales[:, cols],
                         rhs=w2[e][:, s, 2 * h * PASS:2 * (h + 1) * PASS].bitcast(E2M1X4),
                         rhs_scale=w2s[:, 2 * e + s, h * PASS:(h + 1) * PASS],
                         start=(s == 0),
                         stop=(s == 1),
                     )
                 nc.vector.scalar_tensor_tensor(
-                    out=firsts[b, a],
-                    in0=across[b][a // 2][:, a % 2],
+                    out=firsts[b, pair][:, a],
+                    in0=rests[b, pair][:, a],
                     scalar=1.0,
                     in1=dh[:].rearrange("p (m t) -> p t m", t=PACK),
                     op0=SUB,
                     op1=MULT,
                 )
 
-        def turn_back(b, groups=range(GROUPS)):
-            for a in groups:
-                backs[b, a] = ring.tile([P, PACK, P], F32, name="bank")
-                for t in range(PACK):
-                    nc.tensor.transpose(backs[b, a][:, t, :], firsts[b, a][:, t, :], ident[:])
-
-        def make_da1(b, a):
-            nc.vector.tensor_tensor(
-                out=interleaved(grads[b, a, 0]), in0=planes(backs[b, a][:]), in1=planes(slopes[b, a]), op=MULT
+        def make_second(b, pair, slot):
+            if pair == 0:
+                seconds[b] = held([P, 2, 2 * PASS], F32, slot)
+            nc.gpsimd.tensor_tensor(
+                out=seconds[b][:, pair],
+                in0=firsts[b, pair][:].rearrange("p a t m -> p (a t m)"),
+                in1=rests[b, pair][:].rearrange("p a t m -> p (a t m)"),
+                op=MULT,
             )
 
-        def make_da3(b, a):
-            nc.scalar.copy(out=grads[b, a, 1], in_=backs[b, a][:].rearrange("p t c -> p c t"))
+        def place(b, w, a):
+            if b < BLOCKS - 1:
+                return (w * GROUPS + a) * P
+            half = a // 2
+            return ((w if half == 0 else 3 - w) * 2 + a % 2) * P
 
-        def gradients(b):
-            for a in range(GROUPS):
-                make_da1(b, a)
-                make_da3(b, a)
+        def room(b, w, a):
+            first = place(b, w, a)
+            return staged[b][:, first:first + P, :]
 
-        def lay(room, parts):
-            for n, part in enumerate(parts):
-                grads[part] = room[:, n * P:(n + 1) * P, :]
+        def make_da3(b, pair):
+            for a in range(2):
+                bank = turn(firsts[b, pair][:, a])
+                nc.scalar.copy(out=room(b, 1, 2 * pair + a), in_=bank[:].rearrange("p t c -> p c t"))
 
-        def second_pass(dx, b, w, codes, scales, start, stop):
+        def make_da1(b, pair, groups=range(2)):
+            for a in groups:
+                first = (2 * pair + a) * P
+                bank = turn(seconds[b][:, pair, a * PASS:(a + 1) * PASS].rearrange("p (t m) -> p t m", t=PACK))
+                nc.vector.tensor_tensor(
+                    out=interleaved(room(b, 0, 2 * pair + a)),
+                    in0=planes(bank[:]),
+                    in1=planes(a3_t[b][:, :, first:first + P]),
+                    op=MULT,
+                )
+
+        def quantise_block(b, slot, first=0, last=2 * C):
+            if first == 0:
+                d_codes[b] = held([P, 2 * C], U32, slot), held([P, 2 * C], U8, f"d_scales{b}")
+            codes, scales = d_codes[b]
+            quantise(codes[:, first:last], scales[:, first:last], staged[b][:, first:last, :])
+
+        def second_pass(dx, b, w, a, width, start, stop):
+            codes, scales = d_codes[b]
+            cols = slice(place(b, w, a), place(b, w, a) + width)
             nc.tensor.matmul_mx(
-                out=dx[:],
+                out=dx[:, :width],
                 lhsT=w13[w][:, b, :].bitcast(E2M1X4),
                 lhsT_scale=w13s[:, w, b, :],
-                rhs=codes.bitcast(E5M2X4),
-                rhs_scale=scales,
+                rhs=codes[:, cols].bitcast(E5M2X4),
+                rhs_scale=scales[:, cols],
                 start=start,
                 stop=stop,
             )
 
-        def land(dx, first, landing):
-            nc.scalar.activation(out=landing, in_=dx[:, first:first + landing.shape[1]], func=ACT.Copy, scale=-1.0)
+        def put_back(e, a, width, order, slot):
+            dx = pinned.tile([P, C], F32, name="pin")
+            for n, (h, w) in enumerate(order):
+                second_pass(dx, 2 * e + h, w, a, width, n == 0, n == len(order) - 1)
+            landing = held([P, width], F32, slot)
+            nc.scalar.activation(out=landing[:], in_=dx[:, :width], func=ACT.Copy, scale=-1.0)
+            for first in range(0, width, HALF):
+                nc.scalar.activation(
+                    result[:].indirect(slots(e, a * P + first, a * P + first + HALF)), landing[:, first:first + HALF], ACT.Copy
+                )
 
-        def scatter(landing, first):
-            count = landing.shape[1]
-            nc.vector.tensor_copy(result[:].indirect(offsets[:, first // 16:(first + count) // 16]), landing)
-
-        weighed = {(e, 0): held([P, PACK, C], F32, f"weighed{e}0")[:] for e in range(E)}
-        weighed[0, 1] = second[:, 2 * C:].rearrange("p (t c) -> p t c", t=PACK)
-        weighed[1, 1] = second[:, :PACK * C].rearrange("p (t c) -> p t c", t=PACK)
-        gather(0, 0, weighed[0, 0], 0, C // 2)
-        gather(0, 0, weighed[0, 0], C // 2, C)
-        gather(1, 0, weighed[1, 0])
+        make_rest(0, 0, [0])
+        weighed0 = held([P, PACK, C], F32, "weighed0")
+        plain0 = held([P, PACK, C], F32, "plain0")
+        weighed1 = held([P, PACK, C], F32, "weighed1")
+        plain1 = held([P, PACK, C], F32, "plain1")
+        gather_weighed(0, weighed0, 0, HALF)
+        gather_weighed(0, weighed0, HALF, C)
+        gather_plain(0, plain0)
         for k in range(1, PACK):
-            for e in range(E):
-                gather(e, k, weighed[e, 0])
-        for b, half in ((0, 0), (0, 1), (1, 0)):
-            rest_across(b, [0, 1], [half])
-            rest(a1_t[b][:, 2 * half:2 * half + 2, :])
-        staged = held([P, E * C, PACK], BF16, "staged0")
-        for e in range(E):
-            round_g(weighed[e, 0], staged[:, e * C:(e + 1) * C, :])
-        for k in range(PACK, 2 * PACK):
-            gather(0, k, weighed[0, 1])
-        codes, scales = quantise(staged[:], "g0", "g_scales0")
-        for e in range(E):
-            g_codes[e, 0] = codes[:, e * C:(e + 1) * C], scales[:, e * C:(e + 1) * C]
-        staged = {(0, 1): held([P, C, PACK], BF16, "staged01")[:]}
-        round_g(weighed[0, 1], staged[0, 1])
-        rest_across(1, [0, 1], [1])
-        gather(1, PACK, weighed[1, 1])
-        gather(1, PACK + 1, weighed[1, 1])
-        g_codes[0, 1] = quantise(staged[0, 1], "g01", "g_scales01")
-        gather(1, PACK + 2, weighed[1, 1])
-        gather(1, PACK + 3, weighed[1, 1])
-        rest_across(2, [0, 1], [0, 1])
-        staged[1, 1] = held([P, C, PACK], BF16, "staged11")[:]
-        round_g(weighed[1, 1], staged[1, 1])
-        rest(a1_t[1][:, 2:4, :])
+            gather_weighed(k, weighed0)
+            gather_plain(k, plain0)
+        g0 = held([P, 2, C, PACK], BF16, "g0")
+        nc.scalar.copy(out=interleaved(g0[:, 0]), in_=planes(weighed0[:]))
+        for k in range(PACK, PACK + 2):
+            gather_weighed(k, weighed1)
+            gather_plain(k, plain1)
+        g1 = held([P, 2 * C, PACK], BF16, "g1")
+        weigh(plain0[:], g1[:, :C])
+        make_rest(0, 0, [1])
+        make_rest(0, 1)
+        for k in range(PACK + 2, 2 * PACK):
+            gather_weighed(k, weighed1)
+            gather_plain(k, plain1)
+        for s, slot in enumerate(("gate0", "g_codes1")):
+            g_codes[0, s] = held([P, C], U32, slot)[:], held([P, C], U8, f"g_scales{s}")[:]
+        quantise(*g_codes[0, 0], g0[:, 0])
+        nc.vector.tensor_copy(out=interleaved(g0[:, 1]), in_=planes(weighed1[:]))
+        quantise(*g_codes[0, 1], g0[:, 1])
 
-        make_slopes(0, 0, 4, held([P, PACK, C], F32, "gate1")[:])
-        first_products(0)
-        first_products(1)
-        g_codes[1, 1] = quantise(staged[1, 1], "g11", "g_scales11")
-        whole = [held([P, 2 * C, PACK], BF16, slot)[:] for slot in ("weighed00", "weighed01")]
-        for w in range(2):
-            lay(whole[w], [(b, a, w) for b, a in product(range(2), range(GROUPS))])
-        turn_back(0)
-        gradients(0)
-        room = held([P, 2, PACK, HALF], F32, "staged11")
-        make_slopes(1, 0, 2, room[:, 0])
-        make_slopes(1, 2, 4, room[:, 1])
+        staged_slots = ("staged0", "staged1", "a1_0", "a1_1")
         for pair in range(2):
-            rest_pair(2, pair, rests[2, pair])
-        make_slopes(2, 0, 3, held([P, PACK, 3 * P], F32, "a3_0")[:])
-        first_products(2)
-        rest_across(3, [0, 1], [0, 1])
-        turn_back(1)
-        gradients(1)
+            make_first(0, pair)
+        make_second(0, 0, "second0")
+        weigh(plain1[:], g1[:, C:])
+        make_second(0, 1, "second0")
+        make_rest(1, 0)
+        make_first(1, 0)
+        make_rest(1, 1)
+        codes, scales = held([P, 2 * C], U32, "r01"), held([P, 2 * C], U8, "g_scales2")
+        quantise(codes[:], scales[:], g1[:])
+        for s in range(2):
+            g_codes[1, s] = codes[:, s * C:(s + 1) * C], scales[:, s * C:(s + 1) * C]
+        for b in range(1, BLOCKS):
+            last = b == BLOCKS - 1
+            slot = "g1" if b == 1 else staged_slots[b - 2]
+            make_second(b, 0, slot)
+            staged[b - 1] = held([P, 2 * C, PACK], BF16, staged_slots[b - 1])
+            make_first(b, 1)
+            make_second(b, 1, slot)
+            for pair in range(2):
+                make_da3(b - 1, pair)
+            if last:
+                put_back(0, 0, C, list(product(range(2), range(2))), "landing0")
+            for pair in range(2):
+                make_da1(b - 1, pair)
+            if not last:
+                make_rest(b + 1, 0)
+                make_first(b + 1, 0)
+                make_rest(b + 1, 1)
+                quantise_block(b - 1, f"r{b}1")
+        b = BLOCKS - 1
+        staged[b] = held([P, 2 * C, PACK], BF16, staged_slots[b])
         for pair in range(2):
-            rest_pair(3, pair, held([P, PACK, HALF], F32, f"across2{pair}")[:])
-        first_products(3)
-        turn_back(2, (0, 1, 2))
-        dx = [sums[3, GROUPS - 1]]
-        codes, scales = quantise(whole[0], "across30", "d_scales0")
-        for b in range(2):
-            second_pass(dx[0], b, 0, codes[:, b * C:(b + 1) * C], scales[:, b * C:(b + 1) * C], b == 0, False)
-        codes = held([P, 2 * C], U32, "across31")
-        scales = held([P, 2 * C], U8, "d_scales1")
-        for b in range(2):
-            cols = slice(b * C, (b + 1) * C)
-            nc.vector.quantize_mx(
-                out=codes[:, cols].bitcast(E5M2X4), scales=scales[:, cols], in_=whole[1][:, cols, :].rearrange("p c t -> p (c t)")
-            )
-            second_pass(dx[0], b, 1, codes[:, cols], scales[:, cols], False, b == 1)
-
-        turn_back(3, (0, 1, 2, 3))
-        turn_back(2, (3,))
-        dx += [ring.tile([P, C], F32, name="bank") for half in range(2)]
-        room = held([P, 2, PACK, HALF], F32, "weighed01")
-        make_slopes(3, 0, 2, room[:, 0])
-        make_slopes(3, 2, 4, room[:, 1])
-        make_slopes(2, 3, 4, held([P, PACK, P], F32, "across20")[:])
-
-        def room_for(parts, slot):
-            room = held([P, len(parts) * HALF, PACK], BF16, slot)[:]
-            lay(room, [(b, 2 * half + i, w) for b, half, w in parts for i in range(2)])
-            return room
-
-        groups = [[(2, 0, 1), (3, 0, 1)], [(2, 0, 0), (3, 0, 0)], [(2, 1, 1), (3, 1, 1)], [(3, 1, 0)], [(2, 1, 0)]]
-        rooms = {n: room_for(groups[n], slot) for n, slot in ((1, "weighed10"), (4, "dy3"))}
-        early = held([P, EARLY], F32, "staged01")[:]
-        later = held([P, C - EARLY], F32, "dy0")[:]
-        land(dx[0], 0, early)
-        land(dx[0], EARLY, later)
-        for a in range(3):
-            make_da1(2, a)
-        scatter(early, 0)
-        both = room_for(groups[0] + groups[2], "staged01")
-        rooms[0], rooms[2] = both[:, :C, :], both[:, C:, :]
-        for b, a in ((3, 0), (3, 1), (2, 0), (2, 1), (2, 2), (3, 2), (3, 3), (2, 3)):
-            make_da3(b, a)
-        scatter(later, EARLY)
-        for a in range(2):
-            make_da1(3, a)
-
-        codes = held([P, 4 * C], U32, "a3_2")
-        scales = held([P, 4 * C], U8, "a3_3")
-        parts = [part for group in groups for part in group]
-
-        def quantise_group(n):
-            first = parts.index(groups[n][0]) * HALF
-            cols = slice(first, first + len(groups[n]) * HALF)
-            nc.vector.quantize_mx(
-                out=codes[:, cols].bitcast(E5M2X4), scales=scales[:, cols], in_=rooms[n].rearrange("p c t -> p (c t)")
-            )
-
-        def padded_pass(place):
-            b, half, w = parts[place]
-            cols = slice((place - half) * HALF, (place - half) * HALF + C)
-            second_pass(dx[1 + half], b, w, codes[:, cols], scales[:, cols], place % 4 == 0, place % 4 == 3)
-
-        for n, places in enumerate(((0,), (1, 2), (3, 4, 5))):
-            quantise_group(n)
-            for place in places:
-                padded_pass(place)
-        rooms[3] = room_for(groups[3], "weighed10")
-        for b, a in ((3, 2), (3, 3), (2, 3)):
-            make_da1(b, a)
-        for n in (3, 4):
-            quantise_group(n)
-            padded_pass(3 + n)
-        for half, slot in enumerate(("dy1", "staged0")):
-            landing = held([P, HALF], F32, slot)[:]
-            land(dx[1 + half], half * HALF, landing)
-            scatter(landing, C + half * HALF)
+            make_da3(b, pair)
+        make_da1(b, 0)
+        quantise_block(b - 1, "r31")
+        make_da1(b, 1, [0])
+        quantise_block(b, "r00", 0, C)
+        put_back(1, 0, HALF, list(product(range(2), range(2))), "landing1")
+        make_da1(b, 1, [1])
+        quantise_block(b, "r00", C, C + HALF)
+        quantise_block(b, "r00", C + HALF, 2 * C)
+        put_back(1, 2, HALF, [(0, 0), (0, 1), (1, 1), (1, 0)], "landing2")
         nc.sync.dma_start(out=out, in_=result[:])

@@ -1,5 +1,4 @@
 from contextlib import ExitStack
-from itertools import product
 
 import concourse.mybir as mybir
 from concourse.masks import make_identity
@@ -23,6 +22,7 @@ K, T, E, C, H, N = 128, 1024, 2, 512, 1024, 1024
 GROUPS = C // P
 HALF = C // 2
 BLOCKS = 4
+QUARTER = 4096
 FLOPS = 2 * E * C * (N * H + 2 * H * K)
 
 
@@ -32,15 +32,18 @@ def tile_moe_bdx_glu_sigmoid_kernel(
     nc = tc.nc
     with ExitStack() as ctx:
         keep = ctx.enter_context(tc.tile_pool(name="keep", bufs=1))
-        psum = ctx.enter_context(tc.psum_pool(name="psum", bufs=7))
-        pinned = ctx.enter_context(tc.psum_pool(name="pinned", bufs=1))
+        laid = ctx.enter_context(tc.tile_pool(name="laid", bufs=1))
+        banks = ctx.enter_context(tc.psum_pool(name="banks", bufs=1))
 
         def held(shape, dtype, slot):
             return keep.tile(shape, dtype, name=slot, align_bytes=64)
 
+        def placed(shape, dtype, name, region, first):
+            return laid.tile(shape, dtype, name=name, align_bytes=64, offset=(4 * region + first) * QUARTER)
+
         offsets = keep.tile([P, E * C // 16], U16, name="offsets")
         ident = held([P, P], F32, "ident")
-        gate0 = held([P, C], F32, "gate0")
+        gates = [held([P, C], F32, f"gate{e}") for e in range(E)]
         gate_col = held([P, GROUPS], F32, "gate_col")
         dy = [held([P, T], F32, f"dy{k}") for k in range(N // P)]
         w2 = [held([P, 2, 2 * H], U8, f"w2_{e}") for e in range(E)]
@@ -77,38 +80,43 @@ def tile_moe_bdx_glu_sigmoid_kernel(
                 in_=words.bitcast(I32).rearrange("e s p i -> p (e s) i"),
             )
 
-        def load_saved(src, dst, b):
+        def load_saved(src, dst, b, first=0, last=PACK):
             e, h = divmod(b, 2)
             nc.sync.dma_start(
-                out=dst[b][:],
-                in_=src[h * PASS:(h + 1) * PASS, e * C:(e + 1) * C].rearrange("(p j) c -> p j c", j=PACK),
+                out=dst[b][:, first:last],
+                in_=src[h * PASS:(h + 1) * PASS, e * C:(e + 1) * C].rearrange("(p j) c -> p j c", j=PACK)[:, first:last],
             )
 
-        early = held([P, PACK, P], F32, "early")
+        early = held([P, P], F32, "early")
+        first_block = a1[0:PASS, 0:C].rearrange("(p j) c -> p j c", j=PACK)
         nc.sync.dma_start(offsets[:], offs)
-        nc.sync.dma_start(out=early[:], in_=a1[0:PASS, 0:P].rearrange("(p j) c -> p j c", j=PACK))
-        nc.sync.dma_start(out=gate0[:, :HALF], in_=gate[0:P, 0:HALF])
+        nc.sync.dma_start(out=early[:], in_=first_block[:, 0, :P])
+        nc.sync.dma_start(out=gates[0][:, :HALF], in_=gate[0:P, 0:HALF])
         load_dy(0)
-        nc.sync.dma_start(out=gate0[:, HALF:], in_=gate[0:P, HALF:C])
-        for k in range(1, 2 * PACK - 2):
+        nc.sync.dma_start(out=gates[0][:, HALF:], in_=gate[0:P, HALF:C])
+        for k in range(1, PACK + 1):
             load_dy(k)
+        nc.sync.dma_start(out=gates[1][:], in_=gate[0:P, C:])
+        load_dy(PACK + 1)
+        nc.sync.dma_start(out=a1_t[0][:, 0, P:], in_=first_block[:, 0, P:])
+        nc.sync.dma_start(out=a1_t[0][:, 1:, :], in_=first_block[:, 1:, :])
+        load_dy(PACK + 2)
+        load_dy(PACK + 3)
         with nc.allow_non_contiguous_dma(reason="one gate a partition"):
             nc.sync.dma_start(out=gate_col[:], in_=gate[0, C:].rearrange("(a j) -> j a", j=P))
-        nc.sync.dma_start(out=a1_t[0][:, :, P:], in_=a1[0:PASS, P:C].rearrange("(p j) c -> p j c", j=PACK))
-        for k in range(2 * PACK - 2, 2 * PACK):
-            load_dy(k)
-        load_w2(0)
         load_saved(a1, a1_t, 1)
+        load_w2(0)
         load_saved(a1, a1_t, 2)
-        load_saved(a3, a3_t, 0)
+        load_saved(a3, a3_t, 0, 0, 2)
+        load_saved(a3, a3_t, 0, 2, 4)
         load_w2(1)
-        load_saved(a1, a1_t, 3)
         load_saved(a3, a3_t, 1)
+        load_saved(a1, a1_t, 3)
+        load_saved(a3, a3_t, 2)
         load_scales(w13s[:, 0], w1_scales)
         load_scales(w13s[:, 1], w3_scales)
         load_w13(0, w1_words)
         load_w13(1, w3_words)
-        load_saved(a3, a3_t, 2)
         load_saved(a3, a3_t, 3)
 
         def interleaved(dst):
@@ -123,47 +131,41 @@ def tile_moe_bdx_glu_sigmoid_kernel(
         def slots(e, first=0, last=C):
             return offsets[:, (e * C + first) // 16:(e * C + last) // 16]
 
-        def gather_weighed(k, dst, first=0, last=C):
+        def gather_weighed(e, k, dst, first=0, last=C):
             nc.vector.tensor_tensor(
-                out=dst[:, k % PACK, first:last], in0=dy[k][:].indirect(slots(0, first, last)), in1=gate0[:, first:last], op=MULT
+                out=dst[:, k % PACK, first:last],
+                in0=dy[k][:].indirect(slots(e, first, last)),
+                in1=gates[e][:, first:last],
+                op=MULT,
             )
 
-        def gather_plain(k, dst):
-            nc.scalar.activation(dst[:, k % PACK, :], dy[k][:].indirect(slots(1)), ACT.Copy)
+        def gather_plain(e, k, dst):
+            nc.scalar.activation(dst[:, k % PACK, :], dy[k][:].indirect(slots(e)), ACT.Copy)
 
-        def weigh(src, dst):
-            gate1 = pinned.tile([P, C], F32, name="pin")
-            for a in range(GROUPS):
-                nc.tensor.transpose(gate1[:, a * P:(a + 1) * P], gate_col[:, a:a + 1].to_broadcast([P, P]), ident[:])
-            spread = gate1[:].rearrange("p (c i) -> p c i", i=4).unsqueeze(2).to_broadcast([P, C // 4, PACK, 4])
-            nc.vector.tensor_tensor(out=interleaved(dst), in0=planes(src), in1=spread, op=MULT)
+        g_codes, sums, rests, firsts, slopes, backs, staged, d_codes = {}, {}, {}, {}, {}, {}, {}, {}
 
-        g_codes, rests, firsts, seconds, staged, d_codes = {}, {}, {}, {}, {}, {}
-        rest_slots = ("r00", "r01", "r10", "r11", "weighed0", "r21", "plain0", "r31")
-
-        def turn(src):
-            bank = psum.tile([P, PACK, P], F32, name="bank")
-            for t in range(PACK):
+        def turn(tag, src):
+            bank = banks.tile([P, src.shape[1], P], F32, name=tag)
+            for t in range(src.shape[1]):
                 nc.tensor.transpose(bank[:, t, :], src[:, t, :], ident[:])
             return bank
 
-        def make_rest(b, pair, groups=range(2)):
-            if 0 in groups:
-                rests[b, pair] = held([P, 2, PACK, P], F32, rest_slots[2 * b + pair])
-            for a in groups:
-                first = (2 * pair + a) * P
-                bank = turn(early[:] if (b, pair, a) == (0, 0, 0) else a1_t[b][:, :, first:first + P])
-                nc.scalar.activation(out=rests[b, pair][:, a], in_=bank[:], func=ACT.Sigmoid, scale=-1.0)
+        def rest(dst, src):
+            nc.scalar.activation(out=dst, in_=src, func=ACT.Sigmoid, scale=-1.0)
 
-        def make_first(b, pair):
+        def make_rests(b, side):
+            for pair in range(2):
+                both = held([P, 2, PACK, P], F32, f"dy{2 * (b - 1) + pair}")
+                for a in range(2 * pair, 2 * pair + 2):
+                    rests[b, a] = both[:, a % 2]
+                    rest(rests[b, a], turn(f"{side}{a}", a1_t[b][:, :, a * P:(a + 1) * P])[:])
+
+        def first_products(b, side, groups=range(GROUPS)):
             e, h = divmod(b, 2)
-            firsts[b, pair] = held([P, 2, PACK, P], F32, f"dy{2 * b + pair}")
-            for a in range(2):
-                cols = slice((2 * pair + a) * P, (2 * pair + a + 1) * P)
-                if (b, pair, a) == (0, 0, 1):
-                    dh = pinned.tile([P, PASS], F32, name="pin")
-                else:
-                    dh = psum.tile([P, PASS], F32, name="bank")
+            for a in groups:
+                cols = slice(a * P, (a + 1) * P)
+                dh = banks.tile([P, PASS], F32, name=f"{side}{a}")
+                sums[b, a] = dh
                 for s in range(2):
                     codes, scales = g_codes[e, s]
                     nc.tensor.matmul_mx(
@@ -175,152 +177,170 @@ def tile_moe_bdx_glu_sigmoid_kernel(
                         start=(s == 0),
                         stop=(s == 1),
                     )
+
+        def make_first(b):
+            for a in range(GROUPS):
                 nc.vector.scalar_tensor_tensor(
-                    out=firsts[b, pair][:, a],
-                    in0=rests[b, pair][:, a],
+                    out=firsts[b][:, a],
+                    in0=rests[b, a],
                     scalar=1.0,
-                    in1=dh[:].rearrange("p (m t) -> p t m", t=PACK),
+                    in1=sums[b, a][:].rearrange("p (m t) -> p t m", t=PACK),
                     op0=SUB,
                     op1=MULT,
                 )
 
-        def make_second(b, pair, slot):
-            if pair == 0:
-                seconds[b] = held([P, 2, 2 * PASS], F32, slot)
-            nc.gpsimd.tensor_tensor(
-                out=seconds[b][:, pair],
-                in0=firsts[b, pair][:].rearrange("p a t m -> p (a t m)"),
-                in1=rests[b, pair][:].rearrange("p a t m -> p (a t m)"),
-                op=MULT,
-            )
+        def make_slope(b, step=PACK):
+            if b == 0:
+                slopes[b] = held([P, PACK, C], F32, "rounded11")
+            else:
+                slopes[b] = placed([P, PACK, C], F32, f"slope{b}", b - 1, 0)
+                firsts[b] = placed([P, GROUPS, PACK, P], F32, f"first{b}", b - 1, 2)
+            for t in range(0, PACK, step):
+                part = slice(t, t + step)
+                nc.gpsimd.tensor_tensor(out=slopes[b][:, part], in0=plain[b][:, part], in1=a3_t[b][:, part], op=MULT)
 
         def place(b, w, a):
-            if b < BLOCKS - 1:
-                return (w * GROUPS + a) * P
-            half = a // 2
-            return ((w if half == 0 else 3 - w) * 2 + a % 2) * P
+            if b < 2:
+                return b, (w * GROUPS + a) * P
+            part = w if b == 2 else 3 - w
+            return 2 + a // 2, (2 * part + a % 2) * P
 
         def room(b, w, a):
-            first = place(b, w, a)
-            return staged[b][:, first:first + P, :]
+            n, first = place(b, w, a)
+            return staged[n][:, first:first + P, :]
 
-        def make_da3(b, pair):
-            for a in range(2):
-                bank = turn(firsts[b, pair][:, a])
-                nc.scalar.copy(out=room(b, 1, 2 * pair + a), in_=bank[:].rearrange("p t c -> p c t"))
-
-        def make_da1(b, pair, groups=range(2)):
+        def make_da3(b, side, groups=range(GROUPS)):
             for a in groups:
-                first = (2 * pair + a) * P
-                bank = turn(seconds[b][:, pair, a * PASS:(a + 1) * PASS].rearrange("p (t m) -> p t m", t=PACK))
+                backs[b, a] = turn(f"{side}{a}", firsts[b][:, a])
+                nc.scalar.copy(out=room(b, 1, a), in_=backs[b, a][:].rearrange("p t c -> p c t"))
+
+        def make_da1(b, groups=range(GROUPS)):
+            for a in groups:
                 nc.vector.tensor_tensor(
-                    out=interleaved(room(b, 0, 2 * pair + a)),
-                    in0=planes(bank[:]),
-                    in1=planes(a3_t[b][:, :, first:first + P]),
+                    out=interleaved(room(b, 0, a)),
+                    in0=planes(backs[b, a][:]),
+                    in1=planes(slopes[b][:, :, a * P:(a + 1) * P]),
                     op=MULT,
                 )
 
-        def quantise_block(b, slot, first=0, last=2 * C):
+        def quantise_set(n, slot, first=0, last=2 * C):
             if first == 0:
-                d_codes[b] = held([P, 2 * C], U32, slot), held([P, 2 * C], U8, f"d_scales{b}")
-            codes, scales = d_codes[b]
-            quantise(codes[:, first:last], scales[:, first:last], staged[b][:, first:last, :])
+                d_codes[n] = held([P, 2 * C], U32, slot), held([P, 2 * C], U8, f"d_scales{n}")
+            codes, scales = d_codes[n]
+            quantise(codes[:, first:last], scales[:, first:last], staged[n][:, first:last, :])
 
-        def second_pass(dx, b, w, a, width, start, stop):
-            codes, scales = d_codes[b]
-            cols = slice(place(b, w, a), place(b, w, a) + width)
-            nc.tensor.matmul_mx(
-                out=dx[:, :width],
-                lhsT=w13[w][:, b, :].bitcast(E2M1X4),
-                lhsT_scale=w13s[:, w, b, :],
-                rhs=codes[:, cols].bitcast(E5M2X4),
-                rhs_scale=scales[:, cols],
-                start=start,
-                stop=stop,
-            )
-
-        def put_back(e, a, width, order, slot):
-            dx = pinned.tile([P, C], F32, name="pin")
-            for n, (h, w) in enumerate(order):
-                second_pass(dx, 2 * e + h, w, a, width, n == 0, n == len(order) - 1)
-            landing = held([P, width], F32, slot)
-            nc.scalar.activation(out=landing[:], in_=dx[:, :width], func=ACT.Copy, scale=-1.0)
-            for first in range(0, width, HALF):
-                nc.scalar.activation(
-                    result[:].indirect(slots(e, a * P + first, a * P + first + HALF)), landing[:, first:first + HALF], ACT.Copy
+        def second_products(e, half, tag):
+            dx = banks.tile([P, HALF], F32, name=tag)
+            order = ((0, 0), (0, 1), (1, 1), (1, 0))
+            for step, (h, w) in enumerate(order):
+                n, first = place(2 * e + h, w, 2 * half)
+                codes, scales = d_codes[n]
+                nc.tensor.matmul_mx(
+                    out=dx[:],
+                    lhsT=w13[w][:, 2 * e + h, :].bitcast(E2M1X4),
+                    lhsT_scale=w13s[:, w, 2 * e + h, :],
+                    rhs=codes[:, first:first + HALF].bitcast(E5M2X4),
+                    rhs_scale=scales[:, first:first + HALF],
+                    start=step == 0,
+                    stop=step == len(order) - 1,
                 )
+            landing = held([P, HALF], F32, f"dy{2 * e + half}")
+            if (e, half) == (1, 1):
+                nc.vector.tensor_scalar_mul(landing[:], dx[:], -1.0)
+            else:
+                nc.scalar.activation(out=landing[:], in_=dx[:], func=ACT.Copy, scale=-1.0)
+            return landing
 
-        make_rest(0, 0, [0])
-        weighed0 = held([P, PACK, C], F32, "weighed0")
-        plain0 = held([P, PACK, C], F32, "plain0")
-        weighed1 = held([P, PACK, C], F32, "weighed1")
-        plain1 = held([P, PACK, C], F32, "plain1")
-        gather_weighed(0, weighed0, 0, HALF)
-        gather_weighed(0, weighed0, HALF, C)
-        gather_plain(0, plain0)
+        def window(e, half):
+            return result[:].indirect(slots(e, half * HALF, (half + 1) * HALF))
+
+        firsts[0] = held([P, GROUPS, PACK, P], F32, "rest0")
+        for a in range(GROUPS):
+            rests[0, a] = firsts[0][:, a]
+        rest(rests[0, 0][:, :1], turn("x0", early[:].unsqueeze(1))[:])
+        weighed = {
+            (e, s): placed([P, PACK, C], F32, f"weighed{e}{s}", region, 1) for region, (e, s) in enumerate(((1, 1), (0, 0), (0, 1)))
+        }
+        weighed[1, 0] = held([P, PACK, C], F32, "weighed10")
+        gather_weighed(0, 0, weighed[0, 0], 0, HALF)
+        gather_weighed(0, 0, weighed[0, 0], HALF, C)
+        gather_plain(1, 0, weighed[1, 0])
         for k in range(1, PACK):
-            gather_weighed(k, weighed0)
-            gather_plain(k, plain0)
-        g0 = held([P, 2, C, PACK], BF16, "g0")
-        nc.scalar.copy(out=interleaved(g0[:, 0]), in_=planes(weighed0[:]))
-        for k in range(PACK, PACK + 2):
-            gather_weighed(k, weighed1)
-            gather_plain(k, plain1)
-        g1 = held([P, 2 * C, PACK], BF16, "g1")
-        weigh(plain0[:], g1[:, :C])
-        make_rest(0, 0, [1])
-        make_rest(0, 1)
-        for k in range(PACK + 2, 2 * PACK):
-            gather_weighed(k, weighed1)
-            gather_plain(k, plain1)
-        for s, slot in enumerate(("gate0", "g_codes1")):
-            g_codes[0, s] = held([P, C], U32, slot)[:], held([P, C], U8, f"g_scales{s}")[:]
-        quantise(*g_codes[0, 0], g0[:, 0])
-        nc.vector.tensor_copy(out=interleaved(g0[:, 1]), in_=planes(weighed1[:]))
-        quantise(*g_codes[0, 1], g0[:, 1])
+            gather_weighed(0, k, weighed[0, 0])
+            gather_plain(1, k, weighed[1, 0])
+        rounded = {(e, s): held([P, C, PACK], BF16, f"rounded{e}{s}") for e, s in ((0, 0), (0, 1), (1, 1))}
+        nc.scalar.copy(out=interleaved(rounded[0, 0][:]), in_=planes(weighed[0, 0][:]))
+        rest(rests[0, 0][:, 1:], turn("x0", a1_t[0][:, 1:, :P])[:])
+        for a in range(1, GROUPS):
+            rest(rests[0, a], turn(f"x{a}", a1_t[0][:, :, a * P:(a + 1) * P])[:])
+        rest(a1_t[0][:, 0, :P], early[:])
+        rest(a1_t[0][:, 0, P:], a1_t[0][:, 0, P:])
+        rest(a1_t[0][:, 1:, :], a1_t[0][:, 1:, :])
+        for k in range(PACK, 2 * PACK):
+            for e in range(E):
+                gather_weighed(e, k, weighed[e, 1])
 
-        staged_slots = ("staged0", "staged1", "a1_0", "a1_1")
-        for pair in range(2):
-            make_first(0, pair)
-        make_second(0, 0, "second0")
-        weigh(plain1[:], g1[:, C:])
-        make_second(0, 1, "second0")
-        make_rest(1, 0)
-        make_first(1, 0)
-        make_rest(1, 1)
-        codes, scales = held([P, 2 * C], U32, "r01"), held([P, 2 * C], U8, "g_scales2")
-        quantise(codes[:], scales[:], g1[:])
-        for s in range(2):
-            g_codes[1, s] = codes[:, s * C:(s + 1) * C], scales[:, s * C:(s + 1) * C]
-        for b in range(1, BLOCKS):
-            last = b == BLOCKS - 1
-            slot = "g1" if b == 1 else staged_slots[b - 2]
-            make_second(b, 0, slot)
-            staged[b - 1] = held([P, 2 * C, PACK], BF16, staged_slots[b - 1])
-            make_first(b, 1)
-            make_second(b, 1, slot)
-            for pair in range(2):
-                make_da3(b - 1, pair)
-            if last:
-                put_back(0, 0, C, list(product(range(2), range(2))), "landing0")
-            for pair in range(2):
-                make_da1(b - 1, pair)
-            if not last:
-                make_rest(b + 1, 0)
-                make_first(b + 1, 0)
-                make_rest(b + 1, 1)
-                quantise_block(b - 1, f"r{b}1")
+        def quantise_g(e, s, slot):
+            g_codes[e, s] = held([P, C], U32, slot)[:], held([P, C], U8, f"g_scales{e}{s}")[:]
+            quantise(*g_codes[e, s], rounded[e, s][:])
+
+        for e in range(E):
+            nc.vector.tensor_copy(out=interleaved(rounded[e, 1][:]), in_=planes(weighed[e, 1][:]))
+        quantise_g(0, 0, "gate0")
+        quantise_g(0, 1, "g_codes01")
+        quantise_g(1, 1, "g_codes11")
+        for b, side in ((1, "y"), (2, "x")):
+            make_rests(b, side)
+            rest(a1_t[b][:], a1_t[b][:])
+
+        plain = dict(enumerate(a1_t))
+        make_slope(0, 2)
+        spread = banks.tile([P, C], F32, name="y3")
+        for a in range(GROUPS):
+            nc.tensor.transpose(spread[:, a * P:(a + 1) * P], gate_col[:, a:a + 1].to_broadcast([P, P]), ident[:])
+        rounded[1, 0] = laid.tile([P, C, PACK], BF16, name="rounded10", align_bytes=64, offset=3 * QUARTER // 2)
+        nc.vector.tensor_tensor(
+            out=interleaved(rounded[1, 0][:]),
+            in0=planes(weighed[1, 0][:]),
+            in1=spread[:].rearrange("p (c i) -> p c i", i=4).unsqueeze(2).to_broadcast([P, C // 4, PACK, 4]),
+            op=MULT,
+        )
+        first_products(0, "y")
+        make_first(0)
+        first_products(1, "x")
+        quantise_g(1, 0, "a3_0")
+        for b in range(BLOCKS - 1):
+            make_slope(b + 1)
+            if b < BLOCKS - 2:
+                staged[b] = placed([P, 2 * C, PACK], BF16, f"staged{b}", b + 1, 1)
+                make_da3(b, "y")
+            else:
+                for n, slot in ((b, "staged2"), (b + 1, "weighed10")):
+                    staged[n] = held([P, 2 * C, PACK], BF16, slot)
+                make_da3(b, "y", range(GROUPS - 1))
+                landing = second_products(0, 0, "y3")
+                make_da3(b, "y", [GROUPS - 1])
+            make_first(b + 1)
+            if b < BLOCKS - 2:
+                first_products(b + 2, "x")
+            make_da1(b)
+            if b == 0:
+                plain[3] = held([P, PACK, C], F32, "a1_0")
+                rest(plain[3][:], a1_t[3][:])
+                make_rests(3, "y")
+            if b < BLOCKS - 2:
+                quantise_set(b, f"a3_{b + 1}")
         b = BLOCKS - 1
-        staged[b] = held([P, 2 * C, PACK], BF16, staged_slots[b])
-        for pair in range(2):
-            make_da3(b, pair)
-        make_da1(b, 0)
-        quantise_block(b - 1, "r31")
-        make_da1(b, 1, [0])
-        quantise_block(b, "r00", 0, C)
-        put_back(1, 0, HALF, list(product(range(2), range(2))), "landing1")
-        make_da1(b, 1, [1])
-        quantise_block(b, "r00", C, C + HALF)
-        quantise_block(b, "r00", C + HALF, 2 * C)
-        put_back(1, 2, HALF, [(0, 0), (0, 1), (1, 1), (1, 0)], "landing2")
+        make_da3(b, "x")
+        nc.scalar.activation(window(0, 0), landing[:], ACT.Copy)
+        nc.scalar.activation(window(0, 1), second_products(0, 1, "y0")[:], ACT.Copy)
+        make_da1(b, [0, 1])
+        quantise_set(2, "a3_3")
+        nc.scalar.activation(window(1, 0), second_products(1, 0, "y1")[:], ACT.Copy)
+        make_da1(b, [2])
+        quantise_set(3, "dy6", 0, C)
+        make_da1(b, [3])
+        quantise_set(3, "dy6", C, C + HALF)
+        quantise_set(3, "dy6", C + HALF, 2 * C)
+        nc.vector.tensor_copy(window(1, 1), second_products(1, 1, "y2")[:])
         nc.sync.dma_start(out=out, in_=result[:])

@@ -13,6 +13,7 @@ E5M2X4 = mybir.dt.float8_e5m2_x4
 E2M1X4 = mybir.dt.float4_e2m1fn_x4
 ACT = mybir.ActivationFunctionType
 MULT = mybir.AluOpType.mult
+ADD = mybir.AluOpType.add
 SUB = mybir.AluOpType.subtract
 
 P = 128
@@ -43,7 +44,7 @@ def tile_moe_bdx_glu_sigmoid_kernel(
 
         offsets = keep.tile([P, E * C // 16], U16, name="offsets")
         ident = held([P, P], F32, "ident")
-        gates = [held([P, C], F32, f"gate{e}") for e in range(E)]
+        gate0 = held([P, C], F32, "gate0")
         gate_col = held([P, GROUPS], F32, "gate_col")
         dy = [held([P, T], F32, f"dy{k}") for k in range(N // P)]
         w2 = [held([P, 2, 2 * H], U8, f"w2_{e}") for e in range(E)]
@@ -52,11 +53,13 @@ def tile_moe_bdx_glu_sigmoid_kernel(
         w13s = held([P, 2, 4, K], U8, "w13s")
         a1_t = [held([P, PACK, C], F32, f"a1_{b}") for b in range(BLOCKS)]
         a3_t = [held([P, PACK, C], F32, f"a3_{b}") for b in range(BLOCKS)]
-        result = held([P, T], F32, "result")
+        results = [held([P, T], F32, f"result{n}") for n in range(2)]
 
         make_identity(nc, ident[:])
         nc.vector.memset(w2s[:].rearrange("p b i -> p (b i)").bitcast(I32), 0)
         nc.vector.memset(w13s[:].rearrange("p w b k -> p (w b k)").bitcast(I32), 0)
+        for result in results:
+            nc.vector.memset(result[:], 0.0)
 
         def load_dy(k):
             s, j = divmod(k, PACK)
@@ -91,33 +94,29 @@ def tile_moe_bdx_glu_sigmoid_kernel(
         first_block = a1[0:PASS, 0:C].rearrange("(p j) c -> p j c", j=PACK)
         nc.sync.dma_start(offsets[:], offs)
         nc.sync.dma_start(out=early[:], in_=first_block[:, 0, :P])
-        nc.sync.dma_start(out=gates[0][:, :HALF], in_=gate[0:P, 0:HALF])
+        nc.sync.dma_start(out=gate0[:, :HALF], in_=gate[0:P, 0:HALF])
         load_dy(0)
-        nc.sync.dma_start(out=gates[0][:, HALF:], in_=gate[0:P, HALF:C])
-        for k in range(1, PACK + 1):
+        nc.sync.dma_start(out=gate0[:, HALF:], in_=gate[0:P, HALF:C])
+        for k in range(1, 2 * PACK):
             load_dy(k)
-        nc.sync.dma_start(out=gates[1][:], in_=gate[0:P, C:])
-        load_dy(PACK + 1)
         nc.sync.dma_start(out=a1_t[0][:, 0, P:], in_=first_block[:, 0, P:])
         nc.sync.dma_start(out=a1_t[0][:, 1:, :], in_=first_block[:, 1:, :])
-        load_dy(PACK + 2)
-        load_dy(PACK + 3)
         with nc.allow_non_contiguous_dma(reason="one gate a partition"):
             nc.sync.dma_start(out=gate_col[:], in_=gate[0, C:].rearrange("(a j) -> j a", j=P))
         load_saved(a1, a1_t, 1)
-        load_w2(0)
-        load_saved(a1, a1_t, 2)
         load_saved(a3, a3_t, 0, 0, 2)
+        load_w2(0)
         load_saved(a3, a3_t, 0, 2, 4)
-        load_w2(1)
         load_saved(a3, a3_t, 1)
-        load_saved(a1, a1_t, 3)
+        load_w2(1)
+        load_saved(a1, a1_t, 2)
         load_saved(a3, a3_t, 2)
+        load_saved(a1, a1_t, 3)
+        load_saved(a3, a3_t, 3)
         load_scales(w13s[:, 0], w1_scales)
         load_scales(w13s[:, 1], w3_scales)
         load_w13(0, w1_words)
         load_w13(1, w3_words)
-        load_saved(a3, a3_t, 3)
 
         def interleaved(dst):
             return dst.rearrange("p (c i) t -> p c t i", i=4)
@@ -131,16 +130,13 @@ def tile_moe_bdx_glu_sigmoid_kernel(
         def slots(e, first=0, last=C):
             return offsets[:, (e * C + first) // 16:(e * C + last) // 16]
 
-        def gather_weighed(e, k, dst, first=0, last=C):
+        def gather_weighed(k, dst, first=0, last=C):
             nc.vector.tensor_tensor(
-                out=dst[:, k % PACK, first:last],
-                in0=dy[k][:].indirect(slots(e, first, last)),
-                in1=gates[e][:, first:last],
-                op=MULT,
+                out=dst[:, k % PACK, first:last], in0=dy[k][:].indirect(slots(0, first, last)), in1=gate0[:, first:last], op=MULT
             )
 
-        def gather_plain(e, k, dst):
-            nc.scalar.activation(dst[:, k % PACK, :], dy[k][:].indirect(slots(e)), ACT.Copy)
+        def gather_plain(k, dst):
+            nc.scalar.activation(dst[:, k % PACK, :], dy[k][:].indirect(slots(1)), ACT.Copy)
 
         g_codes, sums, rests, firsts, slopes, backs, staged, d_codes = {}, {}, {}, {}, {}, {}, {}, {}
 
@@ -153,12 +149,12 @@ def tile_moe_bdx_glu_sigmoid_kernel(
         def rest(dst, src):
             nc.scalar.activation(out=dst, in_=src, func=ACT.Sigmoid, scale=-1.0)
 
-        def make_rests(b, side):
+        def make_rests(b, tags):
             for pair in range(2):
                 both = held([P, 2, PACK, P], F32, f"dy{2 * (b - 1) + pair}")
                 for a in range(2 * pair, 2 * pair + 2):
                     rests[b, a] = both[:, a % 2]
-                    rest(rests[b, a], turn(f"{side}{a}", a1_t[b][:, :, a * P:(a + 1) * P])[:])
+                    rest(rests[b, a], turn(tags[a], a1_t[b][:, :, a * P:(a + 1) * P])[:])
 
         def first_products(b, side, groups=range(GROUPS)):
             e, h = divmod(b, 2)
@@ -189,15 +185,17 @@ def tile_moe_bdx_glu_sigmoid_kernel(
                     op1=MULT,
                 )
 
-        def make_slope(b, step=PACK):
+        def make_slope(b):
             if b == 0:
-                slopes[b] = held([P, PACK, C], F32, "rounded11")
+                slopes[b] = held([P, PACK, C], F32, "rounded00")
+                parts = [(slice(t, t + 2), slice(0, C)) for t in range(0, PACK, 2)]
             else:
                 slopes[b] = placed([P, PACK, C], F32, f"slope{b}", b - 1, 0)
                 firsts[b] = placed([P, GROUPS, PACK, P], F32, f"first{b}", b - 1, 2)
-            for t in range(0, PACK, step):
-                part = slice(t, t + step)
-                nc.gpsimd.tensor_tensor(out=slopes[b][:, part], in0=plain[b][:, part], in1=a3_t[b][:, part], op=MULT)
+                step = HALF if b == BLOCKS - 1 else C
+                parts = [(slice(0, PACK), slice(first, first + step)) for first in range(0, C, step)]
+            for ts, cols in parts:
+                nc.gpsimd.tensor_tensor(out=slopes[b][:, ts, cols], in0=plain[b][:, ts, cols], in1=a3_t[b][:, ts, cols], op=MULT)
 
         def place(b, w, a):
             if b < 2:
@@ -229,7 +227,7 @@ def tile_moe_bdx_glu_sigmoid_kernel(
             codes, scales = d_codes[n]
             quantise(codes[:, first:last], scales[:, first:last], staged[n][:, first:last, :])
 
-        def second_products(e, half, tag):
+        def second_products(e, half, tag, landing):
             dx = banks.tile([P, HALF], F32, name=tag)
             order = ((0, 0), (0, 1), (1, 1), (1, 0))
             for step, (h, w) in enumerate(order):
@@ -244,7 +242,6 @@ def tile_moe_bdx_glu_sigmoid_kernel(
                     start=step == 0,
                     stop=step == len(order) - 1,
                 )
-            landing = held([P, HALF], F32, f"dy{2 * e + half}")
             if (e, half) == (1, 1):
                 nc.vector.tensor_scalar_mul(landing[:], dx[:], -1.0)
             else:
@@ -252,95 +249,95 @@ def tile_moe_bdx_glu_sigmoid_kernel(
             return landing
 
         def window(e, half):
-            return result[:].indirect(slots(e, half * HALF, (half + 1) * HALF))
+            return results[e * half][:].indirect(slots(e, half * HALF, (half + 1) * HALF))
 
         firsts[0] = held([P, GROUPS, PACK, P], F32, "rest0")
         for a in range(GROUPS):
             rests[0, a] = firsts[0][:, a]
         rest(rests[0, 0][:, :1], turn("x0", early[:].unsqueeze(1))[:])
-        weighed = {
-            (e, s): placed([P, PACK, C], F32, f"weighed{e}{s}", region, 1) for region, (e, s) in enumerate(((1, 1), (0, 0), (0, 1)))
-        }
-        weighed[1, 0] = held([P, PACK, C], F32, "weighed10")
-        gather_weighed(0, 0, weighed[0, 0], 0, HALF)
-        gather_weighed(0, 0, weighed[0, 0], HALF, C)
-        gather_plain(1, 0, weighed[1, 0])
-        for k in range(1, PACK):
-            gather_weighed(0, k, weighed[0, 0])
-            gather_plain(1, k, weighed[1, 0])
-        rounded = {(e, s): held([P, C, PACK], BF16, f"rounded{e}{s}") for e, s in ((0, 0), (0, 1), (1, 1))}
-        nc.scalar.copy(out=interleaved(rounded[0, 0][:]), in_=planes(weighed[0, 0][:]))
+        weighed = [placed([P, PACK, C], F32, f"weighed{s}", region, 1) for s, region in enumerate((1, 0))]
+        picked = [held([P, PACK, C], F32, f"picked{s}") for s in range(2)]
+        rounded = {(0, s): held([P, C, PACK], BF16, f"rounded0{s}") for s in range(2)}
+        gather_weighed(0, weighed[0], 0, HALF)
+        gather_weighed(0, weighed[0], HALF, C)
+        for k in range(2 * PACK):
+            s = k // PACK
+            if k > 0:
+                gather_weighed(k, weighed[s])
+            gather_plain(k, picked[s])
+            if k % PACK == PACK - 1:
+                nc.vector.tensor_copy(out=interleaved(rounded[0, s][:]), in_=planes(weighed[s][:]))
+
+        def quantise_g(e, s, codes, scales):
+            g_codes[e, s] = codes, scales
+            quantise(codes, scales, rounded[e, s][:])
+
+        for s, slot in enumerate(("gate0", "g_codes01")):
+            quantise_g(0, s, held([P, C], U32, slot)[:], held([P, C], U8, f"g_scales0{s}")[:])
+        plain = {0: placed([P, PACK, C], F32, "plain0", 1, 1), 1: a1_t[1]}
+        rest(plain[0][:, 0, :P], early[:])
+        rest(plain[0][:, 0, P:], a1_t[0][:, 0, P:])
+        rest(plain[0][:, 1:, :], a1_t[0][:, 1:, :])
         rest(rests[0, 0][:, 1:], turn("x0", a1_t[0][:, 1:, :P])[:])
         for a in range(1, GROUPS):
             rest(rests[0, a], turn(f"x{a}", a1_t[0][:, :, a * P:(a + 1) * P])[:])
-        rest(a1_t[0][:, 0, :P], early[:])
-        rest(a1_t[0][:, 0, P:], a1_t[0][:, 0, P:])
-        rest(a1_t[0][:, 1:, :], a1_t[0][:, 1:, :])
-        for k in range(PACK, 2 * PACK):
-            for e in range(E):
-                gather_weighed(e, k, weighed[e, 1])
 
-        def quantise_g(e, s, slot):
-            g_codes[e, s] = held([P, C], U32, slot)[:], held([P, C], U8, f"g_scales{e}{s}")[:]
-            quantise(*g_codes[e, s], rounded[e, s][:])
-
-        for e in range(E):
-            nc.vector.tensor_copy(out=interleaved(rounded[e, 1][:]), in_=planes(weighed[e, 1][:]))
-        quantise_g(0, 0, "gate0")
-        quantise_g(0, 1, "g_codes01")
-        quantise_g(1, 1, "g_codes11")
-        for b, side in ((1, "y"), (2, "x")):
-            make_rests(b, side)
-            rest(a1_t[b][:], a1_t[b][:])
-
-        plain = dict(enumerate(a1_t))
-        make_slope(0, 2)
+        make_slope(0)
         spread = banks.tile([P, C], F32, name="y3")
         for a in range(GROUPS):
             nc.tensor.transpose(spread[:, a * P:(a + 1) * P], gate_col[:, a:a + 1].to_broadcast([P, P]), ident[:])
-        rounded[1, 0] = laid.tile([P, C, PACK], BF16, name="rounded10", align_bytes=64, offset=3 * QUARTER // 2)
-        nc.vector.tensor_tensor(
-            out=interleaved(rounded[1, 0][:]),
-            in0=planes(weighed[1, 0][:]),
-            in1=spread[:].rearrange("p (c i) -> p c i", i=4).unsqueeze(2).to_broadcast([P, C // 4, PACK, 4]),
-            op=MULT,
-        )
+        rounded[1, 0] = held([P, C, PACK], BF16, "rounded01")
+        rounded[1, 1] = laid.tile([P, C, PACK], BF16, name="rounded11", align_bytes=64, offset=3 * QUARTER // 2)
+        for s in range(2):
+            nc.vector.tensor_tensor(
+                out=interleaved(rounded[1, s][:]),
+                in0=planes(picked[s][:]),
+                in1=spread[:].rearrange("p (c i) -> p c i", i=4).unsqueeze(2).to_broadcast([P, C // 4, PACK, 4]),
+                op=MULT,
+            )
+        make_rests(1, ("y0", "y1", "y2", "x0"))
+        rest(a1_t[1][:], a1_t[1][:])
         first_products(0, "y")
         make_first(0)
-        first_products(1, "x")
-        quantise_g(1, 0, "a3_0")
+        first_products(1, "y")
+        codes, scales = held([P, 2, C], U32, "a3_0"), held([P, 2, C], U8, "g_scales1")
+        for s in range(2):
+            quantise_g(1, s, codes[:, s], scales[:, s])
         for b in range(BLOCKS - 1):
             make_slope(b + 1)
             if b < BLOCKS - 2:
                 staged[b] = placed([P, 2 * C, PACK], BF16, f"staged{b}", b + 1, 1)
-                make_da3(b, "y")
             else:
-                for n, slot in ((b, "staged2"), (b + 1, "weighed10")):
-                    staged[n] = held([P, 2 * C, PACK], BF16, slot)
-                make_da3(b, "y", range(GROUPS - 1))
-                landing = second_products(0, 0, "y3")
-                make_da3(b, "y", [GROUPS - 1])
+                for n in (b, b + 1):
+                    staged[n] = held([P, 2 * C, PACK], BF16, f"picked{n - b}")
+            make_da3(b, "x")
             make_first(b + 1)
             if b < BLOCKS - 2:
-                first_products(b + 2, "x")
+                first_products(b + 2, "y")
             make_da1(b)
-            if b == 0:
-                plain[3] = held([P, PACK, C], F32, "a1_0")
-                rest(plain[3][:], a1_t[3][:])
-                make_rests(3, "y")
             if b < BLOCKS - 2:
+                make_rests(b + 2, ("x0", "x1", "x2", "x3"))
+                plain[b + 2] = held([P, PACK, C], F32, "rest0") if b == 0 else placed([P, PACK, C], F32, "plain3", 0, 2)
+                for t in range(0, PACK, 2):
+                    rest(plain[b + 2][:, t:t + 2], a1_t[b + 2][:, t:t + 2])
                 quantise_set(b, f"a3_{b + 1}")
         b = BLOCKS - 1
-        make_da3(b, "x")
+        make_da3(b, "y", [0, 1, 3])
+        landing = second_products(0, 0, "y2", held([P, HALF], F32, "dy0"))
+        make_da3(b, "y", [2])
         nc.scalar.activation(window(0, 0), landing[:], ACT.Copy)
-        nc.scalar.activation(window(0, 1), second_products(0, 1, "y0")[:], ACT.Copy)
+        landing = second_products(0, 1, "x0", placed([P, HALF], F32, "landing", 2, 2))
+        nc.scalar.activation(window(0, 1), landing[:], ACT.Copy)
         make_da1(b, [0, 1])
         quantise_set(2, "a3_3")
-        nc.scalar.activation(window(1, 0), second_products(1, 0, "y1")[:], ACT.Copy)
+        nc.scalar.activation(window(1, 0), second_products(1, 0, "x1", held([P, HALF], F32, "dy1"))[:], ACT.Copy)
         make_da1(b, [2])
-        quantise_set(3, "dy6", 0, C)
+        quantise_set(3, "a1_3", 0, C)
         make_da1(b, [3])
-        quantise_set(3, "dy6", C, C + HALF)
-        quantise_set(3, "dy6", C + HALF, 2 * C)
-        nc.vector.tensor_copy(window(1, 1), second_products(1, 1, "y2")[:])
-        nc.sync.dma_start(out=out, in_=result[:])
+        quantise_set(3, "a1_3", C, C + HALF)
+        quantise_set(3, "a1_3", C + HALF, 2 * C)
+        nc.vector.tensor_copy(window(1, 1), second_products(1, 1, "x2", held([P, HALF], F32, "dy2"))[:])
+        for first in range(0, T, C):
+            cols = slice(first, first + C)
+            nc.vector.tensor_tensor(out=results[0][:, cols], in0=results[0][:, cols], in1=results[1][:, cols], op=ADD)
+            nc.sync.dma_start(out=out[:, cols], in_=results[0][:, cols])

@@ -103,9 +103,9 @@ def tile_moe_bdx_glu_sigmoid_kernel(
         nc.sync.dma_start(out=a1_t[0][:, 1:, :], in_=first_block[:, 1:, :])
         with nc.allow_non_contiguous_dma(reason="one gate a partition"):
             nc.sync.dma_start(out=gate_col[:], in_=gate[0, C:].rearrange("(a j) -> j a", j=P))
-        load_saved(a1, a1_t, 1)
         load_saved(a3, a3_t, 0, 0, 2)
         load_w2(0)
+        load_saved(a1, a1_t, 1)
         load_saved(a3, a3_t, 0, 2, 4)
         load_saved(a3, a3_t, 1)
         load_w2(1)
@@ -187,7 +187,7 @@ def tile_moe_bdx_glu_sigmoid_kernel(
 
         def make_slope(b):
             if b == 0:
-                slopes[b] = held([P, PACK, C], F32, "rounded00")
+                slopes[b] = held([P, PACK, C], F32, "rounded01")
                 parts = [(slice(t, t + 2), slice(0, C)) for t in range(0, PACK, 2)]
             else:
                 slopes[b] = placed([P, PACK, C], F32, f"slope{b}", b - 1, 0)
@@ -199,13 +199,12 @@ def tile_moe_bdx_glu_sigmoid_kernel(
 
         def place(b, w, a):
             if b < 2:
-                return b, (w * GROUPS + a) * P
-            part = w if b == 2 else 3 - w
-            return 2 + a // 2, (2 * part + a % 2) * P
+                return b, 1 - w, a * P
+            return 2 + a // 2, b - 2, (2 * (w if b == 2 else 1 - w) + a % 2) * P
 
         def room(b, w, a):
-            n, first = place(b, w, a)
-            return staged[n][:, first:first + P, :]
+            n, part, first = place(b, w, a)
+            return staged[n, part][:, first:first + P, :]
 
         def make_da3(b, side, groups=range(GROUPS)):
             for a in groups:
@@ -221,24 +220,29 @@ def tile_moe_bdx_glu_sigmoid_kernel(
                     op=MULT,
                 )
 
-        def quantise_set(n, slot, first=0, last=2 * C):
-            if first == 0:
-                d_codes[n] = held([P, 2 * C], U32, slot), held([P, 2 * C], U8, f"d_scales{n}")
+        def quantise_set(n, slot, pieces):
+            if n not in d_codes:
+                if n == 2:
+                    scales = placed([P, 2, C], U8, "d_scales2", 1, 0)
+                else:
+                    scales = held([P, 2, C], U8, f"dy{2 * n + 1}")
+                d_codes[n] = held([P, 2, C], U32, slot), scales
             codes, scales = d_codes[n]
-            quantise(codes[:, first:last], scales[:, first:last], staged[n][:, first:last, :])
+            for part, first, last in pieces:
+                quantise(codes[:, part, first:last], scales[:, part, first:last], staged[n, part][:, first:last, :])
 
         def second_products(e, half, tag, landing):
             dx = banks.tile([P, HALF], F32, name=tag)
             order = ((0, 0), (0, 1), (1, 1), (1, 0))
             for step, (h, w) in enumerate(order):
-                n, first = place(2 * e + h, w, 2 * half)
+                n, part, first = place(2 * e + h, w, 2 * half)
                 codes, scales = d_codes[n]
                 nc.tensor.matmul_mx(
                     out=dx[:],
                     lhsT=w13[w][:, 2 * e + h, :].bitcast(E2M1X4),
                     lhsT_scale=w13s[:, w, 2 * e + h, :],
-                    rhs=codes[:, first:first + HALF].bitcast(E5M2X4),
-                    rhs_scale=scales[:, first:first + HALF],
+                    rhs=codes[:, part, first:first + HALF].bitcast(E5M2X4),
+                    rhs_scale=scales[:, part, first:first + HALF],
                     start=step == 0,
                     stop=step == len(order) - 1,
                 )
@@ -251,9 +255,11 @@ def tile_moe_bdx_glu_sigmoid_kernel(
         def window(e, half):
             return results[e * half][:].indirect(slots(e, half * HALF, (half + 1) * HALF))
 
-        firsts[0] = held([P, GROUPS, PACK, P], F32, "rest0")
-        for a in range(GROUPS):
-            rests[0, a] = firsts[0][:, a]
+        firsts[0] = held([P, GROUPS, PACK, P], F32, "first0")
+        for pair in range(2):
+            both = held([P, 2, PACK, P], F32, f"rest0{pair}")
+            for a in range(2):
+                rests[0, 2 * pair + a] = both[:, a]
         rest(rests[0, 0][:, :1], turn("x0", early[:].unsqueeze(1))[:])
         weighed = [placed([P, PACK, C], F32, f"weighed{s}", region, 1) for s, region in enumerate((1, 0))]
         picked = [held([P, PACK, C], F32, f"picked{s}") for s in range(2)]
@@ -286,8 +292,8 @@ def tile_moe_bdx_glu_sigmoid_kernel(
         spread = banks.tile([P, C], F32, name="y3")
         for a in range(GROUPS):
             nc.tensor.transpose(spread[:, a * P:(a + 1) * P], gate_col[:, a:a + 1].to_broadcast([P, P]), ident[:])
-        rounded[1, 0] = held([P, C, PACK], BF16, "rounded01")
-        rounded[1, 1] = laid.tile([P, C, PACK], BF16, name="rounded11", align_bytes=64, offset=3 * QUARTER // 2)
+        for s in range(2):
+            rounded[1, s] = placed([P, C, PACK], BF16, f"rounded1{s}", 0, 2 - s)
         for s in range(2):
             nc.vector.tensor_tensor(
                 out=interleaved(rounded[1, s][:]),
@@ -295,48 +301,55 @@ def tile_moe_bdx_glu_sigmoid_kernel(
                 in1=spread[:].rearrange("p (c i) -> p c i", i=4).unsqueeze(2).to_broadcast([P, C // 4, PACK, 4]),
                 op=MULT,
             )
-        make_rests(1, ("y0", "y1", "y2", "x0"))
-        rest(a1_t[1][:], a1_t[1][:])
+        plain[1] = held([P, PACK, C], F32, "plain1")
+        rest(plain[1][:], a1_t[1][:])
+        make_rests(1, ("x0", "x1", "x2", "x3"))
         first_products(0, "y")
         make_first(0)
-        first_products(1, "y")
-        codes, scales = held([P, 2, C], U32, "a3_0"), held([P, 2, C], U8, "g_scales1")
+        codes, scales = held([P, 2, C], U32, "a3_0"), held([P, 2, C], U8, "rest00")
         for s in range(2):
             quantise_g(1, s, codes[:, s], scales[:, s])
+        whole = [(0, 0, C), (1, 0, C)]
         for b in range(BLOCKS - 1):
             make_slope(b + 1)
             if b < BLOCKS - 2:
-                staged[b] = placed([P, 2 * C, PACK], BF16, f"staged{b}", b + 1, 1)
+                for part in range(2):
+                    staged[b, part] = placed([P, C, PACK], BF16, f"staged{b}{part}", b + 1, 2 - part)
             else:
                 for n in (b, b + 1):
-                    staged[n] = held([P, 2 * C, PACK], BF16, f"picked{n - b}")
-            make_da3(b, "x")
+                    both = held([P, 2, C, PACK], BF16, f"picked{n - b}")
+                    for part in range(2):
+                        staged[n, part] = both[:, part]
+            make_da3(b, "y")
+            if b == 0:
+                first_products(1, "x")
             make_first(b + 1)
             if b < BLOCKS - 2:
-                first_products(b + 2, "y")
+                first_products(b + 2, "x")
             make_da1(b)
             if b < BLOCKS - 2:
-                make_rests(b + 2, ("x0", "x1", "x2", "x3"))
-                plain[b + 2] = held([P, PACK, C], F32, "rest0") if b == 0 else placed([P, PACK, C], F32, "plain3", 0, 2)
-                for t in range(0, PACK, 2):
-                    rest(plain[b + 2][:, t:t + 2], a1_t[b + 2][:, t:t + 2])
-                quantise_set(b, f"a3_{b + 1}")
+                plain[b + 2] = held([P, PACK, C], F32, "first0") if b == 0 else placed([P, PACK, C], F32, "plain3", 0, 2)
+                early_part = C if b == 0 else HALF
+                rest(plain[b + 2][:, :, :early_part], a1_t[b + 2][:, :, :early_part])
+                make_rests(b + 2, ("y0", "y1", "y2", "y3"))
+                if early_part < C:
+                    rest(plain[b + 2][:, :, early_part:], a1_t[b + 2][:, :, early_part:])
+                quantise_set(b, f"a3_{b + 1}", whole)
         b = BLOCKS - 1
-        make_da3(b, "y", [0, 1, 3])
-        landing = second_products(0, 0, "y2", held([P, HALF], F32, "dy0"))
-        make_da3(b, "y", [2])
+        make_da3(b, "x", [0, 1, 3])
+        landing = second_products(0, 0, "x2", held([P, HALF], F32, "dy0"))
+        make_da3(b, "x", [2])
         nc.scalar.activation(window(0, 0), landing[:], ACT.Copy)
-        landing = second_products(0, 1, "x0", placed([P, HALF], F32, "landing", 2, 2))
+        landing = second_products(0, 1, "y0", placed([P, HALF], F32, "landing", 2, 2))
         nc.scalar.activation(window(0, 1), landing[:], ACT.Copy)
         make_da1(b, [0, 1])
-        quantise_set(2, "a3_3")
-        nc.scalar.activation(window(1, 0), second_products(1, 0, "x1", held([P, HALF], F32, "dy1"))[:], ACT.Copy)
+        quantise_set(2, "a3_3", whole)
+        nc.scalar.activation(window(1, 0), second_products(1, 0, "y1", placed([P, HALF], F32, "landing10", 2, 2))[:], ACT.Copy)
         make_da1(b, [2])
-        quantise_set(3, "a1_3", 0, C)
+        quantise_set(3, "picked0", [(0, 0, C)])
         make_da1(b, [3])
-        quantise_set(3, "a1_3", C, C + HALF)
-        quantise_set(3, "a1_3", C + HALF, 2 * C)
-        nc.vector.tensor_copy(window(1, 1), second_products(1, 1, "x2", held([P, HALF], F32, "dy2"))[:])
+        quantise_set(3, "picked0", [(1, 0, HALF), (1, HALF, C)])
+        nc.vector.tensor_copy(window(1, 1), second_products(1, 1, "y2", held([P, HALF], F32, "dy2"))[:])
         for first in range(0, T, C):
             cols = slice(first, first + C)
             nc.vector.tensor_tensor(out=results[0][:, cols], in0=results[0][:, cols], in1=results[1][:, cols], op=ADD)

@@ -260,7 +260,7 @@ def tile_moe_bdx_glu_sigmoid_kernel(
             both = held([P, 2, PACK, P], F32, f"rest0{pair}")
             for a in range(2):
                 rests[0, 2 * pair + a] = both[:, a]
-        rest(rests[0, 0][:, :1], turn("x0", early[:].unsqueeze(1))[:])
+        rest(rests[0, 0][:, :1], turn("y3", early[:].unsqueeze(1))[:])
         weighed = [placed([P, PACK, C], F32, f"weighed{s}", region, 1) for s, region in enumerate((1, 0))]
         picked = [held([P, PACK, C], F32, f"picked{s}") for s in range(2)]
         rounded = {(0, s): held([P, C, PACK], BF16, f"rounded0{s}") for s in range(2)}
@@ -284,12 +284,12 @@ def tile_moe_bdx_glu_sigmoid_kernel(
         rest(plain[0][:, 0, :P], early[:])
         rest(plain[0][:, 0, P:], a1_t[0][:, 0, P:])
         rest(plain[0][:, 1:, :], a1_t[0][:, 1:, :])
-        rest(rests[0, 0][:, 1:], turn("x0", a1_t[0][:, 1:, :P])[:])
+        rest(rests[0, 0][:, 1:], turn("y3", a1_t[0][:, 1:, :P])[:])
         for a in range(1, GROUPS):
             rest(rests[0, a], turn(f"x{a}", a1_t[0][:, :, a * P:(a + 1) * P])[:])
 
         make_slope(0)
-        spread = banks.tile([P, C], F32, name="y3")
+        spread = banks.tile([P, C], F32, name="x0")
         for a in range(GROUPS):
             nc.tensor.transpose(spread[:, a * P:(a + 1) * P], gate_col[:, a:a + 1].to_broadcast([P, P]), ident[:])
         for s in range(2):
@@ -303,9 +303,10 @@ def tile_moe_bdx_glu_sigmoid_kernel(
             )
         plain[1] = held([P, PACK, C], F32, "plain1")
         rest(plain[1][:], a1_t[1][:])
-        make_rests(1, ("x0", "x1", "x2", "x3"))
         first_products(0, "y")
         make_first(0)
+        make_rests(1, ("y0", "y1", "y2", "y3"))
+        first_products(1, "x")
         codes, scales = held([P, 2, C], U32, "a3_0"), held([P, 2, C], U8, "rest00")
         for s in range(2):
             quantise_g(1, s, codes[:, s], scales[:, s])
@@ -321,8 +322,6 @@ def tile_moe_bdx_glu_sigmoid_kernel(
                     for part in range(2):
                         staged[n, part] = both[:, part]
             make_da3(b, "y")
-            if b == 0:
-                first_products(1, "x")
             make_first(b + 1)
             if b < BLOCKS - 2:
                 first_products(b + 2, "x")

@@ -24,6 +24,7 @@ GROUPS = C // P
 HALF = C // 2
 BLOCKS = 4
 QUARTER = 4096
+ON_VECTOR = ((0, 3), (1, 3))
 FLOPS = 2 * E * C * (N * H + 2 * H * K)
 
 
@@ -209,10 +210,13 @@ def tile_moe_bdx_glu_sigmoid_kernel(
         def make_da3(b, side, groups=range(GROUPS)):
             for a in groups:
                 backs[b, a] = turn(f"{side}{a}", firsts[b][:, a])
-                nc.scalar.copy(out=room(b, 1, a), in_=backs[b, a][:].rearrange("p t c -> p c t"))
+                if (b, a) not in ON_VECTOR:
+                    nc.scalar.copy(out=room(b, 1, a), in_=backs[b, a][:].rearrange("p t c -> p c t"))
 
         def make_da1(b, groups=range(GROUPS)):
             for a in groups:
+                if (b, a) in ON_VECTOR:
+                    nc.vector.tensor_copy(out=room(b, 1, a), in_=backs[b, a][:].rearrange("p t c -> p c t"))
                 nc.vector.tensor_tensor(
                     out=interleaved(room(b, 0, a)),
                     in0=planes(backs[b, a][:]),
@@ -246,7 +250,7 @@ def tile_moe_bdx_glu_sigmoid_kernel(
                     start=step == 0,
                     stop=step == len(order) - 1,
                 )
-            if (e, half) == (1, 1):
+            if e == 1:
                 nc.vector.tensor_scalar_mul(landing[:], dx[:], -1.0)
             else:
                 nc.scalar.activation(out=landing[:], in_=dx[:], func=ACT.Copy, scale=-1.0)
@@ -343,7 +347,7 @@ def tile_moe_bdx_glu_sigmoid_kernel(
         nc.scalar.activation(window(0, 1), landing[:], ACT.Copy)
         make_da1(b, [0, 1])
         quantise_set(2, "a3_3", whole)
-        nc.scalar.activation(window(1, 0), second_products(1, 0, "y1", placed([P, HALF], F32, "landing10", 2, 2))[:], ACT.Copy)
+        nc.scalar.activation(window(1, 0), second_products(1, 0, "y1", held([P, HALF], F32, "dy4"))[:], ACT.Copy)
         make_da1(b, [2])
         quantise_set(3, "picked0", [(0, 0, C)])
         make_da1(b, [3])

@@ -100,10 +100,10 @@ def tile_moe_bdx_glu_sigmoid_kernel(
         nc.sync.dma_start(out=gate0[:, HALF:], in_=gate[0:P, HALF:C])
         for k in range(1, 2 * PACK):
             load_dy(k)
-        nc.sync.dma_start(out=a1_t[0][:, 0, P:], in_=first_block[:, 0, P:])
-        nc.sync.dma_start(out=a1_t[0][:, 1:, :], in_=first_block[:, 1:, :])
         with nc.allow_non_contiguous_dma(reason="one gate a partition"):
             nc.sync.dma_start(out=gate_col[:], in_=gate[0, C:].rearrange("(a j) -> j a", j=P))
+        nc.sync.dma_start(out=a1_t[0][:, 0, P:], in_=first_block[:, 0, P:])
+        nc.sync.dma_start(out=a1_t[0][:, 1:, :], in_=first_block[:, 1:, :])
         load_saved(a3, a3_t, 0, 0, 2)
         load_w2(0)
         load_saved(a1, a1_t, 1)
@@ -114,10 +114,10 @@ def tile_moe_bdx_glu_sigmoid_kernel(
         load_saved(a3, a3_t, 2)
         load_saved(a1, a1_t, 3)
         load_saved(a3, a3_t, 3)
-        load_scales(w13s[:, 0], w1_scales)
-        load_scales(w13s[:, 1], w3_scales)
         load_w13(0, w1_words)
         load_w13(1, w3_words)
+        load_scales(w13s[:, 0], w1_scales)
+        load_scales(w13s[:, 1], w3_scales)
 
         def interleaved(dst):
             return dst.rearrange("p (c i) t -> p c t i", i=4)

from contextlib import ExitStack

import concourse.mybir as mybir
from concourse.masks import make_identity

F32 = mybir.dt.float32
BF16 = mybir.dt.bfloat16
I32 = mybir.dt.int32
U32 = mybir.dt.uint32
U16 = mybir.dt.uint16
U8 = mybir.dt.uint8
E5M2X4 = mybir.dt.float8_e5m2_x4
E2M1X4 = mybir.dt.float4_e2m1fn_x4
ACT = mybir.ActivationFunctionType
MULT = mybir.AluOpType.mult
ADD = mybir.AluOpType.add
SUB = mybir.AluOpType.subtract

P = 128
PACK = 4
PASS = P * PACK
K, T, E, C, H, N = 128, 1024, 2, 512, 1024, 1024
GROUPS = C // P
HALF = C // 2
BLOCKS = 4
QUARTER = 4096
ON_VECTOR = ((0, 3), (1, 3))
FLOPS = 2 * E * C * (N * H + 2 * H * K)


def tile_moe_bdx_glu_sigmoid_kernel(
    tc, dyT, a1, a3, w2_words, w2_scales, w1_words, w1_scales, w3_words, w3_scales, gate, offs, out
):
    nc = tc.nc
    with ExitStack() as ctx:
        keep = ctx.enter_context(tc.tile_pool(name="keep", bufs=1))
        laid = ctx.enter_context(tc.tile_pool(name="laid", bufs=1))
        banks = ctx.enter_context(tc.psum_pool(name="banks", bufs=1))

        def held(shape, dtype, slot):
            return keep.tile(shape, dtype, name=slot, align_bytes=64)

        def placed(shape, dtype, name, region, first):
            return laid.tile(shape, dtype, name=name, align_bytes=64, offset=(4 * region + first) * QUARTER)

        offsets = keep.tile([P, E * C // 16], U16, name="offsets")
        ident = held([P, P], F32, "ident")
        gate0 = held([P, C], F32, "gate0")
        gate_col = held([P, GROUPS], F32, "gate_col")
        dy = [held([P, T], F32, f"dy{k}") for k in range(N // P)]
        w2 = [held([P, 2, 2 * H], U8, f"w2_{e}") for e in range(E)]
        w2s = held([P, 2 * E, H], U8, "w2s")
        w13 = [held([P, 4, 2 * K], U8, f"w13_{w}") for w in range(2)]
        w13s = held([P, 2, 4, K], U8, "w13s")
        a1_t = [held([P, PACK, C], F32, f"a1_{b}") for b in range(BLOCKS)]
        a3_t = [held([P, PACK, C], F32, f"a3_{b}") for b in range(BLOCKS)]
        results = [held([P, T], F32, f"result{n}") for n in range(2)]

        make_identity(nc, ident[:])
        nc.vector.memset(w2s[:].rearrange("p b i -> p (b i)").bitcast(I32), 0)
        nc.vector.memset(w13s[:].rearrange("p w b k -> p (w b k)").bitcast(I32), 0)
        for result in results:
            nc.vector.memset(result[:], 0.0)

        def load_dy(k):
            s, j = divmod(k, PACK)
            nc.sync.dma_start(out=dy[k][:], in_=dyT[s * PASS:(s + 1) * PASS].rearrange("(p j) w -> p j w", j=PACK)[:, j, :])

        def load_scales(dst, scales):
            for q in (0, 2, 1, 3):
                nc.sync.dma_start(
                    out=dst[32 * q:32 * q + 4].rearrange("p b i -> p (b i)").bitcast(I32).rearrange("p (b i) -> p b i", b=dst.shape[1]),
                    in_=scales[:, :, 4 * q:4 * q + 4, :].bitcast(I32).rearrange("e s q i -> q (e s) i"),
                )

        def load_w2(e):
            load_scales(w2s[:, 2 * e:2 * e + 2], w2_scales[e:e + 1])
            for s in range(2):
                nc.sync.dma_start(out=w2[e][:, s, :].bitcast(I32), in_=w2_words[e, s].bitcast(I32))

        def load_w13(w, words):
            nc.sync.dma_start(
                out=w13[w][:].rearrange("p b i -> p (b i)").bitcast(I32).rearrange("p (b i) -> p b i", b=4),
                in_=words.bitcast(I32).rearrange("e s p i -> p (e s) i"),
            )

        def load_saved(src, dst, b, first=0, last=PACK):
            e, h = divmod(b, 2)
            nc.sync.dma_start(
                out=dst[b][:, first:last],
                in_=src[h * PASS:(h + 1) * PASS, e * C:(e + 1) * C].rearrange("(p j) c -> p j c", j=PACK)[:, first:last],
            )

        early = held([P, P], F32, "early")
        first_block = a1[0:PASS, 0:C].rearrange("(p j) c -> p j c", j=PACK)
        nc.sync.dma_start(offsets[:], offs)
        nc.sync.dma_start(out=early[:], in_=first_block[:, 0, :P])
        nc.sync.dma_start(out=gate0[:, :HALF], in_=gate[0:P, 0:HALF])
        load_dy(0)
        nc.sync.dma_start(out=gate0[:, HALF:], in_=gate[0:P, HALF:C])
        for k in range(1, 2 * PACK):
            load_dy(k)
        with nc.allow_non_contiguous_dma(reason="one gate a partition"):
            nc.sync.dma_start(out=gate_col[:], in_=gate[0, C:].rearrange("(a j) -> j a", j=P))
        nc.sync.dma_start(out=a1_t[0][:, 0, P:], in_=first_block[:, 0, P:])
        nc.sync.dma_start(out=a1_t[0][:, 1:, :], in_=first_block[:, 1:, :])
        load_saved(a3, a3_t, 0, 0, 2)
        load_w2(0)
        load_saved(a1, a1_t, 1)
        load_saved(a3, a3_t, 0, 2, 4)
        load_saved(a3, a3_t, 1)
        load_w2(1)
        load_saved(a1, a1_t, 2)
        load_saved(a3, a3_t, 2)
        load_saved(a1, a1_t, 3)
        load_saved(a3, a3_t, 3)
        load_w13(0, w1_words)
        load_w13(1, w3_words)
        load_scales(w13s[:, 0], w1_scales)
        load_scales(w13s[:, 1], w3_scales)

        def interleaved(dst):
            return dst.rearrange("p (c i) t -> p c t i", i=4)

        def planes(src):
            return src.rearrange("p t (c i) -> p c t i", i=4)

        def quantise(codes, scales, src):
            nc.vector.quantize_mx(out=codes.bitcast(E5M2X4), scales=scales, in_=src.rearrange("p c t -> p (c t)"))

        def slots(e, first=0, last=C):
            return offsets[:, (e * C + first) // 16:(e * C + last) // 16]

        def gather_weighed(k, dst, first=0, last=C):
            nc.vector.tensor_tensor(
                out=dst[:, k % PACK, first:last], in0=dy[k][:].indirect(slots(0, first, last)), in1=gate0[:, first:last], op=MULT
            )

        def gather_plain(k, dst):
            nc.scalar.activation(dst[:, k % PACK, :], dy[k][:].indirect(slots(1)), ACT.Copy)

        g_codes, sums, rests, firsts, slopes, backs, staged, d_codes = {}, {}, {}, {}, {}, {}, {}, {}

        def turn(tag, src):
            bank = banks.tile([P, src.shape[1], P], F32, name=tag)
            for t in range(src.shape[1]):
                nc.tensor.transpose(bank[:, t, :], src[:, t, :], ident[:])
            return bank

        def rest(dst, src):
            nc.scalar.activation(out=dst, in_=src, func=ACT.Sigmoid, scale=-1.0)

        def make_rests(b, tags):
            for pair in range(2):
                both = held([P, 2, PACK, P], F32, f"dy{2 * (b - 1) + pair}")
                for a in range(2 * pair, 2 * pair + 2):
                    rests[b, a] = both[:, a % 2]
                    rest(rests[b, a], turn(tags[a], a1_t[b][:, :, a * P:(a + 1) * P])[:])

        def first_products(b, side, groups=range(GROUPS)):
            e, h = divmod(b, 2)
            for a in groups:
                cols = slice(a * P, (a + 1) * P)
                dh = banks.tile([P, PASS], F32, name=f"{side}{a}")
                sums[b, a] = dh
                for s in range(2):
                    codes, scales = g_codes[e, s]
                    nc.tensor.matmul_mx(
                        out=dh[:],
                        lhsT=codes[:, cols].bitcast(E5M2X4),
                        lhsT_scale=scales[:, cols],
                        rhs=w2[e][:, s, 2 * h * PASS:2 * (h + 1) * PASS].bitcast(E2M1X4),
                        rhs_scale=w2s[:, 2 * e + s, h * PASS:(h + 1) * PASS],
                        start=(s == 0),
                        stop=(s == 1),
                    )

        def make_first(b):
            for a in range(GROUPS):
                nc.vector.scalar_tensor_tensor(
                    out=firsts[b][:, a],
                    in0=rests[b, a],
                    scalar=1.0,
                    in1=sums[b, a][:].rearrange("p (m t) -> p t m", t=PACK),
                    op0=SUB,
                    op1=MULT,
                )

        def make_slope(b):
            if b == 0:
                slopes[b] = held([P, PACK, C], F32, "rounded01")
                parts = [(slice(t, t + 2), slice(0, C)) for t in range(0, PACK, 2)]
            else:
                slopes[b] = placed([P, PACK, C], F32, f"slope{b}", b - 1, 0)
                firsts[b] = placed([P, GROUPS, PACK, P], F32, f"first{b}", b - 1, 2)
                step = HALF if b == BLOCKS - 1 else C
                parts = [(slice(0, PACK), slice(first, first + step)) for first in range(0, C, step)]
            for ts, cols in parts:
                nc.gpsimd.tensor_tensor(out=slopes[b][:, ts, cols], in0=plain[b][:, ts, cols], in1=a3_t[b][:, ts, cols], op=MULT)

        def place(b, w, a):
            if b < 2:
                return b, 1 - w, a * P
            return 2 + a // 2, b - 2, (2 * (w if b == 2 else 1 - w) + a % 2) * P

        def room(b, w, a):
            n, part, first = place(b, w, a)
            return staged[n, part][:, first:first + P, :]

        def make_da3(b, side, groups=range(GROUPS)):
            for a in groups:
                backs[b, a] = turn(f"{side}{a}", firsts[b][:, a])
                if (b, a) not in ON_VECTOR:
                    nc.scalar.copy(out=room(b, 1, a), in_=backs[b, a][:].rearrange("p t c -> p c t"))

        def make_da1(b, groups=range(GROUPS)):
            for a in groups:
                if (b, a) in ON_VECTOR:
                    nc.vector.tensor_copy(out=room(b, 1, a), in_=backs[b, a][:].rearrange("p t c -> p c t"))
                nc.vector.tensor_tensor(
                    out=interleaved(room(b, 0, a)),
                    in0=planes(backs[b, a][:]),
                    in1=planes(slopes[b][:, :, a * P:(a + 1) * P]),
                    op=MULT,
                )

        def quantise_set(n, slot, pieces):
            if n not in d_codes:
                if n == 2:
                    scales = placed([P, 2, C], U8, "d_scales2", 1, 0)
                else:
                    scales = held([P, 2, C], U8, f"dy{2 * n + 1}")
                d_codes[n] = held([P, 2, C], U32, slot), scales
            codes, scales = d_codes[n]
            for part, first, last in pieces:
                quantise(codes[:, part, first:last], scales[:, part, first:last], staged[n, part][:, first:last, :])

        def second_products(e, half, tag, landing):
            dx = banks.tile([P, HALF], F32, name=tag)
            order = ((0, 0), (0, 1), (1, 1), (1, 0))
            for step, (h, w) in enumerate(order):
                n, part, first = place(2 * e + h, w, 2 * half)
                codes, scales = d_codes[n]
                nc.tensor.matmul_mx(
                    out=dx[:],
                    lhsT=w13[w][:, 2 * e + h, :].bitcast(E2M1X4),
                    lhsT_scale=w13s[:, w, 2 * e + h, :],
                    rhs=codes[:, part, first:first + HALF].bitcast(E5M2X4),
                    rhs_scale=scales[:, part, first:first + HALF],
                    start=step == 0,
                    stop=step == len(order) - 1,
                )
            if e == 1:
                nc.vector.tensor_scalar_mul(landing[:], dx[:], -1.0)
            else:
                nc.scalar.activation(out=landing[:], in_=dx[:], func=ACT.Copy, scale=-1.0)
            return landing

        def window(e, half):
            return results[e * half][:].indirect(slots(e, half * HALF, (half + 1) * HALF))

        firsts[0] = held([P, GROUPS, PACK, P], F32, "first0")
        for pair in range(2):
            both = held([P, 2, PACK, P], F32, f"rest0{pair}")
            for a in range(2):
                rests[0, 2 * pair + a] = both[:, a]
        rest(rests[0, 0][:, :1], turn("y3", early[:].unsqueeze(1))[:])
        weighed = [placed([P, PACK, C], F32, f"weighed{s}", region, 1) for s, region in enumerate((1, 0))]
        picked = [held([P, PACK, C], F32, f"picked{s}") for s in range(2)]
        rounded = {(0, s): held([P, C, PACK], BF16, f"rounded0{s}") for s in range(2)}
        gather_weighed(0, weighed[0], 0, HALF)
        gather_weighed(0, weighed[0], HALF, C)
        for k in range(2 * PACK):
            s = k // PACK
            if k > 0:
                gather_weighed(k, weighed[s])
            gather_plain(k, picked[s])
            if k % PACK == PACK - 1:
                nc.vector.tensor_copy(out=interleaved(rounded[0, s][:]), in_=planes(weighed[s][:]))

        def quantise_g(e, s, codes, scales):
            g_codes[e, s] = codes, scales
            quantise(codes, scales, rounded[e, s][:])

        for s, slot in enumerate(("gate0", "g_codes01")):
            quantise_g(0, s, held([P, C], U32, slot)[:], held([P, C], U8, f"g_scales0{s}")[:])
        plain = {0: placed([P, PACK, C], F32, "plain0", 1, 1), 1: a1_t[1]}
        rest(plain[0][:, 0, :P], early[:])
        rest(plain[0][:, 0, P:], a1_t[0][:, 0, P:])
        rest(plain[0][:, 1:, :], a1_t[0][:, 1:, :])
        rest(rests[0, 0][:, 1:], turn("y3", a1_t[0][:, 1:, :P])[:])
        for a in range(1, GROUPS):
            rest(rests[0, a], turn(f"x{a}", a1_t[0][:, :, a * P:(a + 1) * P])[:])

        make_slope(0)
        spread = banks.tile([P, C], F32, name="x0")
        for a in range(GROUPS):
            nc.tensor.transpose(spread[:, a * P:(a + 1) * P], gate_col[:, a:a + 1].to_broadcast([P, P]), ident[:])
        for s in range(2):
            rounded[1, s] = placed([P, C, PACK], BF16, f"rounded1{s}", 0, 2 - s)
        for s in range(2):
            nc.vector.tensor_tensor(
                out=interleaved(rounded[1, s][:]),
                in0=planes(picked[s][:]),
                in1=spread[:].rearrange("p (c i) -> p c i", i=4).unsqueeze(2).to_broadcast([P, C // 4, PACK, 4]),
                op=MULT,
            )
        plain[1] = held([P, PACK, C], F32, "plain1")
        rest(plain[1][:], a1_t[1][:])
        first_products(0, "y")
        make_first(0)
        make_rests(1, ("y0", "y1", "y2", "y3"))
        first_products(1, "x")
        codes, scales = held([P, 2, C], U32, "a3_0"), held([P, 2, C], U8, "rest00")
        for s in range(2):
            quantise_g(1, s, codes[:, s], scales[:, s])
        whole = [(0, 0, C), (1, 0, C)]
        for b in range(BLOCKS - 1):
            make_slope(b + 1)
            if b < BLOCKS - 2:
                for part in range(2):
                    staged[b, part] = placed([P, C, PACK], BF16, f"staged{b}{part}", b + 1, 2 - part)
            else:
                for n in (b, b + 1):
                    both = held([P, 2, C, PACK], BF16, f"picked{n - b}")
                    for part in range(2):
                        staged[n, part] = both[:, part]
            make_da3(b, "y")
            make_first(b + 1)
            if b < BLOCKS - 2:
                first_products(b + 2, "x")
            make_da1(b)
            if b < BLOCKS - 2:
                plain[b + 2] = held([P, PACK, C], F32, "first0") if b == 0 else placed([P, PACK, C], F32, "plain3", 0, 2)
                early_part = C if b == 0 else HALF
                rest(plain[b + 2][:, :, :early_part], a1_t[b + 2][:, :, :early_part])
                make_rests(b + 2, ("y0", "y1", "y2", "y3"))
                if early_part < C:
                    rest(plain[b + 2][:, :, early_part:], a1_t[b + 2][:, :, early_part:])
                quantise_set(b, f"a3_{b + 1}", whole)
        b = BLOCKS - 1
        make_da3(b, "x", [0, 1, 3])
        landing = second_products(0, 0, "x2", held([P, HALF], F32, "dy0"))
        make_da3(b, "x", [2])
        nc.scalar.activation(window(0, 0), landing[:], ACT.Copy)
        landing = second_products(0, 1, "y0", placed([P, HALF], F32, "landing", 2, 2))
        nc.scalar.activation(window(0, 1), landing[:], ACT.Copy)
        make_da1(b, [0, 1])
        quantise_set(2, "a3_3", whole)
        nc.scalar.activation(window(1, 0), second_products(1, 0, "y1", held([P, HALF], F32, "dy4"))[:], ACT.Copy)
        make_da1(b, [2])
        quantise_set(3, "picked0", [(0, 0, C)])
        make_da1(b, [3])
        quantise_set(3, "picked0", [(1, 0, HALF), (1, HALF, C)])
        nc.vector.tensor_copy(window(1, 1), second_products(1, 1, "y2", held([P, HALF], F32, "dy2"))[:])
        for first in range(0, T, C):
            cols = slice(first, first + C)
            nc.vector.tensor_tensor(out=results[0][:, cols], in0=results[0][:, cols], in1=results[1][:, cols], op=ADD)
            nc.sync.dma_start(out=out[:, cols], in_=results[0][:, cols])
